import numpy as np, ml_dtypes
CORES = [51,54,179,182]
N = 4
BF = ml_dtypes.bfloat16
def gentries(a):
    return np.ascontiguousarray(a.reshape(8, 16, -1).transpose(0, 2, 1)).reshape(8, -1)
def gtable(e):
    e = np.asarray(e); return np.ascontiguousarray(e.reshape(8, -1, 16).transpose(0, 2, 1)).reshape(128, -1).astype(np.int32)
V, E, G, K, A, S, R = 1440, 32, 768, 256, 32, 5, 224
W = V + (N - 1) * E
def far(d, g):
    return (g, 7 - g, (8 - g) % 8)[d % 3]
def watch(rng, ins, nd, out, dens):
    co = np.full((16, W), -1)
    for i in range(16):
        o = rng.permutation(G)[:int(dens * G)]
        j = (rng.random(len(o)) * np.maximum(nd[o], 1)).astype(np.int64)
        c = np.where(nd[o] > 0, ins[j, o], out[rng.integers(0, G, len(o))])
        c, first = np.unique(c, return_index=True); co[i, c] = o[first]
    return co
def lively(rng, dens=None, pa=None, sk=1.5, p=None):
    if dens is None: dens = rng.choice(np.array([0.12, 0.2, 0.3]))
    if pa is None: pa = rng.choice(np.array([0.15, 0.4, 0.65, 0.9]))
    if p is None: p = rng.permutation(V)
    al = rng.choice(np.array([0.06, 0.15, 0.3]))
    out, rest = p[:G].copy(), p[G:]; Z, B, T, U = rest[:R], rest[R:2 * R], rest[2 * R:2 * R + 24], rest[2 * R + 24:]
    x = np.full((16, V), -1); x[:, Z] = 0
    x[:, B] = (rng.random((16, R)) * (1 + rng.integers(1, 16, R))).astype(np.int64)
    x[:, T[:16]] = 15; x[rng.integers(0, 16, 8), T[8:16]] = 14; x[:, T[16:]] = 0; x[rng.integers(0, 16, 8), T[16:]] = 1
    kind = rng.choice(6, G, p=np.array([0.2, 0.33, 0.08, al, 0.06, 0.33 - al]))
    nd = np.where((kind == 1) | (kind == 2), rng.integers(1, 4, G), 0); nd = np.where(kind == 3, 1, nd); nd = np.where(kind == 4, rng.integers(2, 16, G), nd)
    zi = Z[rng.integers(0, R, (15, G))]
    ins = np.where((rng.random((15, G)) < 0.5) | (kind == 3) | (kind == 5), zi, B[rng.integers(0, R, (15, G))])
    h = rng.random((15, G)); ui = U[rng.integers(0, len(U), (15, G))]
    dep = np.where(h < 0.65, out[(G * rng.random((15, G)) ** sk).astype(np.int64)], np.where(h < 0.85, rng.integers(V, W, (15, G)), ui))
    dep = np.where((kind == 4) & (rng.random((15, G)) < 0.7), ui, dep)
    ins = np.where(np.arange(15)[:, None] < nd, dep, ins)
    ins[14] = np.where(kind == 2, T[rng.integers(0, 16, G)], ins[14])
    k5 = np.flatnonzero(kind == 5)
    if len(k5) == 0: k5 = np.arange(G)
    i3 = kind == 3
    ins[13] = np.where(i3 & (rng.random(G) < 0.2), out[k5[rng.integers(0, len(k5), G)]], ins[13])
    ins[12] = np.where(i3 & (rng.random(G) < 0.08), T[rng.integers(16, 24, G)], ins[12])
    ins[0] = np.where(i3 & (rng.random(G) < 0.04), out, ins[0])
    ins[1] = np.where(i3 & (rng.random(G) < 0.06), ins[0], ins[1])
    co = watch(rng, ins, nd, out, dens)
    gv = np.concatenate([np.take_along_axis(ins, np.argsort(rng.random((15, G)), axis=0), 0), out[None]])
    b = np.flatnonzero(rng.random(G) < 0.03); x[:, out[b]] = rng.integers(0, 16, (16, len(b)))
    return x, gv, co, (rng.random(G) < pa).astype(np.int64), out, Z, B, T, U
def alias(rng, q, k, u):
    k = np.asarray(k); q[1][:15, k] = q[5][rng.integers(0, R, (15, len(k)))]; q[1][rng.integers(0, 15, len(k)), k] = u; q[0][:, q[4][k]] = -1
def ready(rng, q, k):
    k = np.asarray(k); n = (15, len(k))
    q[1][:15, k] = np.where(rng.random(n) < 0.5, q[5][rng.integers(0, R, n)], q[6][rng.integers(0, R, n)]); q[0][:, q[4][k]] = -1
def exports(rng, P):
    n = (N - 1) * E
    return np.stack([np.stack([np.where(rng.random(n) < 0.75, q[4][(G * rng.random(n) ** 2).astype(np.int64)], rng.integers(0, V, n)) for q in p]) for p in P])
def pack(P, ex):
    def whole(i): return np.stack([np.concatenate([q[i] for q in p]) for p in P])
    return {"x0": whole(0).astype(np.float32).astype(BF), "gv": whole(1).astype(np.int32), "co": whole(2).astype(np.int32),
            "aw": np.stack([np.stack([q[3] for q in p]) for p in P]).astype(np.int32), "ex": np.stack([gtable(a) for a in ex])}
def setup_inputs(rng):
    P = [[lively(rng) for g in range(8)] for r in range(N)]
    return pack(P, exports(rng, P))
def setup_inputs_spread(rng):
    P = []
    for r in range(N):
        P.append([])
        for g in range(8):
            q = lively(rng, dens=rng.choice(np.array([0.03, 0.4, 0.9])), pa=rng.choice(np.array([0.05, 0.5, 1.0])), sk=4.0)
            s = np.flatnonzero(rng.random(G) < 0.2); q[1][:15, s] = rng.integers(0, W, (15, len(s)))
            q[0][:, q[6]] = np.minimum(np.exp2(4 * rng.random(R)) * rng.random((16, R)), 15).astype(np.int64)
            P[r].append(q)
    return pack(P, exports(rng, P))
def setup_inputs_ends(rng):
    P = []
    for r in range(N):
        P.append([])
        for g in range(8):
            p = np.insert(np.insert(1 + rng.permutation(V - 2), G - 1, V - 1), G, 0)
            q = lively(rng, p=p, pa=(0.15, 0.6)[(g // 2 + r) % 2]); x, gv, co, aw, out, Z, B, T, U = q
            x[:, B] = 15 * rng.integers(0, 2, (16, R))
            t = rng.integers(0, 7, G); ins = np.zeros((15, G), np.int64); own = out[(G * rng.random(G) ** 1.5).astype(np.int64)]
            ins[:4] = np.where(t == 0, B[rng.integers(0, R, (4, G))], 0)
            ins[0] = np.where((t == 1) | (t == 2), W - 1, np.where((t == 3) | (t == 5), own, ins[0]))
            ins[1] = np.where(t == 2, W - 1, np.where(t == 5, T[rng.integers(0, 16, G)], ins[1])); ins[2] = np.where(t == 2, W - 1, ins[2])
            ins = np.where(t == 4, W - 1, ins)
            co[:] = watch(rng, ins, ((t > 0) & (t < 6)).astype(np.int64), out, 0.2)
            gv[:15] = np.take_along_axis(ins, np.argsort(rng.random((15, G)), axis=0), 0)
            co[co == G - 1] = -1
            if g % 2: co[:, W - 1] = G - 1
            else: co[np.arange(16), out[:16]] = G - 1
            aw[0] = 1; aw[G - 1] = 1
            if (g + r) % 2: x[:, V - 1] = 15 * rng.integers(0, 2, 16)
            else:
                x[:, V - 1] = -1; gv[:15, G - 1] = 0; gv[:4, G - 1] = B[rng.integers(0, R, 4)]
            P[r].append(q)
    ex = exports(rng, P)
    ex = np.where(rng.random(ex.shape) < 0.75, np.where(rng.random(ex.shape) < 0.5, 0, V - 1), ex); ex[..., -1] = V - 1
    return pack(P, ex)
def setup_inputs_corners(rng):
    P = []
    for r in range(N):
        P.append([])
        for g in range(8):
            c = (g + 3 * r) % 8
            q = lively(rng, dens=0.9 if c == 7 else None); x, gv, co, aw, out, Z, B, T, U = q
            if c == 0: aw[:] = 0
            elif c == 1:
                aw[:] = 0; aw[G - 1] = 1; ready(rng, q, [G - 1]); hs = rng.permutation(G - 1)[:16]
                co[np.isin(co, hs)] = -1; co[np.arange(16), out[G - 1]] = hs
            elif c < 5:
                m, n = K + c - 3, A + c - 3; ix = np.sort(rng.permutation(G)[:m]); aw[:] = 0; aw[ix] = 1
                ready(rng, q, ix); k = ix[np.sort(rng.permutation(K - 1)[:n])]; u = U[rng.permutation(len(U))[:n]]
                alias(rng, q, k, u); co[:, u] = -1
            elif c == 5: aw[:] = 1
            elif c == 6:
                aw[:] = 1; co[:] = -1; n = min(S, G // K); j = np.arange(A)
                for t in range(n):
                    u = out[(t + 1) * K + j] if t + 1 < n else U[:A]
                    alias(rng, q, t * K + j, u); hs = rng.permutation(G); co[t, out[t * K + j]] = hs[:A]
                    if t + 1 < n: co[t, u[A - 1]] = hs[A]
            else:
                hs = rng.permutation(G)[:24]; aw[:12] = 1; alias(rng, q, np.arange(12), U[:12])
                co[np.isin(co, hs)] = -1; co[:, U[:12]] = -1; co[:, out[:12]] = -1
                for j in range(12):
                    a, b = ((16, 16), (0, 0), (8, 7 + j % 4 // 2))[j // 4]
                    co[:a, out[j]] = hs[j]; co[b:, U[j]] = hs[12 + j]
            P[r].append(q)
    return pack(P, exports(rng, P))
def setup_inputs_crowd(rng):
    P = []; k7 = np.arange(7, G, K)
    for r in range(N):
        P.append([])
        for g in range(8):
            c = (g + r) % 8; q = lively(rng); x, gv, co, aw, out, Z, B, T, U = q
            if c < 6: aw[:] = 1; co[:] = -1
            if c < 2:
                alias(rng, q, np.arange(G), np.full(G, U[0])); co[0, out[0]] = 5; co[0, out[K]] = 6
                if c == 0: alias(rng, q, [K - 1], [U[2]])
                if c == 1: alias(rng, q, k7, np.full(len(k7), U[1])); alias(rng, q, [3], [out[K - 1]])
            elif c < 4:
                gv[:15] = out[0]; x[:, out] = -1; ready(rng, q, [0]); co[np.arange(16), out[0]] = G - 1 - np.arange(16)
                if c == 3: gv[3, k7] = U[0]
            elif c < 6:
                ready(rng, q, np.arange(G))
                for i in range(16): co[i, out[:K]] = rng.permutation(G)[:K]
                co[co == G - 1] = -1; co[np.arange(16), out[:16]] = G - 1
                if c == 5: co[0, out[0]] = -1; gv[14, K - 1] = U[0]
            elif c == 7 and r < 2:
                hs = rng.permutation(G)[:(N - 1) * E]; ready(rng, q, hs); aw[:] = 0; co[:] = -1; co[0, V:] = hs
            P[r].append(q)
    ex = exports(rng, P)
    for r in range(1, N, 2):
        for g in range(8): ex[r, g] = P[r][g][4][0]
    for r in range(2):
        for d in range(1, N):
            g = far(d, 7 - r); ex[r ^ d, g, (d - 1) * E:d * E] = P[r ^ d][g][6][rng.integers(0, R, E)]
    g = far(1, 6); ex[0, g, 0] = P[0][g][8][2]
    return pack(P, ex)
def relay(rng, q):
    x, gv, co, aw, out, Z, B, T, U = q; co[:] = -1; aw[:] = 0; m = G - 1
    p = 1 + rng.permutation(G - 2); b = p[:S]; k, j, c, h, v = p[S:S + 5]
    ready(rng, q, b); gv[rng.integers(0, 15, S - 1), b[1:]] = out[b[:-1]]; co[0, out[b[:-1]]] = b[1:]
    alias(rng, q, [k, m, j, c, v], [out[m], U[0], U[0], U[1], out[b[S - 2]]])
    aw[[b[0], k, c]] = 1; co[1, out[b[S - 3]]] = m; co[1, out[b[S - 2]]] = k; co[2, out[b[S - 2]]] = j
    co[5, out[c]] = 0; co[5, U[1]] = h
    if S > 3: co[3, out[b[S - 4]]] = v
    else: aw[v] = 1
    return [(0, B[0]), (1, out[b[S - 1]]), (2, out[v])]
def quiet(rng, q, idle):
    x, gv, co, aw, out, Z, B, T, U = q; co[:] = -1; aw[:] = 0; y = rng.permutation(G)[:2]
    if idle:
        alias(rng, q, y, [V, V + 1]); aw[y] = 1
        return [(slice(E - 2, None, E), out[y[0]]), (2 * E, out[y[1]])]
    ready(rng, q, y[:1]); co[3, V + 2] = y[0]
    return []
def setup_inputs_calm(rng):
    P = []; put = []
    for r in range(N):
        P.append([])
        for g in range(8):
            odd = (g + r) % 2 == 1; end = odd and g > 5
            q = lively(rng, p=np.insert(1 + rng.permutation(V - 1), G + 2 * R + 24, 0) if end else None); P[r].append(q)
            if end: put += [(r, g, s, v) for s, v in relay(rng, q)]
            elif odd and g < 2: put += [(r, g, s, v) for s, v in quiet(rng, q, r // 2 % 2 == 0)]
            if odd: continue
            x, gv, co, aw, out, Z, B, T, U = q; n = (g // 2 + r) % 4
            co[:] = -1; aw[:] = 0; p = rng.permutation(G); b = p[:S]; a = p[S:4 * S].reshape(3, S); e = p[4 * S:7 * S].reshape(3, S); w = p[7 * S:7 * S + 3]
            ready(rng, q, b); aw[b[0]] = 1; gv[rng.integers(0, 15, S - 1), b[1:]] = out[b[:-1]]
            last = S if n else 3
            co[0, out[b[:last - 1]]] = b[1:last]
            for j in range(n):
                alias(rng, q, a[j], np.concatenate([out[a[j, 1:]], np.array([U[j] if j < 2 else W - 1])]))
                aw[a[j, 0]] = 1; co[1 + j, out[b[:-1]]] = a[j, 1:]; co[8 + np.arange(S), out[a[j]]] = w[j]
            if n == 3:
                for j in range(3):
                    ready(rng, q, e[j]); gv[0, e[j, 1:]] = out[b[:-1]]; gv[1:1 + j, e[j]] = U[10 + j]; co[4 + j, out[b[:-1]]] = e[j, 1:]
    ex = exports(rng, P)
    for r, g, s, v in put: ex[r, g, s] = v
    return pack(P, ex)
def check_inputs(d):
    bad = []
    for k, lo, hi in (("x0", -1, 15), ("gv", 0, W - 1), ("co", -1, G - 1), ("aw", 0, 1), ("ex", 0, V - 1)):
        v = np.asarray(d[k]).astype(np.float64)
        if not (np.min(v) >= lo and np.max(v) <= hi): bad.append("range of " + k)
    v = np.asarray(d["x0"]).astype(np.float32).reshape(N, 8, 16, V)
    if not np.all(v == np.floor(v)): bad.append("x0 holds whole numbers")
    if np.any(np.any(v < 0, axis=2) != np.all(v < 0, axis=2)): bad.append("a column of x0 is -1 on all rows of a group or on none")
    o = np.sort(np.asarray(d["gv"]).reshape(N, 8, 16, G)[:, :, 15], axis=-1)
    if np.min(o) < 0 or np.max(o) >= V: bad.append("range of the outputs in gv")
    if np.any(o[..., 1:] == o[..., :-1]): bad.append("outputs in gv differ")
    c = np.sort(np.asarray(d["co"]), axis=-1)
    if np.any((c[..., 1:] == c[..., :-1]) & (c[..., 1:] >= 0)): bad.append("no goal twice in a row of co")
    return bad
def reference(x0, gv, co, aw, ex):
    X = np.full((N, 8, 16, W), -1, np.int64); X[..., :V] = np.asarray(x0).astype(np.float32).astype(np.int64).reshape(N, 8, 16, V)
    GV = gv.astype(np.int64).reshape(N, 8, 16, G); CO = co.astype(np.int64).reshape(N, 8, 16, W); awake = aw.astype(np.int64)
    EX = np.stack([gentries(a) for a in ex]).astype(np.int64); F = np.tile(np.arange(W), (N, 8, 1))
    for step in range(S):
        woken = np.zeros((N, 8, G), bool); sent = np.zeros((N, 8, 16, (N - 1) * E), np.int64)
        for r in range(N):
            for g in range(8):
                x, f, c = X[r, g], F[r, g], CO[r, g]
                k = np.flatnonzero(awake[r, g])[:K]; awake[r, g, k] = 0
                n = f[GV[r, g][:, k]]; o = n[15]; free = x[0, n[:15]] < 0
                cnt = np.add.reduce(free.astype(np.int64), axis=0); M = np.maximum(np.max(x[:, n[:15]], axis=1), 0)
                u = np.add.reduce(np.where(free, n[:15], 0), axis=0)
                todo = x[0, o] < 0
                binds = todo & ((cnt == 0) | np.all(M == 15, axis=0))
                wants = todo & ~binds & (cnt == 1) & np.all(M == 0, axis=0) & (u != o)
                cand = np.flatnonzero(wants)[:A]; a, b = o[cand], u[cand]
                first = np.zeros(len(cand), bool); first[np.unique(b, return_index=True)[1]] = True
                clash = np.any((c[:, a] >= 0) & (c[:, b] >= 0), axis=0)
                ok = first & ~np.isin(b, o[binds | wants]) & ~clash; a, b = a[ok], b[ok]
                x[:, o[binds]] = M[:, binds]
                hit = c[:, o[binds]].reshape(-1); woken[r, g, hit[hit >= 0]] = True
                c[:, b] = np.where(c[:, a] >= 0, c[:, a], c[:, b])
                f[a] = b; F[r, g] = f[f]
                sent[r, g] = x[:, F[r, g][EX[r, g]]]
        for r in range(N):
            for g in range(8):
                come = np.concatenate([sent[r ^ d, far(d, g)][:, (d - 1) * E:d * E] for d in range(1, N)], axis=1)
                new = V + np.flatnonzero((X[r, g, 0, V:] < 0) & (come[0] >= 0)); X[r, g, :, V:] = come
                hit = CO[r, g][:, new].reshape(-1); woken[r, g, hit[hit >= 0]] = True
        awake[woken] = 1
    return {"yx": X.reshape(N, 128, W).astype(np.float32).astype(BF), "yf": F.astype(np.float32), "yw": awake.astype(np.float32), "yc": np.add.reduce(CO, axis=2).astype(np.float32)}

@@ -1,0 +1,542 @@
+from concourse.bass import DstId, RemoteDMATransfer
+from concourse.mybir import AluOpType as A, ActivationFunctionType as AF
+
+S, V, W, G = 5, 1440, 1536, 768
+TW = 1968
+SENT = 1952
+K0 = 50241
+BIG = float(2 ** 20)
+SA = 24
+NA, NC, NB, NV = 1024, 1024, 1536, 1536
+RA, RB = 2048, 3072
+IA, IB = 1152, 640
+
+f32, bf, i32, u16 = "float32", "bfloat16", "int32", "uint16"
+BUF = {
+    "TT": (TW, bf), "CC": (TW, i32), "CF": (1984, f32), "FF": (TW, f32), "GA": (2304, f32), "GB": (2304, f32), "GC": (256, f32),
+    "XB": (V, bf), "ZB": (V, bf), "CODE": (W, bf), "C392": (256, bf), "C15": (256, bf), "HB": (24, f32), "IDF": (124, f32), "IDU": (124, u16),
+    "GV": (G, i32), "GP": (G, f32), "AWI": (48, i32), "EXI": (6, i32),
+    "AW": (48, bf), "AWF": (48, f32), "SC": (48, bf), "PRE": (48, f32), "NK": (48, f32), "NK2": (48, f32), "POSU": (48, u16),
+    "REM": (48, f32), "REM2": (48, f32), "KC": (48, f32), "KC1": (48, f32), "KC2": (48, f32), "KCU": (48, u16), "ONES": (288, bf), "ZERO": (1024, bf),
+    "OFF": (256, u16), "GG": (4096, bf), "MX": (4096, bf), "MASK": (NV, bf), "M01": (256, f32), "DIAG": (256, f32),
+    "RL": (256, bf), "ZS": (272, f32), "OS": (272, f32), "PN": (256, bf), "EQ": (256, bf), "AO": (16, f32), "NAO": (16, f32),
+    "NDW": (16, f32), "T1": (16, f32), "T2": (16, f32), "LB": (16, u16), "LW": (352, u16), "G2": (5632, bf), "H2": (5632, bf),
+    "TAB": (784, bf), "PW": (48, bf), "PWS": (24, f32), "TWOS": (24, f32),
+    "WA": (256, bf), "PX": (256, bf), "LE": (512, bf), "KU": (2, u16), "TC": (2, f32), "OW": (256, f32),
+    "UD": (64, f32), "US": (64, f32), "UOU": (4, u16), "UOC": (4, f32), "UR": (32, f32), "UT": (64, f32), "TRI2": (64, f32),
+    "CG": (64, f32), "CL": (32, f32), "MG": (32, f32), "CT": (32, bf), "EE": (576, bf), "ES": (576, bf),
+    "X1": (2, f32), "DA": (10, f32), "UW": (2, u16), "AL": (10, u16), "RR": (16, u16),
+    "RG": (256, f32), "RS": (256, f32), "RT": (160, bf), "NEG1": (128, bf),
+    "SB": (96 * S, bf), "LD": (96 * S, bf), "NBD": (96, f32), "C1": (96, f32), "CU": (96, f32), "CM": (96, f32), "DI": (96, f32), "YY": (96, f32),
+    "D0": (128, f32), "D1": (64, f32), "D2": (32, i32), "D3": (192, i32), "D4": (192, f32), "D5": (192, f32), "D6": (12, i32),
+    "D7": (48, i32), "D8": (48, f32),
+    "PC": (1, i32), "GCI": (1, i32), "RCI": (1, i32), "PF": (1, f32), "GF": (1, f32), "RF": (1, f32), "R48": (1, f32), "WC": (8, f32),
+    "TG": (1, f32), "JR": (128, f32), "JG": (128, f32), "B8": (8, f32),
+    "ID": (128, bf), "NID": (128, bf), "BO": (128, bf), "B2K": (128, bf), "TRI": (128, bf), "WZ": (128, bf), "WN": (128, bf), "BOB": (128, bf),
+    "W2B": (128, bf), "IDB": (128, bf), "P1": (128, bf), "P2": (128, bf), "Q1": (128, bf), "Q2": (128, bf), "Q3": (128, bf),
+    "BS": (2048, bf), "WS": (2048, bf), "KE": (16, bf), "KP": (2, bf), "YC": (W, f32), "YX": (W, bf),
+}
+SCRATCH, PLACE, _fill = {}, {}, {}
+for _k, (_n, _d) in BUF.items():
+    if _n > 64 or _k in ("AWI", "EXI", "AWF"):
+        SCRATCH[_k] = ("sbuf", [128, _n], _d)
+        PLACE[_k] = (_k, 0)
+    else:
+        PLACE[_k] = ("pool_" + _d, _fill.get(_d, 0))
+        _fill[_d] = _fill.get(_d, 0) + (_n + 15) // 16 * 16
+for _d, _n in _fill.items():
+    SCRATCH["pool_" + _d] = ("sbuf", [128, _n], _d)
+for _b in range(8):
+    SCRATCH["PS%d" % _b] = ("psum", [128, 512], f32)
+NDMA = 48
+SEMAPHORES = ["sv", "sa", "sp", "sg", "sent"] + ["arr%d" % s for s in range(S)] + ["d%d" % k for k in range(NDMA)]
+
+
+def send_masks(src, peers, topo):
+    near = [p for p in peers if p in topo.cores_of(src)]
+    far = [p for p in peers if p not in near]
+    out, used = {}, []
+    for grp in (far, near):
+        for k, p in enumerate(grp):
+            free = [e for e in topo.engines(src, p) if e not in used]
+            n = max(1, len(free) // (len(grp) - k))
+            while n & (n - 1):
+                n -= 1
+            out[p] = free[:n]
+            used += free[:n]
+    return out
+
+
+def rank_program(g, core, T, topo):
+    rank = T.rank_of(core)
+    if rank is None:
+        return
+    N = len(T.cores)
+    ops = []
+
+    def v(name, lo=0, hi=None, step=1, p=None):
+        n = 512 if name.startswith("PS") else BUF[name][0]
+        return ("v", name, lo, n if hi is None else hi, step, p)
+
+    def ind(win, off):
+        return ("i", win, off)
+
+    def ap(x):
+        if not isinstance(x, tuple):
+            return x
+        if x[0] == "i":
+            return ap(x[1]).indirect(ap(x[2]))
+        _, name, lo, hi, step, p = x
+        ps = slice(None) if p is None else slice(*p)
+        name, base = PLACE.get(name, (name, 0))
+        lo, hi = lo + base, hi + base
+        return T[name][ps, lo:hi:step] if step != 1 else T[name][ps, lo:hi]
+
+    def spans(xs):
+        return [(x[1], x[2], x[3]) for x in xs if isinstance(x, tuple) and x[0] == "v"]
+
+    def op(q, fn, outs, ins, kind="c"):
+        rd, wr = [], []
+        for x in outs:
+            if isinstance(x, tuple) and x[0] == "i":
+                wr += spans([x[1]])
+                rd += spans([x[2]])
+            else:
+                wr += spans([x])
+        for x in ins:
+            rd += spans([x[1], x[2]]) if isinstance(x, tuple) and x[0] == "i" else spans([x])
+        ops.append((q, fn, rd, wr, kind))
+
+    def cp(o, i):
+        op("v", lambda: g.vector.tensor_copy(ap(o), ap(i)), [o], [i])
+
+    def tt(o, a, b, f):
+        op("v", lambda: g.vector.tensor_tensor(ap(o), ap(a), ap(b), f), [o], [a, b])
+
+    def ts(o, a, s1, f1, s2=None, f2=None):
+        if f2 is None:
+            op("v", lambda: g.vector.tensor_scalar(ap(o), ap(a), ap(s1), None, f1), [o], [a, s1])
+        else:
+            op("v", lambda: g.vector.tensor_scalar(ap(o), ap(a), ap(s1), ap(s2), f1, f2), [o], [a, s1, s2])
+
+    def scan(o, d0, d1, f0, f1, init=0.0):
+        op("v", lambda: g.vector.tensor_tensor_scan(ap(o), ap(d0), ap(d1), init, f0, f1), [o], [d0, d1])
+
+    def ms(o, c):
+        op("v", lambda: g.vector.memset(ap(o), c), [o], [])
+
+    def act(o, i, f=AF.Identity, bias=0.0, scale=1.0):
+        if o[0] == "i":
+            op("a", lambda: g.scalar.activation(ap(o), ap(i), f), [o], [i])
+        else:
+            op("a", lambda: g.scalar.activation(ap(o), ap(i), f, bias=ap(bias), scale=ap(scale)), [o], [i, bias, scale])
+
+    def mul(o, i, scale, bias=0.0):
+        act(o, i, AF.Identity, bias, scale)
+
+    def fill(o, c):
+        act(o, v("ZERO", 0, len(range(o[2], o[3], o[4]))), AF.Identity, c, 0.0)
+
+    def mm(items, start=True, stop=True):
+        def fn():
+            last = None
+            for k, (o, l, r) in enumerate(items):
+                first = start and all(o != z[0] for z in items[:k])
+                final = stop and all(o != z[0] for z in items[k + 1:])
+                last = g.tensor.matmul(ap(o), ap(l), ap(r), first, final)
+            return last
+        op("p", fn, [x[0] for x in items], [y for x in items for y in x[1:]])
+
+    def iota(o, pat, base=0, cm=0):
+        if BUF[o[1]][1] == i32:
+            op("g", lambda: g.iota(ap(o), pat, base, cm), [o], [])
+        else:
+            op("g", lambda: g.iota(ap(o), pat, base, cm, allow_small_or_imprecise_dtypes=True), [o], [])
+
+    def keep(o, i, pat, f, base, cm):
+        op("g", lambda: g.affine_select(ap(o), ap(i), pat, f, 0.0, base, cm), [o], [i])
+
+    def dma(o, i, q="s"):
+        e = g.sync if q == "s" else g.scalar
+        op(q, lambda: e.dma_start(ap(o), ap(i)), [o], [i], "d")
+
+    peers = [T.cores[rank ^ d] for d in range(1, N)]
+    masks = send_masks(core, peers, topo)
+    arrive = sum(len(send_masks(p, [T.cores[T.rank_of(p) ^ d] for d in range(1, N)], topo)[core]) for p in peers)
+    leave = sum(len(m) for m in masks.values())
+
+    def send(s):
+        def fn():
+            tr = []
+            for d in range(N - 1, 0, -1):
+                p = peers[d - 1]
+                rid, pid = topo.addr(p, core)
+                c = 96 * s + 32 * (d - 1)
+                tr.append(RemoteDMATransfer(dst_ids=[DstId(rid=rid, pnc=pid)], dma_engine_mask=sum(1 << e for e in masks[p]),
+                                            remote_sem=T.sem["arr%d" % s], src=T.SB[:, c:c + 32], dst=T.LD[:, c:c + 32]))
+            g.remote_dma_fused(tr, local_sem=T.sem.sent)
+        op("g", fn, [], [v("SB", 96 * s, 96 * s + 96)], "r")
+
+    def arrival(s):
+        op("p", lambda: g.tensor.wait_ge(T.sem["arr%d" % s], arrive), [], [], "w")
+
+    dma(v("AWI"), T.aw[:])
+    dma(v("XB"), T.x0[:], "a")
+    dma(v("GV"), T.gv[:])
+    dma(v("EXI"), T.ex[:])
+    iota(v("PC"), [[1, 1]], 0, 1)
+    iota(v("JR"), [[1, 128]])
+    iota(v("JG"), [[1, 8], [0, 16]])
+    ms(v("ZERO"), 0.0)
+    dma(v("WS", 1024, 2048), v("ZERO"))
+    dma(v("TAB"), v("ZERO", 0, 784))
+    dma(v("TT", W, TW), v("ZERO", 0, TW - W))
+    fill(v("ONES"), 1.0)
+    fill(v("TWOS"), 2.0)
+    fill(v("GA", 0, 256), 0.0)
+    fill(v("GB", 0, 256), 0.0)
+    fill(v("KP"), 32768.0)
+    fill(v("KE"), -491520.0)
+    fill(v("ZS", 256, 272), float(K0 + SENT))
+    fill(v("OS", 256, 272), float(K0 + SENT))
+    fill(v("NBD"), 1024.0)
+    keep(v("ID"), v("ONES", 0, 128), [[-1, 128]], A.is_equal, 0, 1)
+    ts(v("RCI"), v("PC"), 15, A.bitwise_and)
+    ts(v("GCI"), v("PC"), 4, A.arith_shift_right)
+    cp(v("RF"), v("RCI"))
+    cp(v("GF"), v("GCI"))
+    ts(v("DIAG", 0, 16), v("JR", 0, 16), v("RF"), A.is_equal)
+    ts(v("BO"), v("JG"), v("GF"), A.is_equal)
+    keep(v("TRI"), v("BO"), [[1, 128]], A.is_gt, 0, -1)
+    ts(v("R48"), v("RF"), 48.0, A.mult)
+    ts(v("WC", 4, 5), v("DIAG", 0, 1), -1.0, A.mult)
+    ts(v("WC", 5, 6), v("DIAG", 2, 3), -391.0, A.mult, -1.0, A.add)
+    ts(v("WC", 6, 7), v("DIAG", 1, 2), -1.0, A.mult)
+    ts(v("KCU"), v("JR", 0, 48), v("R48"), A.add)
+    ts(v("HB"), v("JR", 0, 24), v("WC", 6, 7), A.mult, v("WC", 5, 6), A.add)
+    ts(v("KC1"), v("JR", 0, 48), v("R48"), A.add, float(G), A.add)
+    ts(v("KC2"), v("JR", 0, 48), v("R48"), A.add, float(G + 1), A.add)
+    ts(v("B2K"), v("BO"), 2048.0, A.mult)
+    ts(v("B8"), v("JR", 0, 8), v("GF"), A.is_equal)
+    scan(v("PWS"), v("TWOS"), v("ZERO", 0, 24), A.mult, A.add, 0.5)
+    cp(v("AW"), v("AWI"))
+    iota(v("MASK", 0, 384), [[0, 24], [16, 16]])
+    for q in range(1, 4):
+        dma(v("MASK", 384 * q, 384 * q + 384), v("MASK", 0, 384))
+    dma(v("CC", 0, W), T.co[:])
+    for q in range(1, 16):
+        dma(v("DIAG", 16 * q, 16 * q + 16), v("DIAG", 0, 16))
+    for r in range(16):
+        keep(v("BS", 128 * r, 128 * r + 128), v("B2K"), [[0, 8], [1, 16]], A.is_equal, -r, 0)
+    iota(v("NDW"), [[-16, 16]], -W)
+    for h in range(24):
+        mul(v("CODE", 64 * h, 64 * h + 64), v("JR", 0, 64), v("WC", 4, 5), v("HB", h, h + 1))
+    mul(v("NID"), v("ID"), -8192.0)
+    act(v("ZB"), v("XB"), AF.Relu, 0.0, -1.0)
+    mul(v("PW", 0, 48, 2), v("PWS"), 1.0)
+    mul(v("PW", 1, 48, 2), v("PWS"), -1.0)
+    for q in range(16):
+        dma(v("TAB", 1 + 48 * q, 49 + 48 * q, p=(q, 128, 16)), v("PW", p=(0, 8)))
+
+    def consts_a():
+        mul(v("WC", 0, 1), v("DIAG", 1, 2), 64.0, v("DIAG", 0, 1))
+        mul(v("WC", 1, 2), v("DIAG", 2, 3), 128.0, v("WC", 0, 1))
+        mul(v("WC", 2, 3), v("WC", 1, 2), -1.0)
+        mul(v("WZ"), v("BO"), v("WC", 1, 2))
+        fill(v("C15"), 15.0)
+        mul(v("WN"), v("BO"), v("WC", 2, 3))
+        for r in range(8):
+            keep(v("WS", 128 * r, 128 * r + 128), v("WN"), [[0, 8], [1, 16]], A.is_equal, -r, 0)
+        iota(v("CC", W, TW), [[0, TW - W]], -1)
+        keep(v("M01"), v("ONES", 0, 256), [[0, 16], [1, 16]], A.is_gt, 0, 0)
+        iota(v("DA"), [[16, 10]], W + 256)
+
+    def consts_b():
+        for r in range(8, 16):
+            mul(v("WS", 129 * r, 128 * r + 128, 16), v("B8"), v("WC", 2, 3))
+        mul(v("WC", 3, 4), v("DIAG", 2, 3), BIG)
+        mul(v("BOB"), v("BO"), BIG)
+        mul(v("IDB"), v("ID"), BIG)
+        mul(v("W2B"), v("BO"), v("WC", 3, 4))
+        fill(v("C392"), 392.0)
+
+    def consts_c():
+        ts(v("NDW"), v("NDW"), v("RF"), A.subtract)
+        cp(v("RR", 0, 6), v("EXI"))
+        cp(v("PF"), v("PC"))
+        ts(v("TC"), v("JR", 0, 32, 16), v("RF"), A.add)
+        ts(v("TG"), v("RF"), 2.0, A.mult, v("PF"), A.subtract)
+
+    def consts_e():
+        ts(v("P1"), v("JR"), -112.0, A.add, v("TG"), A.is_equal)
+        ts(v("TRI2", 0, 32), v("JR", 0, 32), v("TC", 0, 1), A.is_lt)
+        ts(v("TRI2", 32, 64), v("JR", 0, 32), v("TC", 1, 2), A.is_lt)
+        ts(v("DA"), v("DA"), v("RF"), A.add)
+
+    def consts_f():
+        mul(v("Q1"), v("P1"), 8192.0)
+        mul(v("Q2", 16, 128), v("P1", 0, 112), 8192.0)
+        mul(v("Q2", 0, 16), v("P1", 112, 128), 8192.0)
+        mul(v("Q3"), v("ID"), 8192.0)
+        mul(v("P2", 16, 128), v("P1", 0, 112), 1.0)
+        mul(v("P2", 0, 16), v("P1", 112, 128), 1.0)
+        mul(v("DI"), v("CODE", V, W), -1.0, -1.0)
+
+    def init_table():
+        for b in range(3):
+            lo, hi = 480 * b, 480 * b + 480
+            mm([(v("PS%d" % b, 0, 480), v("ID"), v("XB", lo, hi)), (v("PS%d" % b, 0, 480), v("NID"), v("ZB", lo, hi))])
+        for b in range(3):
+            lo, hi = 480 * b, 480 * b + 480
+            tt(v("TT", lo, hi), v("PS%d" % b, 0, 480), v("CODE", lo, hi), A.max)
+        mul(v("TT", V, W), v("CODE", V, W), 1.0)
+
+    TTw, FFw = v("TT"), v("FF")
+
+    def sums(bank, src, lo, hi, start=False, stop=False):
+        mm([(v(bank, 0, 64), v("ID"), v(src, c, c + 64)) for c in range(lo, hi, 64)], start, stop)
+
+    def relu(lo, hi, q="v"):
+        if q == "v":
+            ts(v("H2", lo, hi), v("G2", lo, hi), 0.0, A.max)
+        else:
+            act(v("H2", lo, hi), v("G2", lo, hi), AF.Relu)
+
+    for s in range(S):
+        last = s == S - 1
+        CN = "CC" if s == 0 else "CF"
+        CCw = v(CN, 0, TW)
+        scan(v("SC"), v("ONES", 0, 48), v("AW"), A.mult, A.add)
+        mm([(v("PS4", 32, 33), v("TRI"), v("SC", 47, 48))])
+        tt(v("NK2"), v("AW"), v("KC2"), A.mult)
+        tt(v("NK"), v("SC"), v("KC1"), A.add)
+        tt(v("PRE"), v("NK"), v("NK2"), A.subtract)
+        ts(v("POSU"), v("PRE"), v("PS4", 32, 33), A.add)
+        if s == 0:
+            ts(v("GP"), ind(v("GV"), v("KCU")), -1.0, A.mult, float(SENT), A.add)
+        cp(ind(v("GA"), v("POSU", 0, SA)), v("GP", 0, 16 * SA))
+        act(ind(v("GB"), v("POSU", SA, 48)), v("GP", 16 * SA, G), AF.Silu)
+        ts(v("REM2"), v("SC"), v("PS4", 32, 33), A.add, 257.0, A.is_ge)
+        if s == 0:
+            init_table()
+            consts_a()
+        else:
+            mul(v("NBD"), v("TT", V, W), -1024.0)
+        for lo, hi in ((0, NA // 16), (NA // 16, 256)):
+            tt(v("GC", lo, hi), v("GA", lo, hi), v("GB", lo, hi), A.max)
+        for lo, hi in ((0, NA // 16), (NA // 16, 256)):
+            ts(v("OFF", lo, hi), v("GC", lo, hi), -1.0, A.mult, SENT + 0.25, A.add)
+        act(v("GG", 0, NA), ind(TTw, v("OFF", 0, NA // 16)))
+        cp(v("GG", NA + NB, 4096), ind(TTw, v("OFF", (NA + NB) // 16, 256)))
+        act(v("GG", NA, NA + NC), ind(TTw, v("OFF", NA // 16, (NA + NC) // 16)))
+        act(v("GG", NA + NC, NA + NB), ind(TTw, v("OFF", (NA + NC) // 16, (NA + NB) // 16)))
+        chunks = ((0, NA), (NA + NB, 4096), (NA, NA + NC), (NA + NC, NA + NB))
+        if s == 0:
+            consts_b()
+        for lo, hi in chunks:
+            o = v("PS0", lo // 16, hi // 16)
+            mm([(o, v("ID"), v("C15", lo // 16, hi // 16))] + [(o, v("WZ"), v("GG", lo + i, hi, 16)) for i in range(15)])
+        for lo, hi in chunks:
+            scan(v("MX", lo, hi), v("MASK", 0, hi - lo), v("GG", lo, hi), A.min, A.max)
+        mm([(v("PS4", 0, 16), v("WS", 128 * r, 128 * r + 128), v("GG", 16 * r + 15, 4096, 256)) for r in range(16)])
+        tt(v("RL"), v("PS0", 0, 256), v("MX", 14, 4096, 16), A.max)
+        act(v("AO"), v("PS4", 0, 16), AF.Abs, float(-K0), 1.0)
+        mul(v("NAO"), v("AO"), -1.0)
+        mul(v("ZS", 0, 256), v("PS0", 0, 256), -1.0, 15.0)
+        act(v("PN"), v("ZS", 0, 256), AF.Relu, float(-K0 - W + 1), 1.0)
+        mm([(v("PS3", 0, 16), v("ID"), v("KE"))] +
+           [(v("PS3", 0, 16), v("BS", 128 * r, 128 * r + 128), v("RL", r, 256, 16)) for r in range(16)])
+        mm([(v("PS1", 0, 256), v("WN"), v("GG", 15, 4096, 16))])
+        tt(v("REM"), v("REM2"), v("AW"), A.mult)
+        if s == 0:
+            consts_c()
+        if last:
+            cp(ind(TTw, v("AL", 0, 8)), v("NEG1"))
+        mul(v("OS", 0, 256), v("PS1", 0, 256), 1.0)
+        tt(v("T1"), v("PS3", 0, 16), v("NAO"), A.min)
+        tt(v("T2"), v("T1"), v("NDW"), A.max)
+        ts(v("LB"), v("T2"), -1.0, A.mult)
+        ts(v("LW", 0, 256), ind(CCw, v("LB")), 1.0, A.add)
+        tt(v("EQ"), v("PS1", 0, 256), v("ZS", 0, 256), A.is_equal)
+        mm([(v("PS2", 0, 256), v("IDB"), v("C392")), (v("PS2", 0, 256), v("W2B"), v("GG", 15, 4096, 16)),
+            (v("PS2", 0, 256), v("BOB"), v("MX", 14, 4096, 16)), (v("PS2", 0, 256), v("IDB"), v("PN")),
+            (v("PS2", 0, 256), v("IDB"), v("EQ"))])
+        cp(ind(TTw, v("LB")), v("MX", 14, 4096, 16))
+        ts(v("SB", 96 * s, 96 * s + 96), ind(TTw, v("RR", 0, 6)), -1.0, A.max, 1.0, A.add)
+        if s == 0:
+            iota(v("IDF"), [[16, 124]])
+            iota(v("FF"), [[1, TW]])
+        send(s)
+        if s == 0:
+            consts_e()
+        for q in range(4):
+            act(v("G2", 1024 * q, 1024 * q + 1024), ind(v("TAB"), v("LW", 64 * q, 64 * q + 64)))
+        if s == 0:
+            consts_f()
+        relu(0, RA // 2, "a")
+        relu(RA // 2, RA, "a")
+        tt(v("WA"), v("PS2", 0, 256), v("ZS", 0, 256), A.is_lt)
+        scan(v("PX"), v("ONES", 0, 256), v("WA"), A.mult, A.add)
+        tt(v("OW"), v("PS1", 0, 256), v("WA"), A.mult)
+        ts(v("LE", 0, 256), v("PX"), v("TC", 0, 1), A.is_le)
+        ts(v("LE", 256, 512), v("PX"), v("TC", 1, 2), A.is_le)
+        scan(v("EE", 0, 256), v("ONES", 0, 256), v("LE", 0, 256), A.mult, A.add)
+        scan(v("EE", 256, 512), v("ONES", 0, 256), v("LE", 256, 512), A.mult, A.add)
+        cp(v("KU"), v("EE", 255, 512, 256))
+        sums("PS5", "G2", 0, 2048, True)
+        tt(v("UD", 0, 32), ind(v("ZS"), v("KU")), v("DIAG", 0, 32), A.mult)
+        tt(v("UD", 32, 64), ind(v("OS"), v("KU")), v("DIAG", 0, 32), A.mult)
+        tt(v("UT", 0, 32), ind(v("ZS"), v("KU")), v("TRI2", 0, 32), A.mult)
+        scan(v("US"), v("M01", 0, 64), v("UD"), A.mult, A.add)
+        tt(v("UT", 32, 64), ind(v("ZS"), v("KU")), v("TRI2", 32, 64), A.mult)
+        ts(v("UOU"), v("US", 15, 64, 16), float(-K0), A.add)
+        ts(v("EE", 0, 256), v("OW"), v("US", 15, 16), A.is_equal, 2048.0, A.mult)
+        cp(v("CG"), ind(CCw, v("UOU")))
+        ts(v("EE", 256, 288), v("UT", 0, 32), v("US", 15, 16), A.is_equal, 2048.0, A.mult)
+        tt(v("CL"), v("CG", 0, 32), v("CG", 32, 64), A.min)
+        scan(v("ES", 0, 288), v("ONES"), v("EE", 0, 288), A.mult, A.max)
+        ts(v("EE", 544, 576), v("UT", 32, 64), v("US", 31, 32), A.is_equal, 2048.0, A.mult)
+        tt(v("CT"), ind(TTw, v("UOU", 0, 2)), v("CL"), A.max)
+        mm([(v("PS3", 32, 34), v("ID"), v("KP"))] +
+           [(v("PS3", 32, 34), v("BS", 128 * r, 128 * r + 128), v("CT", r, 32, 16)) for r in range(16)])
+        ts(v("EE", 288, 544), v("OW"), v("US", 31, 32), A.is_equal, 2048.0, A.mult)
+        ts(v("UOC"), v("US", 15, 64, 16), float(K0 + W), A.min, float(-K0), A.add)
+        scan(v("ES", 288, 576), v("ONES"), v("EE", 288, 576), A.mult, A.max)
+        tt(v("MG"), v("CG", 0, 32), v("CG", 32, 64), A.max)
+        tt(v("X1"), v("PS3", 32, 34), v("ES", 287, 576, 288), A.max)
+        ts(v("UR"), ind(v("ZS"), v("KU")), float(-K0), A.add)
+        for c in range(2):
+            ts(v("UW", c, c + 1), v("X1", c, c + 1), v("DA", 2 * s + c, 2 * s + c + 1), A.min, v("UOC", c, c + 1), A.max)
+        for c in range(2):
+            ts(v("AL", 2 * s + c, 2 * s + c + 1), v("X1", c, c + 1), v("DA", 2 * s + c, 2 * s + c + 1), A.min, v("UOC", 2 + c, 3 + c), A.max)
+        cp(ind(CCw, v("UW")), v("MG"))
+        cp(v("RR", 6 + 2 * s, 8 + 2 * s), v("AL", 2 * s, 2 * s + 2))
+        ts(v("C1"), v(CN, V, W), 1.0, A.add)
+        cp(ind(FFw, v("AL", 2 * s, 2 * s + 2)), v("UR"))
+        tt(v("CU"), v("C1"), v("NBD"), A.min)
+        sums("PS5", "G2", 2048, 4096)
+        relu(RA, RB)
+        sums("PS6", "H2", 0, RA // 2, True)
+        arrival(s)
+        c = 96 * s
+        mm([(v("PS7", 32 * d, 32 * d + 32), v(("Q1", "Q2", "Q3")[d]), v("LD", c + 32 * d, c + 32 * d + 32)) for d in range(3)])
+        for d in range(3):
+            mm([(v("PS2", 32 * d, 32 * d + 32), v(("P1", "P2", "ID")[d]), v("LD", c + 32 * d, c + 32 * d + 32)),
+                (v("PS2", 32 * d, 32 * d + 32), v("ID"), v("CODE", V + 32 * d, V + 32 * d + 32))])
+        sums("PS6", "H2", RA, RB)
+        sums("PS6", "H2", RA // 2, RA)
+        tt(v("CM"), v("PS7", 0, 96), v("CU"), A.min)
+        cp(v("LW", 256, 352), v("CM"))
+        relu(RB, 4096)
+        sums("PS6", "H2", RB, 4096)
+        cp(v("G2", 4096 + IA, 5632), ind(v("TAB"), v("LW", 256 + IA // 16, 352)))
+        act(v("G2", 4096, 4096 + IB), ind(v("TAB"), v("LW", 256, 256 + IB // 16)))
+        act(v("G2", 4096 + IB, 4096 + IA), ind(v("TAB"), v("LW", 256 + IB // 16, 256 + IA // 16)))
+        parts = ((4096, 4096 + IB), (4096 + IA, 5632), (4096 + IB, 4096 + IA))
+        for k, (lo, hi) in enumerate(parts):
+            relu(lo, hi)
+            sums("PS5", "G2", lo, hi, False, k == 2)
+            sums("PS6", "H2", lo, hi, False, k == 2)
+        tt(v("YY"), v("PS7", 0, 96), v("DI"), A.min)
+        nr, na = 8 + 2 * s, 2 * s + 2
+        if not last:
+            tt(v("RG", 0, 16 * nr), ind(FFw, v("RR", 0, nr)), v("DIAG", 0, 16 * nr), A.mult)
+            tt(v("TT", V, W), v("PS2", 0, 96), v("YY"), A.add)
+            fill(v("GA", 0, 256), 0.0)
+            fill(v("GB", 0, 256), 0.0)
+        else:
+            act(v("RG", 0, 160), ind(FFw, v("RR", 6, 16)))
+            tt(v("TT", V, W), v("PS2", 0, 96), v("YY"), A.add)
+            for b in range(3):
+                mm([(v("PS%d" % b, p=(0, 8)), v("B8"), v("CF", 512 * b, 512 * b + 512))])
+            ts(v("YX"), v("TT", 0, W), -1.0, A.max)
+            dma(T.yx[:], v("YX"))
+        cp(v("D0", 0, 128, 2), v("PS6", 0, 64))
+        tt(v("D0", 1, 128, 2), v("D0", 0, 128, 2), v("PS5", 0, 64), A.subtract)
+        if not last:
+            scan(v("RS", 0, 16 * nr), v("M01", 0, 16 * nr), v("RG", 0, 16 * nr), A.mult, A.add)
+        else:
+            cp(ind(FFw, v("AL")), v("RG", 0, 160))
+            dma(T.yf[:], v("FF", 0, W, p=(0, 128, 16)))
+            for b in range(3):
+                mul(v("YC", 512 * b, 512 * b + 512, p=(0, 8)), v("PS%d" % b, p=(0, 8)), 1.0)
+            dma(T.yc[:], v("YC", p=(0, 8)), "a")
+        tt(v("D1"), v("D0", 0, 64), v("D0", 64, 128), A.add)
+        if not last:
+            cp(v("RR", 0, nr), v("RS", 15, 16 * nr, 16))
+            act(v("RT", 0, 16 * na), ind(TTw, v("RR", 6, 6 + na)))
+        if s == 0:
+            ts(v("IDU"), v("IDF"), v("RF"), A.add, float(TW - 1), A.min)
+            act(v("CF"), ind(CCw, v("IDU")))
+        if s == S - 2:
+            fill(v("NEG1"), -1.0)
+        for w in range(2):
+            tt(v("D2", 16 * w, 16 * w + 16), v("D1", w, 32, 2), v("D1", 32 + w, 64, 2), A.add)
+        for k in range(6):
+            ts(v("D3", 32 * k, 32 * k + 32), v("D2"), k, A.logical_shift_right, 0o01010101, A.bitwise_and)
+        cp(v("D4"), v("D3"))
+        scan(v("D5"), v("M01", 0, 192), v("D4"), A.mult, A.add)
+        if not last:
+            cp(ind(TTw, v("AL", 0, na)), v("RT", 0, 16 * na))
+        cp(v("D6"), v("D5", 15, 192, 16))
+        for f in range(4):
+            ts(v("D7", 12 * f, 12 * f + 12), v("D6"), 63 << (6 * f), A.bitwise_and)
+        tt(v("D8"), v("D7"), v("REM"), A.max)
+        if not last:
+            ts(v("AW"), v("D8"), 1.0, A.min)
+        else:
+            ts(v("AWF"), v("D8"), 1.0, A.min)
+            dma(T.yw[:], v("AWF"))
+
+    Q = {"v": g.vector, "a": g.scalar, "p": g.tensor, "g": g, "s": g.sync}
+    SEM = {"v": "sv", "a": "sa", "p": "sp", "g": "sg"}
+    count = {k: 0 for k in SEMAPHORES}
+    known = {q: {} for q in Q}
+    hist = {}
+    nd = 0
+    waited = {}
+    for q, fn, rd, wr, kind in ops:
+        need = {}
+        for spn, isw in [(x, False) for x in rd] + [(x, True) for x in wr]:
+            name, lo, hi = spn
+            ps = name.startswith("PS")
+            for (l2, h2, w2, q2, sem, val, kn) in hist.get(name, []):
+                if ps and q2 != q:
+                    hit = True
+                elif name == "TAB" and isw and q2 == q and h2 - l2 == 48:
+                    hit = False
+                else:
+                    hit = l2 < hi and lo < h2 and (isw or w2) and not (q == "p" and q2 == "p")
+                if hit and known[q].get(sem, 0) < val and need.get(sem, (0,))[0] < val:
+                    need[sem] = (val, kn)
+        for sem, (val, kn) in sorted(need.items(), key=lambda z: -len(z[1][1])):
+            if known[q].get(sem, 0) >= val:
+                continue
+            Q[q].wait_ge(T.sem[sem], val)
+            known[q][sem] = val
+            waited[sem] = max(waited.get(sem, 0), val)
+            for k2, v2 in kn.items():
+                if known[q].get(k2, 0) < v2:
+                    known[q][k2] = v2
+        ins = fn()
+        if kind in "rw":
+            continue
+        if kind == "d":
+            sem = "d%d" % nd
+            nd += 1
+            count[sem] += 16
+            ins.then_inc(T.sem[sem], 16)
+        else:
+            sem = SEM[q]
+            count[sem] += 1
+            ins.then_inc(T.sem[sem], 1)
+        kn = dict(known[q])
+        for spn, isw in [(x, False) for x in rd] + [(x, True) for x in wr]:
+            h = hist.setdefault(spn[0], [])
+            if isw:
+                h[:] = [e for e in h if not (spn[1] <= e[0] and e[1] <= spn[2] and known[q].get(e[4], 0) >= e[5])]
+            h.append((spn[1], spn[2], isw, q, sem, count[sem], kn))
+    g.wait_ge(T.sem.sent, leave * S)
+    for k, n in count.items():
+        if n > waited.get(k, 0):
+            g.wait_ge(T.sem[k], n)

@@ -6,10 +6,10 @@ TW = 1968
 SENT = 1952
 K0 = 50241
 BIG = float(2 ** 20)
-SA = 24
+SA = 22
 NA, NC, NB, NV = 1024, 1024, 1536, 1536
 RA, RB = 2048, 3072
-IA, IB = 1152, 640
+IA, IB = 832, 512
 
 f32, bf, i32, u16 = "float32", "bfloat16", "int32", "uint16"
 BUF = {
@@ -17,24 +17,23 @@ BUF = {
     "XB": (V, bf), "ZB": (V, bf), "CODE": (W, bf), "C392": (256, bf), "C15": (256, bf), "HB": (24, f32), "IDF": (124, f32), "IDU": (124, u16),
     "GV": (G, i32), "GP": (G, f32), "AWI": (48, i32), "EXI": (6, i32),
     "AW": (48, bf), "AWF": (48, f32), "SC": (48, bf), "PRE": (48, f32), "NK": (48, f32), "NK2": (48, f32), "POSU": (48, u16),
-    "REM": (48, f32), "REM2": (48, f32), "KC": (48, f32), "KC1": (48, f32), "KC2": (48, f32), "KCU": (48, u16), "ONES": (288, bf), "ZERO": (1024, bf),
-    "OFF": (256, u16), "GG": (4096, bf), "MX": (4096, bf), "MASK": (NV, bf), "M01": (256, f32), "DIAG": (256, f32),
+    "REM": (48, f32), "REM2": (48, f32), "KC1": (48, f32), "KC2": (48, f32), "KCU": (48, u16), "ONES": (288, bf), "ZERO": (1024, bf),
+    "OFF": (256, u16), "GG": (4096, bf), "MX": (4096, bf), "MASK": (NV, bf), "M01": (192, f32), "DIAG": (32, f32),
     "RL": (256, bf), "ZS": (272, f32), "OS": (272, f32), "PN": (256, bf), "EQ": (256, bf), "AO": (16, f32), "NAO": (16, f32),
     "NDW": (16, f32), "T1": (16, f32), "T2": (16, f32), "LB": (16, u16), "LW": (352, u16), "G2": (5632, bf), "H2": (5632, bf),
     "TAB": (784, bf), "PW": (48, bf), "PWS": (24, f32), "TWOS": (24, f32),
-    "WA": (256, bf), "PX": (256, bf), "LE": (512, bf), "KU": (2, u16), "TC": (2, f32), "OW": (256, f32),
-    "UD": (64, f32), "US": (64, f32), "UOU": (4, u16), "UOC": (4, f32), "UR": (32, f32), "UT": (64, f32), "TRI2": (64, f32),
+    "WA": (256, bf), "PX": (256, bf), "LE": (512, bf), "KU": (2, u16), "TC": (2, f32),
+    "UD": (64, f32), "US": (64, f32), "UOU": (4, u16), "UOC": (4, f32), "UR": (32, f32), "UT": (64, f32), "TRI2": (64, f32), "UB": (2, f32),
     "CG": (64, f32), "CL": (32, f32), "MG": (32, f32), "CT": (32, bf), "EE": (576, bf), "ES": (576, bf),
     "X1": (2, f32), "DA": (10, f32), "UW": (2, u16), "AL": (10, u16), "RR": (16, u16),
-    "RG": (256, f32), "RS": (256, f32), "RT": (160, bf), "NEG1": (128, bf),
-    "SB": (96 * S, bf), "LD": (96 * S, bf), "NBD": (96, f32), "C1": (96, f32), "CU": (96, f32), "CM": (96, f32), "DI": (96, f32), "YY": (96, f32),
-    "D0": (128, f32), "D1": (64, f32), "D2": (32, i32), "D3": (192, i32), "D4": (192, f32), "D5": (192, f32), "D6": (12, i32),
-    "D7": (48, i32), "D8": (48, f32),
+    "RG": (256, f32), "RT": (160, bf), "NEG1": (128, bf),
+    "SB": (96 * S, bf), "LD": (96 * S, bf), "NBD": (96, bf), "CM": (96, f32), "DI": (96, f32), "YY": (96, f32),
+    "D0": (128, f32), "D1": (64, f32), "D2": (32, i32), "D3": (192, i32), "D4": (192, f32), "D5": (192, f32), "D6": (12, i32), "D7": (48, i32),
     "PC": (1, i32), "GCI": (1, i32), "RCI": (1, i32), "PF": (1, f32), "GF": (1, f32), "RF": (1, f32), "R48": (1, f32), "WC": (8, f32),
     "TG": (1, f32), "JR": (128, f32), "JG": (128, f32), "B8": (8, f32),
     "ID": (128, bf), "NID": (128, bf), "BO": (128, bf), "B2K": (128, bf), "TRI": (128, bf), "WZ": (128, bf), "WN": (128, bf), "BOB": (128, bf),
     "W2B": (128, bf), "IDB": (128, bf), "P1": (128, bf), "P2": (128, bf), "Q1": (128, bf), "Q2": (128, bf), "Q3": (128, bf),
-    "BS": (2048, bf), "WS": (2048, bf), "KE": (16, bf), "KP": (2, bf), "YC": (W, f32), "YX": (W, bf),
+    "BS": (2048, bf), "WS": (2048, bf), "BF": (2048, f32), "KE": (16, bf), "KP": (2, bf), "YC": (W, f32), "YX": (TW, bf), "YR": (TW, bf),
 }
 SCRATCH, PLACE, _fill = {}, {}, {}
 for _k, (_n, _d) in BUF.items():
@@ -48,7 +47,7 @@ for _d, _n in _fill.items():
     SCRATCH["pool_" + _d] = ("sbuf", [128, _n], _d)
 for _b in range(8):
     SCRATCH["PS%d" % _b] = ("psum", [128, 512], f32)
-NDMA = 48
+NDMA = 36
 SEMAPHORES = ["sv", "sa", "sp", "sg", "sent"] + ["arr%d" % s for s in range(S)] + ["d%d" % k for k in range(NDMA)]
 
 
@@ -122,9 +121,6 @@ def rank_program(g, core, T, topo):
     def scan(o, d0, d1, f0, f1, init=0.0):
         op("v", lambda: g.vector.tensor_tensor_scan(ap(o), ap(d0), ap(d1), init, f0, f1), [o], [d0, d1])
 
-    def ms(o, c):
-        op("v", lambda: g.vector.memset(ap(o), c), [o], [])
-
     def act(o, i, f=AF.Identity, bias=0.0, scale=1.0):
         if o[0] == "i":
             op("a", lambda: g.scalar.activation(ap(o), ap(i), f), [o], [i])
@@ -135,7 +131,7 @@ def rank_program(g, core, T, topo):
         act(o, i, AF.Identity, bias, scale)
 
     def fill(o, c):
-        act(o, v("ZERO", 0, len(range(o[2], o[3], o[4]))), AF.Identity, c, 0.0)
+        act(o, v("ZERO", 0, o[3] - o[2]), AF.Identity, c, 0.0)
 
     def mm(items, start=True, stop=True):
         def fn():
@@ -181,13 +177,13 @@ def rank_program(g, core, T, topo):
         op("p", lambda: g.tensor.wait_ge(T.sem["arr%d" % s], arrive), [], [], "w")
 
     dma(v("AWI"), T.aw[:])
-    dma(v("XB"), T.x0[:], "a")
     dma(v("GV"), T.gv[:])
+    dma(v("XB"), T.x0[:], "a")
     dma(v("EXI"), T.ex[:])
     iota(v("PC"), [[1, 1]], 0, 1)
     iota(v("JR"), [[1, 128]])
     iota(v("JG"), [[1, 8], [0, 16]])
-    ms(v("ZERO"), 0.0)
+    op("v", lambda: g.vector.memset(ap(v("ZERO")), 0.0), [v("ZERO")], [])
     dma(v("WS", 1024, 2048), v("ZERO"))
     dma(v("TAB"), v("ZERO", 0, 784))
     dma(v("TT", W, TW), v("ZERO", 0, TW - W))
@@ -199,7 +195,8 @@ def rank_program(g, core, T, topo):
     fill(v("KE"), -491520.0)
     fill(v("ZS", 256, 272), float(K0 + SENT))
     fill(v("OS", 256, 272), float(K0 + SENT))
-    fill(v("NBD"), 1024.0)
+    fill(v("NBD"), 0.0)
+    fill(v("NEG1"), -1.0)
     keep(v("ID"), v("ONES", 0, 128), [[-1, 128]], A.is_equal, 0, 1)
     ts(v("RCI"), v("PC"), 15, A.bitwise_and)
     ts(v("GCI"), v("PC"), 4, A.arith_shift_right)
@@ -224,8 +221,6 @@ def rank_program(g, core, T, topo):
     for q in range(1, 4):
         dma(v("MASK", 384 * q, 384 * q + 384), v("MASK", 0, 384))
     dma(v("CC", 0, W), T.co[:])
-    for q in range(1, 16):
-        dma(v("DIAG", 16 * q, 16 * q + 16), v("DIAG", 0, 16))
     for r in range(16):
         keep(v("BS", 128 * r, 128 * r + 128), v("B2K"), [[0, 8], [1, 16]], A.is_equal, -r, 0)
     iota(v("NDW"), [[-16, 16]], -W)
@@ -248,7 +243,7 @@ def rank_program(g, core, T, topo):
         for r in range(8):
             keep(v("WS", 128 * r, 128 * r + 128), v("WN"), [[0, 8], [1, 16]], A.is_equal, -r, 0)
         iota(v("CC", W, TW), [[0, TW - W]], -1)
-        keep(v("M01"), v("ONES", 0, 256), [[0, 16], [1, 16]], A.is_gt, 0, 0)
+        keep(v("M01"), v("ONES", 0, 192), [[0, 12], [1, 16]], A.is_gt, 0, 0)
         iota(v("DA"), [[16, 10]], W + 256)
 
     def consts_b():
@@ -263,14 +258,10 @@ def rank_program(g, core, T, topo):
     def consts_c():
         ts(v("NDW"), v("NDW"), v("RF"), A.subtract)
         cp(v("RR", 0, 6), v("EXI"))
-        cp(v("PF"), v("PC"))
-        ts(v("TC"), v("JR", 0, 32, 16), v("RF"), A.add)
         ts(v("TG"), v("RF"), 2.0, A.mult, v("PF"), A.subtract)
 
     def consts_e():
         ts(v("P1"), v("JR"), -112.0, A.add, v("TG"), A.is_equal)
-        ts(v("TRI2", 0, 32), v("JR", 0, 32), v("TC", 0, 1), A.is_lt)
-        ts(v("TRI2", 32, 64), v("JR", 0, 32), v("TC", 1, 2), A.is_lt)
         ts(v("DA"), v("DA"), v("RF"), A.add)
 
     def consts_f():
@@ -306,6 +297,7 @@ def rank_program(g, core, T, topo):
         last = s == S - 1
         CN = "CC" if s == 0 else "CF"
         CCw = v(CN, 0, TW)
+        XW = v("YX") if last else TTw
         scan(v("SC"), v("ONES", 0, 48), v("AW"), A.mult, A.add)
         mm([(v("PS4", 32, 33), v("TRI"), v("SC", 47, 48))])
         tt(v("NK2"), v("AW"), v("KC2"), A.mult)
@@ -313,15 +305,22 @@ def rank_program(g, core, T, topo):
         tt(v("PRE"), v("NK"), v("NK2"), A.subtract)
         ts(v("POSU"), v("PRE"), v("PS4", 32, 33), A.add)
         if s == 0:
+            cp(v("DIAG", 16, 32), v("DIAG", 0, 16))
+            cp(v("PF"), v("PC"))
+            ts(v("TC"), v("JR", 0, 32, 16), v("RF"), A.add)
+            ts(v("TRI2", 0, 32), v("JR", 0, 32), v("TC", 0, 1), A.is_lt)
+            ts(v("TRI2", 32, 64), v("JR", 0, 32), v("TC", 1, 2), A.is_lt)
             ts(v("GP"), ind(v("GV"), v("KCU")), -1.0, A.mult, float(SENT), A.add)
+        else:
+            cp(ind(TTw, v("AL", 0, 2 * s)), v("RT", 0, 32 * s))
         cp(ind(v("GA"), v("POSU", 0, SA)), v("GP", 0, 16 * SA))
         act(ind(v("GB"), v("POSU", SA, 48)), v("GP", 16 * SA, G), AF.Silu)
-        ts(v("REM2"), v("SC"), v("PS4", 32, 33), A.add, 257.0, A.is_ge)
+        ts(v("REM2"), v("SC"), v("PS4", 32, 33), A.add, 257.0, A.is_lt)
         if s == 0:
             init_table()
             consts_a()
         else:
-            mul(v("NBD"), v("TT", V, W), -1024.0)
+            act(v("NBD"), v("TT", V, W), AF.Relu, 1024.0, 1024.0)
         for lo, hi in ((0, NA // 16), (NA // 16, 256)):
             tt(v("GC", lo, hi), v("GA", lo, hi), v("GB", lo, hi), A.max)
         for lo, hi in ((0, NA // 16), (NA // 16, 256)):
@@ -338,154 +337,161 @@ def rank_program(g, core, T, topo):
             mm([(o, v("ID"), v("C15", lo // 16, hi // 16))] + [(o, v("WZ"), v("GG", lo + i, hi, 16)) for i in range(15)])
         for lo, hi in chunks:
             scan(v("MX", lo, hi), v("MASK", 0, hi - lo), v("GG", lo, hi), A.min, A.max)
+        mm([(v("PS1", 0, 256), v("WN"), v("GG", 15, 4096, 16))])
         mm([(v("PS4", 0, 16), v("WS", 128 * r, 128 * r + 128), v("GG", 16 * r + 15, 4096, 256)) for r in range(16)])
         tt(v("RL"), v("PS0", 0, 256), v("MX", 14, 4096, 16), A.max)
+        mul(v("ZS", 0, 256), v("PS0", 0, 256), -1.0, 15.0)
         act(v("AO"), v("PS4", 0, 16), AF.Abs, float(-K0), 1.0)
         mul(v("NAO"), v("AO"), -1.0)
-        mul(v("ZS", 0, 256), v("PS0", 0, 256), -1.0, 15.0)
         act(v("PN"), v("ZS", 0, 256), AF.Relu, float(-K0 - W + 1), 1.0)
         mm([(v("PS3", 0, 16), v("ID"), v("KE"))] +
            [(v("PS3", 0, 16), v("BS", 128 * r, 128 * r + 128), v("RL", r, 256, 16)) for r in range(16)])
-        mm([(v("PS1", 0, 256), v("WN"), v("GG", 15, 4096, 16))])
-        tt(v("REM"), v("REM2"), v("AW"), A.mult)
+        tt(v("REM"), v("REM2"), v("AW"), A.is_ge)
         if s == 0:
             consts_c()
         if last:
-            cp(ind(TTw, v("AL", 0, 8)), v("NEG1"))
+            cp(ind(XW, v("AL", 0, 8)), v("NEG1"))
+        tt(v("EQ"), v("PS1", 0, 256), v("ZS", 0, 256), A.is_equal)
         mul(v("OS", 0, 256), v("PS1", 0, 256), 1.0)
         tt(v("T1"), v("PS3", 0, 16), v("NAO"), A.min)
         tt(v("T2"), v("T1"), v("NDW"), A.max)
         ts(v("LB"), v("T2"), -1.0, A.mult)
-        ts(v("LW", 0, 256), ind(CCw, v("LB")), 1.0, A.add)
-        tt(v("EQ"), v("PS1", 0, 256), v("ZS", 0, 256), A.is_equal)
+        ts(v("LW", 0, 64), ind(CCw, v("LB", 0, 4)), 1.0, A.add)
+        ts(v("LW", 64, 256), ind(CCw, v("LB", 4, 16)), 1.0, A.add)
         mm([(v("PS2", 0, 256), v("IDB"), v("C392")), (v("PS2", 0, 256), v("W2B"), v("GG", 15, 4096, 16)),
             (v("PS2", 0, 256), v("BOB"), v("MX", 14, 4096, 16)), (v("PS2", 0, 256), v("IDB"), v("PN")),
             (v("PS2", 0, 256), v("IDB"), v("EQ"))])
-        cp(ind(TTw, v("LB")), v("MX", 14, 4096, 16))
-        ts(v("SB", 96 * s, 96 * s + 96), ind(TTw, v("RR", 0, 6)), -1.0, A.max, 1.0, A.add)
+        cp(ind(XW, v("LB")), v("MX", 14, 4096, 16))
+        tt(v("WA"), v("PS2", 0, 256), v("ZS", 0, 256), A.is_lt)
+        ts(v("SB", 96 * s, 96 * s + 96), ind(XW, v("RR", 0, 6)), -1.0, A.max, 1.0, A.add)
+        if last:
+            dma(T.yx[:, 0:V], v("YX", 0, V))
         if s == 0:
             iota(v("IDF"), [[16, 124]])
             iota(v("FF"), [[1, TW]])
         send(s)
         if s == 0:
+            for r in range(16):
+                keep(v("BF", 128 * r, 128 * r + 128), v("BO"), [[0, 8], [1, 16]], A.is_equal, -r, 0)
             consts_e()
         for q in range(4):
             act(v("G2", 1024 * q, 1024 * q + 1024), ind(v("TAB"), v("LW", 64 * q, 64 * q + 64)))
         if s == 0:
             consts_f()
-        relu(0, RA // 2, "a")
-        relu(RA // 2, RA, "a")
-        tt(v("WA"), v("PS2", 0, 256), v("ZS", 0, 256), A.is_lt)
+        relu(RA, RB, "a")
+        relu(RB, 4096, "a")
         scan(v("PX"), v("ONES", 0, 256), v("WA"), A.mult, A.add)
-        tt(v("OW"), v("PS1", 0, 256), v("WA"), A.mult)
+        mm([(v("PS0", 0, 256), v("WN"), v("GG", 15, 4096, 16)), (v("PS0", 0, 256), v("IDB"), v("WA"))])
         ts(v("LE", 0, 256), v("PX"), v("TC", 0, 1), A.is_le)
         ts(v("LE", 256, 512), v("PX"), v("TC", 1, 2), A.is_le)
         scan(v("EE", 0, 256), v("ONES", 0, 256), v("LE", 0, 256), A.mult, A.add)
         scan(v("EE", 256, 512), v("ONES", 0, 256), v("LE", 256, 512), A.mult, A.add)
         cp(v("KU"), v("EE", 255, 512, 256))
         sums("PS5", "G2", 0, 2048, True)
-        tt(v("UD", 0, 32), ind(v("ZS"), v("KU")), v("DIAG", 0, 32), A.mult)
-        tt(v("UD", 32, 64), ind(v("OS"), v("KU")), v("DIAG", 0, 32), A.mult)
+        relu(0, 1024)
+        sums("PS6", "H2", 0, 1024, True)
+        sums("PS5", "G2", 2048, 3072)
+        tt(v("UD", 0, 32), ind(v("ZS"), v("KU")), v("DIAG"), A.mult)
+        tt(v("UD", 32, 64), ind(v("OS"), v("KU")), v("DIAG"), A.mult)
         tt(v("UT", 0, 32), ind(v("ZS"), v("KU")), v("TRI2", 0, 32), A.mult)
         scan(v("US"), v("M01", 0, 64), v("UD"), A.mult, A.add)
         tt(v("UT", 32, 64), ind(v("ZS"), v("KU")), v("TRI2", 32, 64), A.mult)
         ts(v("UOU"), v("US", 15, 64, 16), float(-K0), A.add)
-        ts(v("EE", 0, 256), v("OW"), v("US", 15, 16), A.is_equal, 2048.0, A.mult)
+        ts(v("UB"), v("US", 15, 32, 16), BIG, A.add)
         cp(v("CG"), ind(CCw, v("UOU")))
+        ts(v("EE", 0, 256), v("PS0", 0, 256), v("UB", 0, 1), A.is_equal, 2048.0, A.mult)
         ts(v("EE", 256, 288), v("UT", 0, 32), v("US", 15, 16), A.is_equal, 2048.0, A.mult)
         tt(v("CL"), v("CG", 0, 32), v("CG", 32, 64), A.min)
         scan(v("ES", 0, 288), v("ONES"), v("EE", 0, 288), A.mult, A.max)
         ts(v("EE", 544, 576), v("UT", 32, 64), v("US", 31, 32), A.is_equal, 2048.0, A.mult)
-        tt(v("CT"), ind(TTw, v("UOU", 0, 2)), v("CL"), A.max)
+        tt(v("CT"), ind(XW, v("UOU", 0, 2)), v("CL"), A.max)
         mm([(v("PS3", 32, 34), v("ID"), v("KP"))] +
            [(v("PS3", 32, 34), v("BS", 128 * r, 128 * r + 128), v("CT", r, 32, 16)) for r in range(16)])
-        ts(v("EE", 288, 544), v("OW"), v("US", 31, 32), A.is_equal, 2048.0, A.mult)
+        relu(1024, RA)
+        sums("PS6", "H2", 1024, RA)
+        ts(v("EE", 288, 544), v("PS0", 0, 256), v("UB", 1, 2), A.is_equal, 2048.0, A.mult)
         ts(v("UOC"), v("US", 15, 64, 16), float(K0 + W), A.min, float(-K0), A.add)
         scan(v("ES", 288, 576), v("ONES"), v("EE", 288, 576), A.mult, A.max)
-        tt(v("MG"), v("CG", 0, 32), v("CG", 32, 64), A.max)
         tt(v("X1"), v("PS3", 32, 34), v("ES", 287, 576, 288), A.max)
-        ts(v("UR"), ind(v("ZS"), v("KU")), float(-K0), A.add)
-        for c in range(2):
-            ts(v("UW", c, c + 1), v("X1", c, c + 1), v("DA", 2 * s + c, 2 * s + c + 1), A.min, v("UOC", c, c + 1), A.max)
-        for c in range(2):
-            ts(v("AL", 2 * s + c, 2 * s + c + 1), v("X1", c, c + 1), v("DA", 2 * s + c, 2 * s + c + 1), A.min, v("UOC", 2 + c, 3 + c), A.max)
+        tt(v("MG"), v("CG", 0, 32), v("CG", 32, 64), A.max)
+        for name, base, src in (("UW", 0, 0), ("AL", 2 * s, 2)):
+            for k in range(2):
+                ts(v(name, base + k, base + k + 1), v("X1", k, k + 1), v("DA", 2 * s + k, 2 * s + k + 1), A.min,
+                   v("UOC", src + k, src + k + 1), A.max)
         cp(ind(CCw, v("UW")), v("MG"))
-        cp(v("RR", 6 + 2 * s, 8 + 2 * s), v("AL", 2 * s, 2 * s + 2))
-        ts(v("C1"), v(CN, V, W), 1.0, A.add)
-        cp(ind(FFw, v("AL", 2 * s, 2 * s + 2)), v("UR"))
-        tt(v("CU"), v("C1"), v("NBD"), A.min)
-        sums("PS5", "G2", 2048, 4096)
-        relu(RA, RB)
-        sums("PS6", "H2", 0, RA // 2, True)
+        ts(v("UR"), ind(v("ZS"), v("KU")), float(-K0), A.add)
+        sums("PS5", "G2", 3072, 4096)
         arrival(s)
         c = 96 * s
-        mm([(v("PS7", 32 * d, 32 * d + 32), v(("Q1", "Q2", "Q3")[d]), v("LD", c + 32 * d, c + 32 * d + 32)) for d in range(3)])
         for d in range(3):
+            o = v("PS7", 128 + 32 * d, 160 + 32 * d)
+            mm([(o, v("NID"), v("NBD", 32 * d, 32 * d + 32)), (o, v("ID"), v("NEG1", 0, 32)),
+                (o, v(("Q1", "Q2", "Q3")[d]), v("LD", c + 32 * d, c + 32 * d + 32))])
+        tt(v("CM"), v("PS7", 128, 224), v(CN, V, W), A.min)
+        sums("PS6", "H2", RA, RB)
+        mm([(v("PS7", 32 * d, 32 * d + 32), v(("Q1", "Q2", "Q3")[d]), v("LD", c + 32 * d, c + 32 * d + 32)) for d in range(3)])
+        for d in range(0 if last else 3):
             mm([(v("PS2", 32 * d, 32 * d + 32), v(("P1", "P2", "ID")[d]), v("LD", c + 32 * d, c + 32 * d + 32)),
                 (v("PS2", 32 * d, 32 * d + 32), v("ID"), v("CODE", V + 32 * d, V + 32 * d + 32))])
-        sums("PS6", "H2", RA, RB)
-        sums("PS6", "H2", RA // 2, RA)
-        tt(v("CM"), v("PS7", 0, 96), v("CU"), A.min)
-        cp(v("LW", 256, 352), v("CM"))
-        relu(RB, 4096)
+        cp(v("RR", 6 + 2 * s, 8 + 2 * s), v("AL", 2 * s, 2 * s + 2))
+        ts(v("LW", 256, 352), v("CM"), 1.0, A.add)
         sums("PS6", "H2", RB, 4096)
         cp(v("G2", 4096 + IA, 5632), ind(v("TAB"), v("LW", 256 + IA // 16, 352)))
         act(v("G2", 4096, 4096 + IB), ind(v("TAB"), v("LW", 256, 256 + IB // 16)))
         act(v("G2", 4096 + IB, 4096 + IA), ind(v("TAB"), v("LW", 256 + IB // 16, 256 + IA // 16)))
         parts = ((4096, 4096 + IB), (4096 + IA, 5632), (4096 + IB, 4096 + IA))
+        sums("PS5", "G2", *parts[0])
+        sums("PS5", "G2", *parts[1])
         for k, (lo, hi) in enumerate(parts):
             relu(lo, hi)
-            sums("PS5", "G2", lo, hi, False, k == 2)
             sums("PS6", "H2", lo, hi, False, k == 2)
-        tt(v("YY"), v("PS7", 0, 96), v("DI"), A.min)
+            if k == 0:
+                sums("PS5", "G2", *parts[2], False, True)
+        cp(ind(FFw, v("AL", 2 * s, 2 * s + 2)), v("UR"))
         nr, na = 8 + 2 * s, 2 * s + 2
         if not last:
-            tt(v("RG", 0, 16 * nr), ind(FFw, v("RR", 0, nr)), v("DIAG", 0, 16 * nr), A.mult)
+            act(v("RG", 0, 16 * nr), ind(FFw, v("RR", 0, nr)))
+            mm([(v("PS4", 64, 64 + nr), v("BF", 128 * r, 128 * r + 128), v("RG", r, 16 * nr, 16)) for r in range(16)])
+            tt(v("YY"), v("PS7", 0, 96), v("DI"), A.min)
             tt(v("TT", V, W), v("PS2", 0, 96), v("YY"), A.add)
             fill(v("GA", 0, 256), 0.0)
             fill(v("GB", 0, 256), 0.0)
+            if s == S - 2:
+                act(v("YR"), TTw, AF.Relu, 1.0, 1.0)
         else:
             act(v("RG", 0, 160), ind(FFw, v("RR", 6, 16)))
-            tt(v("TT", V, W), v("PS2", 0, 96), v("YY"), A.add)
+            mul(v("YX", V, W), v("PS7", 0, 96), 1.0 / 8192, -1.0)
+            dma(T.yx[:, V:W], v("YX", V, W))
             for b in range(3):
                 mm([(v("PS%d" % b, p=(0, 8)), v("B8"), v("CF", 512 * b, 512 * b + 512))])
-            ts(v("YX"), v("TT", 0, W), -1.0, A.max)
-            dma(T.yx[:], v("YX"))
         cp(v("D0", 0, 128, 2), v("PS6", 0, 64))
         tt(v("D0", 1, 128, 2), v("D0", 0, 128, 2), v("PS5", 0, 64), A.subtract)
-        if not last:
-            scan(v("RS", 0, 16 * nr), v("M01", 0, 16 * nr), v("RG", 0, 16 * nr), A.mult, A.add)
-        else:
+        if last:
             cp(ind(FFw, v("AL")), v("RG", 0, 160))
             dma(T.yf[:], v("FF", 0, W, p=(0, 128, 16)))
             for b in range(3):
                 mul(v("YC", 512 * b, 512 * b + 512, p=(0, 8)), v("PS%d" % b, p=(0, 8)), 1.0)
             dma(T.yc[:], v("YC", p=(0, 8)), "a")
         tt(v("D1"), v("D0", 0, 64), v("D0", 64, 128), A.add)
-        if not last:
-            cp(v("RR", 0, nr), v("RS", 15, 16 * nr, 16))
-            act(v("RT", 0, 16 * na), ind(TTw, v("RR", 6, 6 + na)))
         if s == 0:
             ts(v("IDU"), v("IDF"), v("RF"), A.add, float(TW - 1), A.min)
             act(v("CF"), ind(CCw, v("IDU")))
-        if s == S - 2:
-            fill(v("NEG1"), -1.0)
         for w in range(2):
             tt(v("D2", 16 * w, 16 * w + 16), v("D1", w, 32, 2), v("D1", 32 + w, 64, 2), A.add)
         for k in range(6):
             ts(v("D3", 32 * k, 32 * k + 32), v("D2"), k, A.logical_shift_right, 0o01010101, A.bitwise_and)
         cp(v("D4"), v("D3"))
-        scan(v("D5"), v("M01", 0, 192), v("D4"), A.mult, A.add)
+        scan(v("D5"), v("M01"), v("D4"), A.mult, A.add)
         if not last:
-            cp(ind(TTw, v("AL", 0, na)), v("RT", 0, 16 * na))
+            ts(v("RR", 0, nr), v("PS4", 64, 64 + nr), 1.0 / 16, A.mult)
+            act(v("RT", 0, 16 * na), ind(TTw, v("RR", 6, 6 + na)))
+            if s == S - 2:
+                mul(v("YX"), v("YR"), 1.0, -1.0)
         cp(v("D6"), v("D5", 15, 192, 16))
         for f in range(4):
             ts(v("D7", 12 * f, 12 * f + 12), v("D6"), 63 << (6 * f), A.bitwise_and)
-        tt(v("D8"), v("D7"), v("REM"), A.max)
-        if not last:
-            ts(v("AW"), v("D8"), 1.0, A.min)
-        else:
-            ts(v("AWF"), v("D8"), 1.0, A.min)
+        tt(v("AWF" if last else "AW"), v("D7"), v("REM"), A.is_ge)
+        if last:
             dma(T.yw[:], v("AWF"))
 
     Q = {"v": g.vector, "a": g.scalar, "p": g.tensor, "g": g, "s": g.sync}
@@ -503,8 +509,6 @@ def rank_program(g, core, T, topo):
             for (l2, h2, w2, q2, sem, val, kn) in hist.get(name, []):
                 if ps and q2 != q:
                     hit = True
-                elif name == "TAB" and isw and q2 == q and h2 - l2 == 48:
-                    hit = False
                 else:
                     hit = l2 < hi and lo < h2 and (isw or w2) and not (q == "p" and q2 == "p")
                 if hit and known[q].get(sem, 0) < val and need.get(sem, (0,))[0] < val:

@@ -1,39 +1,49 @@
+import math
 from concourse.bass import DstId, RemoteDMATransfer
 from concourse.mybir import AluOpType as A, ActivationFunctionType as AF
 
 S, V, W, G = 5, 1440, 1536, 768
 TW = 1968
 SENT = 1952
-K0 = 50241
+C2 = 480
+K0 = 257 + 256 * C2
 BIG = float(2 ** 20)
+MID, DX = 1184.5, 2.0 ** -14
+KX = 0.25 - (768 * DX) ** 2 / 64
+UNY, UNC = -1.0 / (DX * KX), SENT - MID + 0.25 + 0.5 / (DX * KX)
+OA, OW, LOW = 136, 170, 40
+Z0, Z1 = 88.0, 176.0 * OA - 64.0 * OW
+LN2 = math.log(2.0)
 SA = 22
-NA, NC, NB, NV = 1024, 1024, 1536, 1536
-RA, RB = 2048, 3072
-IA, IB = 832, 512
+NA, NC, NV = 1024, 1024, 1280
+NL = NA + NC + NV
+NM, NI = 1536, 12
 
 f32, bf, i32, u16 = "float32", "bfloat16", "int32", "uint16"
 BUF = {
-    "TT": (TW, bf), "CC": (TW, i32), "CF": (1984, f32), "FF": (TW, f32), "GA": (2304, f32), "GB": (2304, f32), "GC": (256, f32),
-    "XB": (V, bf), "ZB": (V, bf), "CODE": (W, bf), "C392": (256, bf), "C15": (256, bf), "HB": (24, f32), "IDF": (124, f32), "IDU": (124, u16),
-    "GV": (G, i32), "GP": (G, f32), "AWI": (48, i32), "EXI": (6, i32),
-    "AW": (48, bf), "AWF": (48, f32), "SC": (48, bf), "PRE": (48, f32), "NK": (48, f32), "NK2": (48, f32), "POSU": (48, u16),
-    "REM": (48, f32), "REM2": (48, f32), "KC1": (48, f32), "KC2": (48, f32), "KCU": (48, u16), "ONES": (288, bf), "ZERO": (1024, bf),
-    "OFF": (256, u16), "GG": (4096, bf), "MX": (4096, bf), "MASK": (NV, bf), "M01": (192, f32), "DIAG": (32, f32),
-    "RL": (256, bf), "ZS": (272, f32), "OS": (272, f32), "PN": (256, bf), "EQ": (256, bf), "AO": (16, f32), "NAO": (16, f32),
-    "NDW": (16, f32), "T1": (16, f32), "T2": (16, f32), "LB": (16, u16), "LW": (352, u16), "G2": (5632, bf), "H2": (5632, bf),
-    "TAB": (784, bf), "PW": (48, bf), "PWS": (24, f32), "TWOS": (24, f32),
-    "WA": (256, bf), "PX": (256, bf), "LE": (512, bf), "KU": (2, u16), "TC": (2, f32),
-    "UD": (64, f32), "US": (64, f32), "UOU": (4, u16), "UOC": (4, f32), "UR": (32, f32), "UT": (64, f32), "TRI2": (64, f32), "UB": (2, f32),
-    "CG": (64, f32), "CL": (32, f32), "MG": (32, f32), "CT": (32, bf), "EE": (576, bf), "ES": (576, bf),
+    "TT": (TW, bf), "CC": (TW, i32), "CF": (1984, f32), "FF": (TW, f32), "FC": (TW, bf), "GA": (2304, f32), "GB": (2304, f32), "GC": (256, f32),
+    "XB": (V, bf), "ZB": (V, bf), "CODE": (W, bf), "CC2": (256, bf), "C15": (256, bf), "HB": (6, f32), "IDF": (124, f32), "IDU": (124, u16),
+    "GV": (G, i32), "GP": (G, f32), "AWI": (48, i32), "EXI": (6, i32), "FILL": (256, f32),
+    "AW": (48, bf), "AWF": (48, f32), "NK": (48, bf), "PRE": (48, f32), "NK2": (48, f32), "POSU": (48, u16),
+    "REM": (48, f32), "REM2": (48, f32), "KC2": (48, f32), "KCU": (48, u16), "ONES": (256, bf), "ZO": (256, bf),
+    "OFF": (256, u16), "GG": (4096, bf), "MX": (4096, bf), "MASK": (NM, bf), "M01": (192, f32), "DIAG": (32, f32),
+    "RL": (256, bf), "RC": (256, bf), "ZS": (272, f32), "OS": (272, f32), "AD": (256, bf), "EQ": (256, bf),
+    "LO": (16, u16), "DO": (32, f32), "LS": (32, f32), "LB": (16, u16), "KD": (64, bf),
+    "CW": (272, f32), "AA": (384, bf), "WB": (384, bf), "WW": (768, bf), "OH": (6144, bf), "WO": (256, f32), "WL": (2, u16),
+    "WA": (256, bf), "PX": (256, bf), "LE": (512, bf), "KA": (2, f32), "KU": (2, u16), "TC": (2, f32), "TC5": (2, f32),
+    "UD": (64, f32), "US": (64, f32), "UL": (2, u16), "FI": (2, u16), "UOC": (4, f32), "UR": (32, bf), "UT": (64, f32), "TRI2": (64, f32),
+    "MG": (32, f32), "CT": (32, bf), "ET": (64, bf), "EE": (512, bf), "ES": (512, bf),
     "X1": (2, f32), "DA": (10, f32), "UW": (2, u16), "AL": (10, u16), "RR": (16, u16),
-    "RG": (256, f32), "RT": (160, bf), "NEG1": (128, bf),
-    "SB": (96 * S, bf), "LD": (96 * S, bf), "NBD": (96, bf), "CM": (96, f32), "DI": (96, f32), "YY": (96, f32),
-    "D0": (128, f32), "D1": (64, f32), "D2": (32, i32), "D3": (192, i32), "D4": (192, f32), "D5": (192, f32), "D6": (12, i32), "D7": (48, i32),
-    "PC": (1, i32), "GCI": (1, i32), "RCI": (1, i32), "PF": (1, f32), "GF": (1, f32), "RF": (1, f32), "R48": (1, f32), "WC": (8, f32),
-    "TG": (1, f32), "JR": (128, f32), "JG": (128, f32), "B8": (8, f32),
-    "ID": (128, bf), "NID": (128, bf), "BO": (128, bf), "B2K": (128, bf), "TRI": (128, bf), "WZ": (128, bf), "WN": (128, bf), "BOB": (128, bf),
-    "W2B": (128, bf), "IDB": (128, bf), "P1": (128, bf), "P2": (128, bf), "Q1": (128, bf), "Q2": (128, bf), "Q3": (128, bf),
-    "BS": (2048, bf), "WS": (2048, bf), "BF": (2048, f32), "KE": (16, bf), "KP": (2, bf), "YC": (W, f32), "YX": (TW, bf), "YR": (TW, bf),
+    "RG": (256, bf), "RO": (160, f32), "RT": (160, bf), "NEG1": (256, bf),
+    "SB": (96 * S, bf), "LD": (96 * S, bf), "NBD": (128, bf), "CI": (128, f32), "FL": (144, bf),
+    "D2": (32, i32), "D3": (192, i32), "D5": (192, i32), "D7": (48, i32), "ZC": (512, bf), "ZI": (256, bf),
+    "PC": (1, i32), "GCI": (1, i32), "RCI": (1, i32), "PF": (1, f32), "GF": (1, f32), "RF": (1, f32), "R48": (1, f32), "WC": (10, f32),
+    "TG": (1, f32), "G15": (1, f32), "PMC": (1, f32), "JR": (256, bf), "JG": (128, bf), "JG2": (256, bf), "B8": (8, f32),
+    "ID": (128, bf), "NID": (128, bf), "BO": (128, bf), "TRI": (128, bf), "WZ": (128, bf), "WN": (128, bf), "BOB": (128, bf),
+    "W2B": (128, bf), "IDB": (128, bf), "P1": (128, bf), "P2": (128, bf),
+    "PM": (128, f32), "IZ": (128 * 4, bf), "GZ": (256, bf), "NGZ": (256, bf), "G2Z": (256, bf),
+    "BS": (144, bf), "BN": (144, bf), "B2": (144, bf), "B15": (144, f32), "WS": (144, bf), "KP": (2, bf),
+    "YC": (W, f32), "YX": (TW, bf), "YR": (TW, bf),
 }
 SCRATCH, PLACE, _fill = {}, {}, {}
 for _k, (_n, _d) in BUF.items():
@@ -92,7 +102,7 @@ def rank_program(g, core, T, topo):
         return T[name][ps, lo:hi:step] if step != 1 else T[name][ps, lo:hi]
 
     def spans(xs):
-        return [(x[1], x[2], x[3]) for x in xs if isinstance(x, tuple) and x[0] == "v"]
+        return [(x[1], x[2], x[3], x[4]) for x in xs if isinstance(x, tuple) and x[0] == "v"]
 
     def op(q, fn, outs, ins, kind="c"):
         rd, wr = [], []
@@ -121,9 +131,14 @@ def rank_program(g, core, T, topo):
     def scan(o, d0, d1, f0, f1, init=0.0):
         op("v", lambda: g.vector.tensor_tensor_scan(ap(o), ap(d0), ap(d1), init, f0, f1), [o], [d0, d1])
 
-    def act(o, i, f=AF.Identity, bias=0.0, scale=1.0):
+    def mset(o, c):
+        op("v", lambda: g.vector.memset(ap(o), c), [o], [])
+
+    def act(o, i, f=AF.Identity, bias=0.0, scale=1.0, acc=None):
         if o[0] == "i":
             op("a", lambda: g.scalar.activation(ap(o), ap(i), f), [o], [i])
+        elif acc is not None:
+            op("a", lambda: g.scalar.activation(ap(o), ap(i), f, bias=ap(bias), scale=ap(scale), accum_out=ap(acc)), [o, acc], [i, bias, scale])
         else:
             op("a", lambda: g.scalar.activation(ap(o), ap(i), f, bias=ap(bias), scale=ap(scale)), [o], [i, bias, scale])
 
@@ -131,14 +146,14 @@ def rank_program(g, core, T, topo):
         act(o, i, AF.Identity, bias, scale)
 
     def fill(o, c):
-        act(o, v("ZERO", 0, o[3] - o[2]), AF.Identity, c, 0.0)
+        act(o, v("ZO", 0, len(range(o[2], o[3], o[4])), p=o[5]), AF.Identity, c, 0.0)
 
-    def mm(items, start=True, stop=True):
+    def mm(items, whole=False, start=True, stop=True):
         def fn():
             last = None
             for k, (o, l, r) in enumerate(items):
-                first = start and all(o != z[0] for z in items[:k])
-                final = stop and all(o != z[0] for z in items[k + 1:])
+                first = start and (k == 0 if whole else all(o != z[0] for z in items[:k]))
+                final = stop and (k == len(items) - 1 if whole else all(o != z[0] for z in items[k + 1:]))
                 last = g.tensor.matmul(ap(o), ap(l), ap(r), first, final)
             return last
         op("p", fn, [x[0] for x in items], [y for x in items for y in x[1:]])
@@ -155,6 +170,9 @@ def rank_program(g, core, T, topo):
     def dma(o, i, q="s"):
         e = g.sync if q == "s" else g.scalar
         op(q, lambda: e.dma_start(ap(o), ap(i)), [o], [i], "d")
+
+    def wrap(o, mat, src, lo, hi, step=1):
+        return [(o, v(mat, 15 - r, 143 - r), v(src, lo + step * r, hi, 16 * step)) for r in range(16)]
 
     peers = [T.cores[rank ^ d] for d in range(1, N)]
     masks = send_masks(core, peers, topo)
@@ -180,98 +198,114 @@ def rank_program(g, core, T, topo):
     dma(v("GV"), T.gv[:])
     dma(v("XB"), T.x0[:], "a")
     dma(v("EXI"), T.ex[:])
+    dma(v("CC", 0, W), T.co[:])
     iota(v("PC"), [[1, 1]], 0, 1)
-    iota(v("JR"), [[1, 128]])
+    iota(v("JR"), [[1, 256]])
     iota(v("JG"), [[1, 8], [0, 16]])
-    op("v", lambda: g.vector.memset(ap(v("ZERO")), 0.0), [v("ZERO")], [])
-    dma(v("WS", 1024, 2048), v("ZERO"))
-    dma(v("TAB"), v("ZERO", 0, 784))
-    dma(v("TT", W, TW), v("ZERO", 0, TW - W))
-    fill(v("ONES"), 1.0)
-    fill(v("TWOS"), 2.0)
-    fill(v("GA", 0, 256), 0.0)
-    fill(v("GB", 0, 256), 0.0)
-    fill(v("KP"), 32768.0)
-    fill(v("KE"), -491520.0)
-    fill(v("ZS", 256, 272), float(K0 + SENT))
-    fill(v("OS", 256, 272), float(K0 + SENT))
-    fill(v("NBD"), 0.0)
-    fill(v("NEG1"), -1.0)
-    keep(v("ID"), v("ONES", 0, 128), [[-1, 128]], A.is_equal, 0, 1)
+    mset(v("ZO"), 0.0)
+    act(v("ONES"), v("ZO"), AF.Sigmoid, 40.0, 0.0)
+    mset(v("FILL"), 0.5 - MID * DX * KX)
+    dma(v("GA", 0, 256), v("FILL"))
+    dma(v("GB", 0, 256), v("FILL"))
+    mset(v("TT", W, TW), 0.0)
     ts(v("RCI"), v("PC"), 15, A.bitwise_and)
     ts(v("GCI"), v("PC"), 4, A.arith_shift_right)
+    cp(v("PF"), v("PC"))
     cp(v("RF"), v("RCI"))
     cp(v("GF"), v("GCI"))
+    ts(v("R48"), v("RF"), 48.0, A.mult)
     ts(v("DIAG", 0, 16), v("JR", 0, 16), v("RF"), A.is_equal)
+    ts(v("KCU"), v("JR", 0, 48), v("R48"), A.add)
+    ts(v("KC2"), v("JR", 0, 48), v("R48"), A.add, float(G + 2), A.add)
     ts(v("BO"), v("JG"), v("GF"), A.is_equal)
     keep(v("TRI"), v("BO"), [[1, 128]], A.is_gt, 0, -1)
-    ts(v("R48"), v("RF"), 48.0, A.mult)
-    ts(v("WC", 4, 5), v("DIAG", 0, 1), -1.0, A.mult)
-    ts(v("WC", 5, 6), v("DIAG", 2, 3), -391.0, A.mult, -1.0, A.add)
-    ts(v("WC", 6, 7), v("DIAG", 1, 2), -1.0, A.mult)
-    ts(v("KCU"), v("JR", 0, 48), v("R48"), A.add)
-    ts(v("HB"), v("JR", 0, 24), v("WC", 6, 7), A.mult, v("WC", 5, 6), A.add)
-    ts(v("KC1"), v("JR", 0, 48), v("R48"), A.add, float(G), A.add)
-    ts(v("KC2"), v("JR", 0, 48), v("R48"), A.add, float(G + 1), A.add)
-    ts(v("B2K"), v("BO"), 2048.0, A.mult)
-    ts(v("B8"), v("JR", 0, 8), v("GF"), A.is_equal)
-    scan(v("PWS"), v("TWOS"), v("ZERO", 0, 24), A.mult, A.add, 0.5)
-    cp(v("AW"), v("AWI"))
+    ts(v("ID"), v("JR", 0, 128), v("PF"), A.is_equal)
     iota(v("MASK", 0, 384), [[0, 24], [16, 16]])
     for q in range(1, 4):
         dma(v("MASK", 384 * q, 384 * q + 384), v("MASK", 0, 384))
-    dma(v("CC", 0, W), T.co[:])
-    for r in range(16):
-        keep(v("BS", 128 * r, 128 * r + 128), v("B2K"), [[0, 8], [1, 16]], A.is_equal, -r, 0)
-    iota(v("NDW"), [[-16, 16]], -W)
-    for h in range(24):
-        mul(v("CODE", 64 * h, 64 * h + 64), v("JR", 0, 64), v("WC", 4, 5), v("HB", h, h + 1))
+    ts(v("WC", 4, 5), v("DIAG", 0, 1), -1.0, A.mult)
+    ts(v("WC", 5, 6), v("DIAG", 2, 3), 1.0 - C2, A.mult, -1.0, A.add)
+    ts(v("WC", 6, 7), v("DIAG", 1, 2), -1.0, A.mult)
+    ts(v("G15"), v("GF"), 16.0, A.mult, 15.0, A.add)
+    ts(v("HB"), v("JR", 0, 6), v("WC", 6, 7), A.mult, v("WC", 5, 6), A.add)
+    cp(v("AW"), v("AWI"))
+    for h in range(6):
+        ts(v("CODE", 256 * h, 256 * h + 256), v("JR"), v("WC", 4, 5), A.mult, v("HB", h, h + 1), A.add)
+    dma(v("FC", 0, W), v("CODE"))
+    dma(v("FC", W, TW), v("TT", W, TW))
+    fill(v("KP"), 32768.0)
+    fill(v("ZS", 256, 272), float(K0 + SENT))
+    fill(v("OS", 256, 272), float(K0 + SENT))
+    fill(v("CW", 256, 272), -1.0)
+    fill(v("C15"), 15.0)
+    mul(v("WC", 0, 1), v("DIAG", 1, 2), 256.0, v("DIAG", 0, 1))
+    mul(v("WC", 3, 4), v("DIAG", 2, 3), BIG)
+    mul(v("WC", 1, 2), v("DIAG", 2, 3), 256.0, v("WC", 0, 1))
+    mul(v("WC", 7, 8), v("DIAG", 2, 3), 2.0 ** 24)
+    mul(v("WC", 8, 9), v("DIAG", 2, 3), -2.0)
+    mul(v("WC", 2, 3), v("WC", 1, 2), -1.0)
     mul(v("NID"), v("ID"), -8192.0)
+    mul(v("WZ"), v("BO"), v("WC", 1, 2))
+    mul(v("WN"), v("BO"), v("WC", 2, 3))
     act(v("ZB"), v("XB"), AF.Relu, 0.0, -1.0)
-    mul(v("PW", 0, 48, 2), v("PWS"), 1.0)
-    mul(v("PW", 1, 48, 2), v("PWS"), -1.0)
-    for q in range(16):
-        dma(v("TAB", 1 + 48 * q, 49 + 48 * q, p=(q, 128, 16)), v("PW", p=(0, 8)))
+    iota(v("JG2"), [[0, 16], [1, 8], [0, 2]])
+    iota(v("CC", W, TW), [[0, TW - W]], -1)
+    keep(v("M01"), v("ONES", 0, 192), [[0, 12], [1, 16]], A.is_gt, 0, 0)
+    iota(v("DA"), [[16, 10]], W + 256, 0)
+    iota(v("IDF"), [[16, 124]])
+    iota(v("FF"), [[1, TW]])
 
     def consts_a():
-        mul(v("WC", 0, 1), v("DIAG", 1, 2), 64.0, v("DIAG", 0, 1))
-        mul(v("WC", 1, 2), v("DIAG", 2, 3), 128.0, v("WC", 0, 1))
-        mul(v("WC", 2, 3), v("WC", 1, 2), -1.0)
-        mul(v("WZ"), v("BO"), v("WC", 1, 2))
-        fill(v("C15"), 15.0)
-        mul(v("WN"), v("BO"), v("WC", 2, 3))
-        for r in range(8):
-            keep(v("WS", 128 * r, 128 * r + 128), v("WN"), [[0, 8], [1, 16]], A.is_equal, -r, 0)
-        iota(v("CC", W, TW), [[0, TW - W]], -1)
-        keep(v("M01"), v("ONES", 0, 192), [[0, 12], [1, 16]], A.is_gt, 0, 0)
-        iota(v("DA"), [[16, 10]], W + 256)
+        cp(v("DIAG", 16, 32), v("DIAG", 0, 16))
+        ts(v("TC"), v("JR", 0, 32, 16), v("RF"), A.add)
+        ts(v("B15"), v("JR", 0, 144), v("G15"), A.is_equal, v("DIAG", 15, 16), A.mult)
+        ts(v("BS"), v("JR", 0, 144), v("G15"), A.is_equal, 2048.0, A.mult)
+        ts(v("BN"), v("JR", 0, 144), v("G15"), A.is_equal, -2048.0, A.mult)
+        ts(v("PMC"), v("RF"), 8.0, A.mult, v("GF"), A.add)
+        ts(v("TC5"), v("TC"), 0.5, A.add)
+        ts(v("TRI2", 0, 32), v("JR", 0, 32), v("TC", 0, 1), A.is_gt)
+        ts(v("TRI2", 32, 64), v("JR", 0, 32), v("TC", 1, 2), A.is_gt)
+        ts(v("B8"), v("JR", 0, 8), v("GF"), A.is_equal)
+        ts(v("PM"), v("JR", 0, 128), v("PMC"), A.is_equal)
+        mset(v("DO", 0, 32, 2), 1e29)
+        mset(v("KD", 0, 32, 2), C2 * 2.0 ** 24)
+        ts(v("KD", 1, 32, 2), v("JR", 0, 256, 16), float(W), A.add)
+        mset(v("KD", 32, 64, 2), 240 * 2048.0)
+        ts(v("KD", 33, 64, 2), v("JR", 0, 16), 0.0, A.mult, v("RF"), A.add)
+        ts(v("WL"), v("JR", 0, 2), v("PMC"), A.add, v("PMC"), A.add)
+        ts(v("TG"), v("RF"), 2.0, A.mult, v("PF"), A.subtract)
 
     def consts_b():
-        for r in range(8, 16):
-            mul(v("WS", 129 * r, 128 * r + 128, 16), v("B8"), v("WC", 2, 3))
-        mul(v("WC", 3, 4), v("DIAG", 2, 3), BIG)
+        ts(v("B2"), v("JR", 0, 144), v("G15"), A.is_equal, v("WC", 7, 8), A.mult)
+        ts(v("WS"), v("JR", 0, 144), v("G15"), A.is_equal, v("WC", 2, 3), A.mult)
+        ts(v("GZ"), v("JG2"), v("GF"), A.is_equal, 64.0, A.mult)
+        ts(v("G2Z"), v("JG2"), v("GF"), A.is_equal, v("WC", 8, 9), A.mult)
+        ts(v("P1"), v("JR", 0, 128), -112.0, A.add, v("TG"), A.is_equal)
+        cp(v("RR", 0, 6), v("EXI"))
+        ts(v("DA"), v("DA"), v("RF"), A.add)
+
+    def consts_c():
+        fill(v("CC2"), float(C2))
         mul(v("BOB"), v("BO"), BIG)
         mul(v("IDB"), v("ID"), BIG)
         mul(v("W2B"), v("BO"), v("WC", 3, 4))
-        fill(v("C392"), 392.0)
 
-    def consts_c():
-        ts(v("NDW"), v("NDW"), v("RF"), A.subtract)
-        cp(v("RR", 0, 6), v("EXI"))
-        ts(v("TG"), v("RF"), 2.0, A.mult, v("PF"), A.subtract)
+    def consts_d():
+        fill(v("NEG1"), -1.0)
+        fill(v("ZC", 0, 512, 2), Z0 - 2 * C2)
+        fill(v("ZC", 1, 512, 2), Z1 - 2 * C2)
+        for k, c in enumerate((-64.0, 80.0, 64.0, -176.0)):
+            mul(v("IZ", 128 * k, 128 * k + 128), v("ID"), c)
 
     def consts_e():
-        ts(v("P1"), v("JR"), -112.0, A.add, v("TG"), A.is_equal)
-        ts(v("DA"), v("DA"), v("RF"), A.add)
-
-    def consts_f():
-        mul(v("Q1"), v("P1"), 8192.0)
-        mul(v("Q2", 16, 128), v("P1", 0, 112), 8192.0)
-        mul(v("Q2", 0, 16), v("P1", 112, 128), 8192.0)
-        mul(v("Q3"), v("ID"), 8192.0)
+        for w, z in enumerate((Z0, Z1)):
+            fill(v("ZI", w, 256, 2, p=(0, 96)), z)
+            fill(v("ZI", w, 256, 2, p=(96, 128)), z - 1024)
+        mul(v("NGZ"), v("GZ"), -1.0)
+        fill(v("NBD"), 0.0)
+        fill(v("FL"), 1.0)
         mul(v("P2", 16, 128), v("P1", 0, 112), 1.0)
         mul(v("P2", 0, 16), v("P1", 112, 128), 1.0)
-        mul(v("DI"), v("CODE", V, W), -1.0, -1.0)
 
     def init_table():
         for b in range(3):
@@ -280,219 +314,246 @@ def rank_program(g, core, T, topo):
         for b in range(3):
             lo, hi = 480 * b, 480 * b + 480
             tt(v("TT", lo, hi), v("PS%d" % b, 0, 480), v("CODE", lo, hi), A.max)
-        mul(v("TT", V, W), v("CODE", V, W), 1.0)
+        cp(v("TT", V, W), v("CODE", V, W))
 
-    TTw, FFw = v("TT"), v("FF")
+    TTw, FFw, FCw = v("TT"), v("FF"), v("FC")
 
-    def sums(bank, src, lo, hi, start=False, stop=False):
-        mm([(v(bank, 0, 64), v("ID"), v(src, c, c + 64)) for c in range(lo, hi, 64)], start, stop)
+    def turn(src):
+        mm([(v("PS5", 128 * t, 128 * t + 128), x, v("PM")) for t, x in src])
 
-    def relu(lo, hi, q="v"):
-        if q == "v":
-            ts(v("H2", lo, hi), v("G2", lo, hi), 0.0, A.max)
-        else:
-            act(v("H2", lo, hi), v("G2", lo, hi), AF.Relu)
+    def split(tiles):
+        lo, hi = 128 * tiles[0], 128 * tiles[-1] + 128
+        mul(v("AA", lo, hi), v("PS5", lo, hi), 1.0 / 48, OA - 23.5 / 48)
+        mul(v("WB", lo, hi), v("PS5", lo, hi), 1.0 / 24, OW - 11.5 / 24)
 
+    def z_open(bank, const, src):
+        t0 = src[0][0]
+        return [(v(bank, 0, const[3]), v("ID"), const)] + \
+               [(v(bank, 256 * (t - t0) + w, 256 * (t - t0) + 256, 2), x, v("PM")) for w in range(2) for t, x in src]
+
+    def z_split(bank, tiles):
+        lo, hi = 128 * tiles[0], 128 * tiles[-1] + 128
+        return [(v(bank, w, 2 * (hi - lo), 2), v("IZ", 256 * w + 128 * k, 256 * w + 128 * k + 128), v(("WB", "AA")[k], lo, hi))
+                for w in range(2) for k in range(2)]
+
+    def powers(bank, tiles):
+        act(v("WW", 256 * tiles[0], 256 * tiles[-1] + 256), v(bank, 0, 256 * len(tiles)), AF.Sigmoid, -LN2 * (LOW + Z0), LN2)
+
+    def onehot(tiles, lo, hi):
+        for a in range(lo, hi):
+            ts(v("OH", 2048 * tiles[0] + a, 2048 * tiles[-1] + 2048, 16), v("AA", 128 * tiles[0], 128 * tiles[-1] + 128),
+               float(OA + a), A.is_equal)
+
+    def words(tiles, start, stop):
+        head = [(v("PS7", 0, 256), v("ID"), v("ZO"))] if start else []
+        mm(head + [(v("PS7", 16 * i, 16 * i + 16), v("OH", 2048 * t + 128 * i, 2048 * t + 128 * i + 128),
+                    v("WW", 256 * t + 16 * i, 256 * t + 16 * i + 16)) for t in tiles for i in range(16)], True, start, stop)
+
+    OWN, IMP, PI, PU = (0, 1), (2,), (0, 96), (96, 128)
     for s in range(S):
         last = s == S - 1
         CN = "CC" if s == 0 else "CF"
         CCw = v(CN, 0, TW)
         XW = v("YX") if last else TTw
-        scan(v("SC"), v("ONES", 0, 48), v("AW"), A.mult, A.add)
-        mm([(v("PS4", 32, 33), v("TRI"), v("SC", 47, 48))])
-        tt(v("NK2"), v("AW"), v("KC2"), A.mult)
-        tt(v("NK"), v("SC"), v("KC1"), A.add)
-        tt(v("PRE"), v("NK"), v("NK2"), A.subtract)
-        ts(v("POSU"), v("PRE"), v("PS4", 32, 33), A.add)
         if s == 0:
-            cp(v("DIAG", 16, 32), v("DIAG", 0, 16))
-            cp(v("PF"), v("PC"))
-            ts(v("TC"), v("JR", 0, 32, 16), v("RF"), A.add)
-            ts(v("TRI2", 0, 32), v("JR", 0, 32), v("TC", 0, 1), A.is_lt)
-            ts(v("TRI2", 32, 64), v("JR", 0, 32), v("TC", 1, 2), A.is_lt)
-            ts(v("GP"), ind(v("GV"), v("KCU")), -1.0, A.mult, float(SENT), A.add)
-        else:
-            cp(ind(TTw, v("AL", 0, 2 * s)), v("RT", 0, 32 * s))
+            scan(v("NK"), v("ONES", 0, 48), v("AW"), A.add, A.add)
+            mm([(v("PS4", 32, 33), v("TRI"), v("NK", 47, 48))])
+            tt(v("NK2"), v("AW"), v("KC2"), A.mult)
+        tt(v("PRE"), v("NK"), v("NK2"), A.subtract)
+        ts(v("POSU"), v("PRE"), v("PS4", 32, 33), A.add, float(G), A.add)
+        if s == 0:
+            consts_a()
+            ts(v("GP", 0, 16 * SA), ind(v("GV"), v("KCU", 0, SA)), -DX * KX, A.mult, 0.5 + (SENT - MID) * DX * KX, A.add)
+            act(v("GP", 16 * SA, G), ind(v("GV"), v("KCU", SA, 48)), AF.Identity, (SENT - MID) * DX, -DX)
+            consts_b()
+        ts(v("REM2"), v("PRE"), v("PS4", 32, 33), A.add, 256.0 - G, A.is_lt)
         cp(ind(v("GA"), v("POSU", 0, SA)), v("GP", 0, 16 * SA))
-        act(ind(v("GB"), v("POSU", SA, 48)), v("GP", 16 * SA, G), AF.Silu)
-        ts(v("REM2"), v("SC"), v("PS4", 32, 33), A.add, 257.0, A.is_lt)
+        act(ind(v("GB"), v("POSU", SA, 48)), v("GP", 16 * SA, G), AF.Sigmoid)
         if s == 0:
             init_table()
-            consts_a()
-        else:
-            act(v("NBD"), v("TT", V, W), AF.Relu, 1024.0, 1024.0)
-        for lo, hi in ((0, NA // 16), (NA // 16, 256)):
-            tt(v("GC", lo, hi), v("GA", lo, hi), v("GB", lo, hi), A.max)
-        for lo, hi in ((0, NA // 16), (NA // 16, 256)):
-            ts(v("OFF", lo, hi), v("GC", lo, hi), -1.0, A.mult, SENT + 0.25, A.add)
-        act(v("GG", 0, NA), ind(TTw, v("OFF", 0, NA // 16)))
-        cp(v("GG", NA + NB, 4096), ind(TTw, v("OFF", (NA + NB) // 16, 256)))
-        act(v("GG", NA, NA + NC), ind(TTw, v("OFF", NA // 16, (NA + NC) // 16)))
-        act(v("GG", NA + NC, NA + NB), ind(TTw, v("OFF", (NA + NC) // 16, (NA + NB) // 16)))
-        chunks = ((0, NA), (NA + NB, 4096), (NA, NA + NC), (NA + NC, NA + NB))
-        if s == 0:
-            consts_b()
-        for lo, hi in chunks:
-            o = v("PS0", lo // 16, hi // 16)
-            mm([(o, v("ID"), v("C15", lo // 16, hi // 16))] + [(o, v("WZ"), v("GG", lo + i, hi, 16)) for i in range(15)])
-        for lo, hi in chunks:
-            scan(v("MX", lo, hi), v("MASK", 0, hi - lo), v("GG", lo, hi), A.min, A.max)
-        mm([(v("PS1", 0, 256), v("WN"), v("GG", 15, 4096, 16))])
-        mm([(v("PS4", 0, 16), v("WS", 128 * r, 128 * r + 128), v("GG", 16 * r + 15, 4096, 256)) for r in range(16)])
-        tt(v("RL"), v("PS0", 0, 256), v("MX", 14, 4096, 16), A.max)
-        mul(v("ZS", 0, 256), v("PS0", 0, 256), -1.0, 15.0)
-        act(v("AO"), v("PS4", 0, 16), AF.Abs, float(-K0), 1.0)
-        mul(v("NAO"), v("AO"), -1.0)
-        act(v("PN"), v("ZS", 0, 256), AF.Relu, float(-K0 - W + 1), 1.0)
-        mm([(v("PS3", 0, 16), v("ID"), v("KE"))] +
-           [(v("PS3", 0, 16), v("BS", 128 * r, 128 * r + 128), v("RL", r, 256, 16)) for r in range(16)])
-        tt(v("REM"), v("REM2"), v("AW"), A.is_ge)
-        if s == 0:
             consts_c()
+        else:
+            ts(v("RR", 0, 6 + 2 * s), v("PS3", 64, 70 + 2 * s), float(-K0), A.add)
+            act(v("RT", 0, 32 * s), ind(TTw, v("RR", 6, 6 + 2 * s)))
+            act(v("NBD", 0, 96), v("TT", V, W), AF.Relu, 1.0, 1.0)
+        parts = ((0, NA // 16), (NA // 16, NL // 16), (NL // 16, 256))
+        for lo, hi in parts:
+            tt(v("GC", lo, hi), v("GA", lo, hi), v("GB", lo, hi), A.max)
+        if s > 0:
+            cp(ind(TTw, v("AL", 0, 2 * s)), v("RT", 0, 32 * s))
+        for lo, hi in parts:
+            ts(v("OFF", lo, hi), v("GC", lo, hi), UNY, A.mult, UNC, A.add)
+        mm(wrap(v("PS4", 0, 16), "B15", "GC", 0, 256))
+        if not last:
+            dma(v("GA", 0, 256), v("FILL"))
+            dma(v("GB", 0, 256), v("FILL"))
+        act(v("GG", 0, NA), ind(TTw, v("OFF", 0, NA // 16)))
+        cp(v("GG", NA + NC, NL), ind(TTw, v("OFF", (NA + NC) // 16, NL // 16)))
+        act(v("GG", NA, NA + NC), ind(TTw, v("OFF", NA // 16, (NA + NC) // 16)))
+        act(v("GG", NL, 4096), ind(TTw, v("OFF", NL // 16, 256)))
+        chunks = ((0, NA, "PS0"), (NA + NC, NA + NC + NV, "PS0"), (NA, NA + NC, "PS0"), (NL, 4096, "PS5"))
+        for lo, hi, bank in chunks:
+            o = v(bank, lo // 16, hi // 16)
+            mm([(o, v("ID"), v("C15", lo // 16, hi // 16))] + [(o, v("WZ"), v("GG", lo + i, hi, 16)) for i in range(15)])
+        halves = ((0, NL // 16, "PS0"), (NL // 16, 256, "PS5"))
+
+        def largest(k):
+            lo, hi, bank = halves[k]
+            tt(v("RL", lo, hi), v(bank, lo, hi), v("MX", 16 * lo + 14, 16 * hi, 16), A.max)
+
+        def sums(k):
+            lo, hi, bank = halves[k]
+            mul(v("ZS", lo, hi), v(bank, lo, hi), -1.0, 15.0)
+            act(v("AD", lo, hi), v(bank, lo, hi), AF.Abs, float(K0 + W // 2 - 15), 1.0)
+
+        for k, (lo, hi, bank) in enumerate(chunks):
+            if k == 1:
+                ts(v("LO"), v("PS4", 0, 16), UNY, A.mult, UNC, A.add)
+                ts(v("DO", 1, 32, 2), v("PS4", 0, 16), UNY, A.mult, UNC, A.add)
+            if k == 3:
+                tt(v("REM"), v("REM2"), v("AW"), A.is_ge)
+                largest(0)
+            scan(v("MX", lo, hi), v("MASK", 0, hi - lo), v("GG", lo, hi), A.min, A.max)
+        sums(0)
+        act(v("CW", 0, 256), ind(CCw, v("LO")))
+        mm([(v("PS1", 0, 256), v("WN"), v("GG", 15, 4096, 16))])
+        mm([(v("PS3", 0, 32), v("ID"), v("KD", 0, 32))] + wrap(v("PS3", 0, 32, 2), "B2", "GG", 15, 4096, 16), True, True, False)
+        cp(v("CI", 0, 96), v(CN, V, W))
+        largest(1)
+        mm([(v("PS3", 0, 32), v("ID"), v("KD", 32, 64))] + wrap(v("PS3", 0, 32, 2), "BN", "RL", 0, 256), True, False, True)
+        sums(1)
+        mm([(v("PS2", 0, 256), v("IDB"), v("CC2")), (v("PS2", 0, 256), v("W2B"), v("GG", 15, 4096, 16)),
+            (v("PS2", 0, 256), v("BOB"), v("MX", 14, 4096, 16))], False, True, False)
+        own = [(t, v("CW", 128 * t, 128 * t + 128)) for t in OWN]
+        imp = [(2, v("CI"))]
         if last:
-            cp(ind(XW, v("AL", 0, 8)), v("NEG1"))
+            cp(ind(XW, v("AL", 0, 8)), v("NEG1", 0, 128))
+        ts(v("RC"), v("RL"), 15.0, A.min, -15.0, A.add)
         tt(v("EQ"), v("PS1", 0, 256), v("ZS", 0, 256), A.is_equal)
+        scan(v("LS"), v("DO"), v("PS3", 0, 32), A.max, A.min)
+        mm([(v("PS2", 0, 256), v("ID"), v("AD")), (v("PS2", 0, 256), v("IDB"), v("EQ"))], False, False, True)
+        turn(own)
+        if s == 0:
+            consts_d()
         mul(v("OS", 0, 256), v("PS1", 0, 256), 1.0)
-        tt(v("T1"), v("PS3", 0, 16), v("NAO"), A.min)
-        tt(v("T2"), v("T1"), v("NDW"), A.max)
-        ts(v("LB"), v("T2"), -1.0, A.mult)
-        ts(v("LW", 0, 64), ind(CCw, v("LB", 0, 4)), 1.0, A.add)
-        ts(v("LW", 64, 256), ind(CCw, v("LB", 4, 16)), 1.0, A.add)
-        mm([(v("PS2", 0, 256), v("IDB"), v("C392")), (v("PS2", 0, 256), v("W2B"), v("GG", 15, 4096, 16)),
-            (v("PS2", 0, 256), v("BOB"), v("MX", 14, 4096, 16)), (v("PS2", 0, 256), v("IDB"), v("PN")),
-            (v("PS2", 0, 256), v("IDB"), v("EQ"))])
+        cp(v("LB"), v("LS", 1, 32, 2))
+        act(v("WA"), v("PS2", 0, 256), AF.Sigmoid, 5000.0, -1.0)
         cp(ind(XW, v("LB")), v("MX", 14, 4096, 16))
-        tt(v("WA"), v("PS2", 0, 256), v("ZS", 0, 256), A.is_lt)
+        split(OWN)
+        mm(z_open("PS6", v("ZC"), own) +
+           [(v("PS6", 256 * t, 256 * t + 256), v("GG", 2048 * t + 15, 2048 * t + 2048, 16), v("G2Z")) for t in OWN] +
+           [(v("PS6", 256 * t, 256 * t + 256), v("RC", 128 * t, 128 * t + 128), v("GZ")) for t in OWN], True, True, False)
+        scan(v("PX"), v("ONES"), v("WA"), A.mult, A.add)
         ts(v("SB", 96 * s, 96 * s + 96), ind(XW, v("RR", 0, 6)), -1.0, A.max, 1.0, A.add)
         if last:
             dma(T.yx[:, 0:V], v("YX", 0, V))
-        if s == 0:
-            iota(v("IDF"), [[16, 124]])
-            iota(v("FF"), [[1, TW]])
         send(s)
+        for k in range(2):
+            act(v("LE", 256 * k, 256 * k + 256), v("PX"), AF.Sign, v("TC5", k, k + 1), -1.0, v("KA", k, k + 1))
+        mm(z_split("PS6", OWN), True, False, True)
+        mm([(v("PS0", 0, 256), v("WN"), v("GG", 15, 4096, 16)), (v("PS0", 0, 256), v("IDB"), v("WA")), (v("PS0", 0, 256), v("IDB"), v("NEG1"))])
         if s == 0:
-            for r in range(16):
-                keep(v("BF", 128 * r, 128 * r + 128), v("BO"), [[0, 8], [1, 16]], A.is_equal, -r, 0)
             consts_e()
-        for q in range(4):
-            act(v("G2", 1024 * q, 1024 * q + 1024), ind(v("TAB"), v("LW", 64 * q, 64 * q + 64)))
-        if s == 0:
-            consts_f()
-        relu(RA, RB, "a")
-        relu(RB, 4096, "a")
-        scan(v("PX"), v("ONES", 0, 256), v("WA"), A.mult, A.add)
-        mm([(v("PS0", 0, 256), v("WN"), v("GG", 15, 4096, 16)), (v("PS0", 0, 256), v("IDB"), v("WA"))])
-        ts(v("LE", 0, 256), v("PX"), v("TC", 0, 1), A.is_le)
-        ts(v("LE", 256, 512), v("PX"), v("TC", 1, 2), A.is_le)
-        scan(v("EE", 0, 256), v("ONES", 0, 256), v("LE", 0, 256), A.mult, A.add)
-        scan(v("EE", 256, 512), v("ONES", 0, 256), v("LE", 256, 512), A.mult, A.add)
-        cp(v("KU"), v("EE", 255, 512, 256))
-        sums("PS5", "G2", 0, 2048, True)
-        relu(0, 1024)
-        sums("PS6", "H2", 0, 1024, True)
-        sums("PS5", "G2", 2048, 3072)
+        powers("PS6", OWN)
+        onehot(OWN, 0, 6)
+        ts(v("KU"), v("KA"), 0.5, A.mult, 128.0, A.add)
+        onehot(OWN, 6, 8)
+        CO, CL = v("CI", 96, 128), v("NBD", 96, 128)
+        cp(CO, ind(v("CW"), v("KU")))
         tt(v("UD", 0, 32), ind(v("ZS"), v("KU")), v("DIAG"), A.mult)
-        tt(v("UD", 32, 64), ind(v("OS"), v("KU")), v("DIAG"), A.mult)
+        turn(imp)
+        split(IMP)
+        mm(z_open("PS2", v("ZI"), imp), True, True, False)
         tt(v("UT", 0, 32), ind(v("ZS"), v("KU")), v("TRI2", 0, 32), A.mult)
-        scan(v("US"), v("M01", 0, 64), v("UD"), A.mult, A.add)
         tt(v("UT", 32, 64), ind(v("ZS"), v("KU")), v("TRI2", 32, 64), A.mult)
-        ts(v("UOU"), v("US", 15, 64, 16), float(-K0), A.add)
-        ts(v("UB"), v("US", 15, 32, 16), BIG, A.add)
-        cp(v("CG"), ind(CCw, v("UOU")))
-        ts(v("EE", 0, 256), v("PS0", 0, 256), v("UB", 0, 1), A.is_equal, 2048.0, A.mult)
-        ts(v("EE", 256, 288), v("UT", 0, 32), v("US", 15, 16), A.is_equal, 2048.0, A.mult)
-        tt(v("CL"), v("CG", 0, 32), v("CG", 32, 64), A.min)
-        scan(v("ES", 0, 288), v("ONES"), v("EE", 0, 288), A.mult, A.max)
-        ts(v("EE", 544, 576), v("UT", 32, 64), v("US", 31, 32), A.is_equal, 2048.0, A.mult)
-        tt(v("CT"), ind(XW, v("UOU", 0, 2)), v("CL"), A.max)
-        mm([(v("PS3", 32, 34), v("ID"), v("KP"))] +
-           [(v("PS3", 32, 34), v("BS", 128 * r, 128 * r + 128), v("CT", r, 32, 16)) for r in range(16)])
-        relu(1024, RA)
-        sums("PS6", "H2", 1024, RA)
-        ts(v("EE", 288, 544), v("PS0", 0, 256), v("UB", 1, 2), A.is_equal, 2048.0, A.mult)
+        scan(v("US", 0, 32), v("M01", 0, 32), v("UD", 0, 32), A.mult, A.add)
+        onehot(OWN, 8, 10)
+        ts(v("UL"), v("US", 15, 32, 16), float(-K0), A.add)
+        ts(v("FI"), v("US", 15, 32, 16), float(16 - K0 - V), A.add, 111.0, A.min)
+        for k in range(2):
+            ts(v("ET", 32 * k, 32 * k + 32), v("UT", 32 * k, 32 * k + 32), v("US", 15 + 16 * k, 16 + 16 * k), A.is_equal)
+        tt(CL, ind(CCw, v("UL")), CO, A.min)
+        act(v("UR"), ind(TTw, v("UL")))
+        onehot(OWN, 10, 16)
+        mm([(v("PS2", 0, 256, p=PU), v("ET", 32 * k, 32 * k + 32), v("NGZ")) for k in range(2)] +
+           [(v("PS2", 0, 256), v("NBD"), v("NGZ"))] + z_split("PS2", IMP), True, False, False)
+        arrival(s)
+        c = 96 * s
+        land = [(v("PS1", 32 * d, 32 * d + 32), v(("P1", "P2", "ID")[d]), v("LD", c + 32 * d, c + 32 * d + 32)) for d in range(3)]
+        mm(land)
+        words(OWN, True, False)
+        act(v("FL", 16, 112), v("PS1", 0, 96), AF.Relu, 1.0, -1.0)
+        onehot(IMP, 0, NI)
+        cp(v("FL", 112, 144), ind(v("FL", 0, 112), v("FI")))
+        onehot(IMP, NI, 16)
+        mm([(v("PS2", 0, 256), v("FL", 16, 144), v("NGZ"))], True, False, True)
+        powers("PS2", IMP)
+        tt(v("CT"), ind(XW, v("UL")), CL, A.max)
+        tt(v("UD", 32, 64), ind(v("OS"), v("KU")), v("DIAG"), A.mult)
+        mm([(v("PS3", 32, 34), v("ID"), v("KP"))] + wrap(v("PS3", 32, 34), "BS", "ET", 0, 32), False, True, False)
+        words(IMP, False, True)
+        mul(v("WO"), v("PS7", 0, 256), 2.0 ** LOW)
+        mm(wrap(v("PS3", 32, 34), "BS", "ET", 32, 64) + wrap(v("PS3", 32, 34), "BS", "CT", 0, 32), False, False, True)
+        for k in range(2):
+            ts(v("EE", 256 * k, 256 * k + 256), v("PS0", 0, 256), v("US", 15 + 16 * k, 16 + 16 * k), A.is_equal, 2048.0, A.mult)
+        scan(v("US", 32, 64), v("M01", 0, 32), v("UD", 32, 64), A.mult, A.add)
+        if last:
+            mul(v("YX", V, W), v("PS1", 0, 96), 1.0, -1.0)
+            dma(T.yx[:, V:W], v("YX", V, W))
+        else:
+            mm([(v("PS1", 128, 224), v("ID"), v("NEG1", 0, 96)), (v("PS1", 128, 224), v("NID"), v("FL", 16, 112))] +
+               [(v("PS1", 128 + o[2], 128 + o[3]), l, r) for o, l, r in land], True)
+        for k in range(2):
+            scan(v("ES", 256 * k, 256 * k + 256), v("ONES"), v("EE", 256 * k, 256 * k + 256), A.mult, A.max)
         ts(v("UOC"), v("US", 15, 64, 16), float(K0 + W), A.min, float(-K0), A.add)
-        scan(v("ES", 288, 576), v("ONES"), v("EE", 288, 576), A.mult, A.max)
-        tt(v("X1"), v("PS3", 32, 34), v("ES", 287, 576, 288), A.max)
-        tt(v("MG"), v("CG", 0, 32), v("CG", 32, 64), A.max)
-        for name, base, src in (("UW", 0, 0), ("AL", 2 * s, 2)):
+        tt(v("MG"), ind(CCw, v("UL")), CO, A.max)
+        cp(v("D2"), ind(v("WO"), v("WL")))
+        for k in range(6):
+            ts(v("D3", 32 * k, 32 * k + 32), v("D2"), k, A.logical_shift_right, 0o01010101, A.bitwise_and)
+        tt(v("X1"), v("PS3", 32, 34), v("ES", 255, 512, 256), A.max)
+        scan(v("D5"), v("M01"), v("D3"), A.mult, A.add)
+
+        def pick(name, base, src):
             for k in range(2):
                 ts(v(name, base + k, base + k + 1), v("X1", k, k + 1), v("DA", 2 * s + k, 2 * s + k + 1), A.min,
                    v("UOC", src + k, src + k + 1), A.max)
-        cp(ind(CCw, v("UW")), v("MG"))
-        ts(v("UR"), ind(v("ZS"), v("KU")), float(-K0), A.add)
-        sums("PS5", "G2", 3072, 4096)
-        arrival(s)
-        c = 96 * s
-        for d in range(3):
-            o = v("PS7", 128 + 32 * d, 160 + 32 * d)
-            mm([(o, v("NID"), v("NBD", 32 * d, 32 * d + 32)), (o, v("ID"), v("NEG1", 0, 32)),
-                (o, v(("Q1", "Q2", "Q3")[d]), v("LD", c + 32 * d, c + 32 * d + 32))])
-        tt(v("CM"), v("PS7", 128, 224), v(CN, V, W), A.min)
-        sums("PS6", "H2", RA, RB)
-        mm([(v("PS7", 32 * d, 32 * d + 32), v(("Q1", "Q2", "Q3")[d]), v("LD", c + 32 * d, c + 32 * d + 32)) for d in range(3)])
-        for d in range(0 if last else 3):
-            mm([(v("PS2", 32 * d, 32 * d + 32), v(("P1", "P2", "ID")[d]), v("LD", c + 32 * d, c + 32 * d + 32)),
-                (v("PS2", 32 * d, 32 * d + 32), v("ID"), v("CODE", V + 32 * d, V + 32 * d + 32))])
-        cp(v("RR", 6 + 2 * s, 8 + 2 * s), v("AL", 2 * s, 2 * s + 2))
-        ts(v("LW", 256, 352), v("CM"), 1.0, A.add)
-        sums("PS6", "H2", RB, 4096)
-        cp(v("G2", 4096 + IA, 5632), ind(v("TAB"), v("LW", 256 + IA // 16, 352)))
-        act(v("G2", 4096, 4096 + IB), ind(v("TAB"), v("LW", 256, 256 + IB // 16)))
-        act(v("G2", 4096 + IB, 4096 + IA), ind(v("TAB"), v("LW", 256 + IB // 16, 256 + IA // 16)))
-        parts = ((4096, 4096 + IB), (4096 + IA, 5632), (4096 + IB, 4096 + IA))
-        sums("PS5", "G2", *parts[0])
-        sums("PS5", "G2", *parts[1])
-        for k, (lo, hi) in enumerate(parts):
-            relu(lo, hi)
-            sums("PS6", "H2", lo, hi, False, k == 2)
-            if k == 0:
-                sums("PS5", "G2", *parts[2], False, True)
-        cp(ind(FFw, v("AL", 2 * s, 2 * s + 2)), v("UR"))
-        nr, na = 8 + 2 * s, 2 * s + 2
         if not last:
-            act(v("RG", 0, 16 * nr), ind(FFw, v("RR", 0, nr)))
-            mm([(v("PS4", 64, 64 + nr), v("BF", 128 * r, 128 * r + 128), v("RG", r, 16 * nr, 16)) for r in range(16)])
-            tt(v("YY"), v("PS7", 0, 96), v("DI"), A.min)
-            tt(v("TT", V, W), v("PS2", 0, 96), v("YY"), A.add)
-            fill(v("GA", 0, 256), 0.0)
-            fill(v("GB", 0, 256), 0.0)
+            tt(v("TT", V, W), v("PS1", 128, 224), v("CODE", V, W), A.max)
+        pick("AL", 2 * s, 2)
+        pick("RR", 6 + 2 * s, 2)
+        for f in range(4):
+            ts(v("D7", 12 * f, 12 * f + 12), v("D5", 15, 192, 16), 63 << (6 * f), A.bitwise_and)
+        cp(ind(FCw, v("AL", 2 * s, 2 * s + 2)), v("UR"))
+        nr = 8 + 2 * s
+        r0 = 6 if last else 0
+        act(v("RG", 16 * r0, 16 * nr), ind(FCw, v("RR", r0, nr)))
+        for w in range(2):
+            tt(v("AWF" if last else "AW", 24 * w, 24 * w + 24), v("D7", w, 48, 2), v("REM", 24 * w, 24 * w + 24), A.is_ge)
+        pick("UW", 0, 0)
+        if not last:
+            scan(v("NK"), v("ONES", 0, 48), v("AW"), A.add, A.add)
+            mm([(v("PS4", 32, 33), v("TRI"), v("NK", 47, 48))])
+            tt(v("NK2"), v("AW"), v("KC2"), A.mult)
+        cp(ind(CCw, v("UW")), v("MG"))
+        if not last:
+            mm(wrap(v("PS3", 64, 64 + nr), "WS", "RG", 0, 16 * nr))
+            if s == 0:
+                ts(v("IDU"), v("IDF"), v("RF"), A.add, float(TW - 1), A.min)
+                act(v("CF"), ind(CCw, v("IDU")))
             if s == S - 2:
                 act(v("YR"), TTw, AF.Relu, 1.0, 1.0)
+                mul(v("YX"), v("YR"), 1.0, -1.0)
         else:
-            act(v("RG", 0, 160), ind(FFw, v("RR", 6, 16)))
-            mul(v("YX", V, W), v("PS7", 0, 96), 1.0 / 8192, -1.0)
-            dma(T.yx[:, V:W], v("YX", V, W))
+            dma(T.yw[:], v("AWF"))
+            mm([(v("PS4", 0, 160), v("WN"), v("RG", 96, 256))])
             for b in range(3):
                 mm([(v("PS%d" % b, p=(0, 8)), v("B8"), v("CF", 512 * b, 512 * b + 512))])
-        cp(v("D0", 0, 128, 2), v("PS6", 0, 64))
-        tt(v("D0", 1, 128, 2), v("D0", 0, 128, 2), v("PS5", 0, 64), A.subtract)
-        if last:
-            cp(ind(FFw, v("AL")), v("RG", 0, 160))
+            mul(v("RO"), v("PS4", 0, 160), 1.0, float(-K0))
+            cp(ind(FFw, v("AL")), v("RO"))
             dma(T.yf[:], v("FF", 0, W, p=(0, 128, 16)))
             for b in range(3):
                 mul(v("YC", 512 * b, 512 * b + 512, p=(0, 8)), v("PS%d" % b, p=(0, 8)), 1.0)
             dma(T.yc[:], v("YC", p=(0, 8)), "a")
-        tt(v("D1"), v("D0", 0, 64), v("D0", 64, 128), A.add)
-        if s == 0:
-            ts(v("IDU"), v("IDF"), v("RF"), A.add, float(TW - 1), A.min)
-            act(v("CF"), ind(CCw, v("IDU")))
-        for w in range(2):
-            tt(v("D2", 16 * w, 16 * w + 16), v("D1", w, 32, 2), v("D1", 32 + w, 64, 2), A.add)
-        for k in range(6):
-            ts(v("D3", 32 * k, 32 * k + 32), v("D2"), k, A.logical_shift_right, 0o01010101, A.bitwise_and)
-        cp(v("D4"), v("D3"))
-        scan(v("D5"), v("M01"), v("D4"), A.mult, A.add)
-        if not last:
-            ts(v("RR", 0, nr), v("PS4", 64, 64 + nr), 1.0 / 16, A.mult)
-            act(v("RT", 0, 16 * na), ind(TTw, v("RR", 6, 6 + na)))
-            if s == S - 2:
-                mul(v("YX"), v("YR"), 1.0, -1.0)
-        cp(v("D6"), v("D5", 15, 192, 16))
-        for f in range(4):
-            ts(v("D7", 12 * f, 12 * f + 12), v("D6"), 63 << (6 * f), A.bitwise_and)
-        tt(v("AWF" if last else "AW"), v("D7"), v("REM"), A.is_ge)
-        if last:
-            dma(T.yw[:], v("AWF"))
 
     Q = {"v": g.vector, "a": g.scalar, "p": g.tensor, "g": g, "s": g.sync}
     SEM = {"v": "sv", "a": "sa", "p": "sp", "g": "sg"}
@@ -504,13 +565,14 @@ def rank_program(g, core, T, topo):
     for q, fn, rd, wr, kind in ops:
         need = {}
         for spn, isw in [(x, False) for x in rd] + [(x, True) for x in wr]:
-            name, lo, hi = spn
+            name, lo, hi, st = spn
             ps = name.startswith("PS")
-            for (l2, h2, w2, q2, sem, val, kn) in hist.get(name, []):
+            for (l2, h2, w2, q2, sem, val, kn, s2) in hist.get(name, []):
                 if ps and q2 != q:
                     hit = True
                 else:
                     hit = l2 < hi and lo < h2 and (isw or w2) and not (q == "p" and q2 == "p")
+                    hit = hit and not (st == s2 > 1 and (lo - l2) % st)
                 if hit and known[q].get(sem, 0) < val and need.get(sem, (0,))[0] < val:
                     need[sem] = (val, kn)
         for sem, (val, kn) in sorted(need.items(), key=lambda z: -len(z[1][1])):
@@ -538,8 +600,8 @@ def rank_program(g, core, T, topo):
         for spn, isw in [(x, False) for x in rd] + [(x, True) for x in wr]:
             h = hist.setdefault(spn[0], [])
             if isw:
-                h[:] = [e for e in h if not (spn[1] <= e[0] and e[1] <= spn[2] and known[q].get(e[4], 0) >= e[5])]
-            h.append((spn[1], spn[2], isw, q, sem, count[sem], kn))
+                h[:] = [e for e in h if not (spn[3] == 1 and spn[1] <= e[0] and e[1] <= spn[2] and known[q].get(e[4], 0) >= e[5])]
+            h.append((spn[1], spn[2], isw, q, sem, count[sem], kn, spn[3]))
     g.wait_ge(T.sem.sent, leave * S)
     for k, n in count.items():
         if n > waited.get(k, 0):

@@ -32,8 +32,8 @@ BUF = {
     "CW": (272, f32), "AA": (384, bf), "WB": (384, bf), "WW": (768, bf), "OH": (6144, bf), "WO": (256, f32), "WL": (2, u16),
     "WA": (256, bf), "PX": (256, bf), "LE": (512, bf), "KA": (2, f32), "KU": (2, u16), "TC": (2, f32), "TC5": (2, f32),
     "UD": (64, f32), "US": (64, f32), "UL": (2, u16), "FI": (2, u16), "UOC": (4, f32), "UR": (32, bf), "UT": (64, f32), "TRI2": (64, f32),
-    "MG": (32, f32), "CT": (32, bf), "ET": (64, bf), "EE": (512, bf), "ES": (512, bf),
-    "X1": (2, f32), "DA": (10, f32), "UW": (2, u16), "AL": (10, u16), "RR": (16, u16),
+    "MG": (32, f32), "CL": (32, bf), "EM": (32, bf), "CT": (32, bf), "ET": (64, bf), "EE": (512, bf), "ES": (512, bf),
+    "X1": (2, f32), "DA": (10, f32), "UW": (4, u16), "AL": (10, u16), "RR": (16, u16),
     "RG": (256, bf), "RO": (160, f32), "RT": (160, bf), "NEG1": (256, bf),
     "SB": (96 * S, bf), "LD": (96 * S, bf), "NBD": (128, bf), "CI": (128, f32), "FL": (144, bf),
     "D2": (32, i32), "D3": (192, i32), "D5": (192, i32), "D7": (48, i32), "ZC": (512, bf), "ZI": (256, bf),
@@ -43,7 +43,7 @@ BUF = {
     "W2B": (128, bf), "IDB": (128, bf), "P1": (128, bf), "P2": (128, bf),
     "PM": (128, f32), "IZ": (128 * 4, bf), "GZ": (256, bf), "NGZ": (256, bf), "G2Z": (256, bf),
     "BS": (144, bf), "BN": (144, bf), "B2": (144, bf), "B15": (144, f32), "WS": (144, bf), "KP": (2, bf),
-    "YC": (W, f32), "YX": (TW, bf), "YR": (TW, bf),
+    "YC": (TW, f32), "YM": (64, f32), "YX": (TW, bf), "BOF": (128, f32), "B60": (128, bf), "L2": (128, bf),
 }
 SCRATCH, PLACE, _fill = {}, {}, {}
 for _k, (_n, _d) in BUF.items():
@@ -167,9 +167,9 @@ def rank_program(g, core, T, topo):
     def keep(o, i, pat, f, base, cm):
         op("g", lambda: g.affine_select(ap(o), ap(i), pat, f, 0.0, base, cm), [o], [i])
 
-    def dma(o, i, q="s"):
+    def dma(o, i, q="s", after=None):
         e = g.sync if q == "s" else g.scalar
-        op(q, lambda: e.dma_start(ap(o), ap(i)), [o], [i], "d")
+        op(q, lambda: e.dma_start(ap(o), ap(i)), [o], [i, after], "d")
 
     def wrap(o, mat, src, lo, hi, step=1):
         return [(o, v(mat, 15 - r, 143 - r), v(src, lo + step * r, hi, 16 * step)) for r in range(16)]
@@ -194,127 +194,127 @@ def rank_program(g, core, T, topo):
     def arrival(s):
         op("p", lambda: g.tensor.wait_ge(T.sem["arr%d" % s], arrive), [], [], "w")
 
-    dma(v("AWI"), T.aw[:])
+    dma(v("AWI"), T.aw[:], "a")
     dma(v("GV"), T.gv[:])
-    dma(v("XB"), T.x0[:], "a")
-    dma(v("EXI"), T.ex[:])
-    dma(v("CC", 0, W), T.co[:])
+    dma(v("XB"), T.x0[:])
+    dma(v("EXI"), T.ex[:], "a")
+    dma(v("CC", 0, W), T.co[:], after=v("XB"))
     iota(v("PC"), [[1, 1]], 0, 1)
     iota(v("JR"), [[1, 256]])
     iota(v("JG"), [[1, 8], [0, 16]])
     mset(v("ZO"), 0.0)
     act(v("ONES"), v("ZO"), AF.Sigmoid, 40.0, 0.0)
-    mset(v("FILL"), 0.5 - MID * DX * KX)
-    dma(v("GA", 0, 256), v("FILL"))
-    dma(v("GB", 0, 256), v("FILL"))
+    mset(v("GA", 0, 256), 0.5 - MID * DX * KX)
     mset(v("TT", W, TW), 0.0)
     ts(v("RCI"), v("PC"), 15, A.bitwise_and)
     ts(v("GCI"), v("PC"), 4, A.arith_shift_right)
     cp(v("PF"), v("PC"))
+    mset(v("GB", 0, 256), 0.5 - MID * DX * KX)
     cp(v("RF"), v("RCI"))
     cp(v("GF"), v("GCI"))
-    ts(v("R48"), v("RF"), 48.0, A.mult)
+    mset(v("DO", 0, 32, 2), 1e29)
+    mset(v("KD", 0, 32, 2), C2 * 2.0 ** 24)
+    mset(v("KD", 32, 64, 2), 240 * 2048.0)
     ts(v("DIAG", 0, 16), v("JR", 0, 16), v("RF"), A.is_equal)
-    ts(v("KCU"), v("JR", 0, 48), v("R48"), A.add)
-    ts(v("KC2"), v("JR", 0, 48), v("R48"), A.add, float(G + 2), A.add)
+    ts(v("R48"), v("RF"), 48.0, A.mult)
+    ts(v("ID"), v("JR", 0, 128), v("PF"), A.is_equal)
+    ts(v("G15"), v("GF"), 16.0, A.mult, 15.0, A.add)
     ts(v("BO"), v("JG"), v("GF"), A.is_equal)
     keep(v("TRI"), v("BO"), [[1, 128]], A.is_gt, 0, -1)
-    ts(v("ID"), v("JR", 0, 128), v("PF"), A.is_equal)
-    iota(v("MASK", 0, 384), [[0, 24], [16, 16]])
-    for q in range(1, 4):
-        dma(v("MASK", 384 * q, 384 * q + 384), v("MASK", 0, 384))
-    ts(v("WC", 4, 5), v("DIAG", 0, 1), -1.0, A.mult)
     ts(v("WC", 5, 6), v("DIAG", 2, 3), 1.0 - C2, A.mult, -1.0, A.add)
     ts(v("WC", 6, 7), v("DIAG", 1, 2), -1.0, A.mult)
-    ts(v("G15"), v("GF"), 16.0, A.mult, 15.0, A.add)
+    ts(v("WC", 4, 5), v("DIAG", 0, 1), -1.0, A.mult)
+    ts(v("WC", 8, 9), v("DIAG", 2, 3), -2.0, A.mult)
+    ts(v("KCU"), v("JR", 0, 48), v("R48"), A.add)
+    ts(v("KC2"), v("JR", 0, 48), v("R48"), A.add, float(G + 2), A.add)
     ts(v("HB"), v("JR", 0, 6), v("WC", 6, 7), A.mult, v("WC", 5, 6), A.add)
+    ts(v("B60"), v("BO"), C2 / 8.0, A.mult)
+    ts(v("L2"), v("BO"), v("WC", 8, 9), A.mult)
     cp(v("AW"), v("AWI"))
     for h in range(6):
         ts(v("CODE", 256 * h, 256 * h + 256), v("JR"), v("WC", 4, 5), A.mult, v("HB", h, h + 1), A.add)
-    dma(v("FC", 0, W), v("CODE"))
-    dma(v("FC", W, TW), v("TT", W, TW))
+    iota(v("MASK", 0, 384), [[0, 24], [16, 16]])
+    for q in range(1, 4):
+        dma(v("MASK", 384 * q, 384 * q + 384), v("MASK", 0, 384))
+    fill(v("FILL"), 0.5 - MID * DX * KX)
     fill(v("KP"), 32768.0)
     fill(v("ZS", 256, 272), float(K0 + SENT))
     fill(v("OS", 256, 272), float(K0 + SENT))
     fill(v("CW", 256, 272), -1.0)
-    fill(v("C15"), 15.0)
     mul(v("WC", 0, 1), v("DIAG", 1, 2), 256.0, v("DIAG", 0, 1))
     mul(v("WC", 3, 4), v("DIAG", 2, 3), BIG)
-    mul(v("WC", 1, 2), v("DIAG", 2, 3), 256.0, v("WC", 0, 1))
     mul(v("WC", 7, 8), v("DIAG", 2, 3), 2.0 ** 24)
-    mul(v("WC", 8, 9), v("DIAG", 2, 3), -2.0)
+    mul(v("IDB"), v("ID"), BIG)
+    mul(v("WC", 1, 2), v("DIAG", 2, 3), 256.0, v("WC", 0, 1))
+    mul(v("BOB"), v("BO"), BIG)
     mul(v("WC", 2, 3), v("WC", 1, 2), -1.0)
-    mul(v("NID"), v("ID"), -8192.0)
     mul(v("WZ"), v("BO"), v("WC", 1, 2))
+    mul(v("W2B"), v("BO"), v("WC", 3, 4))
     mul(v("WN"), v("BO"), v("WC", 2, 3))
-    act(v("ZB"), v("XB"), AF.Relu, 0.0, -1.0)
     iota(v("JG2"), [[0, 16], [1, 8], [0, 2]])
+    iota(v("C15"), [[0, 256]], 15)
     iota(v("CC", W, TW), [[0, TW - W]], -1)
+    iota(v("CC2"), [[0, 256]], C2)
+    iota(v("ZC"), [[0, 256], [int(Z1 - Z0), 2]], int(Z0 - 2 * C2))
+    iota(v("NEG1"), [[0, 256]], -1)
     keep(v("M01"), v("ONES", 0, 192), [[0, 12], [1, 16]], A.is_gt, 0, 0)
+    iota(v("ZI"), [[0, 128], [int(Z1 - Z0), 2]], int(Z0))
+    iota(v("NBD"), [[0, 128]], 0)
+    iota(v("FL"), [[0, 144]], 1)
     iota(v("DA"), [[16, 10]], W + 256, 0)
     iota(v("IDF"), [[16, 124]])
-    iota(v("FF"), [[1, TW]])
 
     def consts_a():
-        cp(v("DIAG", 16, 32), v("DIAG", 0, 16))
-        ts(v("TC"), v("JR", 0, 32, 16), v("RF"), A.add)
         ts(v("B15"), v("JR", 0, 144), v("G15"), A.is_equal, v("DIAG", 15, 16), A.mult)
-        ts(v("BS"), v("JR", 0, 144), v("G15"), A.is_equal, 2048.0, A.mult)
-        ts(v("BN"), v("JR", 0, 144), v("G15"), A.is_equal, -2048.0, A.mult)
+        ts(v("TC"), v("JR", 0, 32, 16), v("RF"), A.add)
         ts(v("PMC"), v("RF"), 8.0, A.mult, v("GF"), A.add)
-        ts(v("TC5"), v("TC"), 0.5, A.add)
-        ts(v("TRI2", 0, 32), v("JR", 0, 32), v("TC", 0, 1), A.is_gt)
-        ts(v("TRI2", 32, 64), v("JR", 0, 32), v("TC", 1, 2), A.is_gt)
-        ts(v("B8"), v("JR", 0, 8), v("GF"), A.is_equal)
-        ts(v("PM"), v("JR", 0, 128), v("PMC"), A.is_equal)
-        mset(v("DO", 0, 32, 2), 1e29)
-        mset(v("KD", 0, 32, 2), C2 * 2.0 ** 24)
-        ts(v("KD", 1, 32, 2), v("JR", 0, 256, 16), float(W), A.add)
-        mset(v("KD", 32, 64, 2), 240 * 2048.0)
-        ts(v("KD", 33, 64, 2), v("JR", 0, 16), 0.0, A.mult, v("RF"), A.add)
-        ts(v("WL"), v("JR", 0, 2), v("PMC"), A.add, v("PMC"), A.add)
         ts(v("TG"), v("RF"), 2.0, A.mult, v("PF"), A.subtract)
+        ts(v("BN"), v("JR", 0, 144), v("G15"), A.is_equal, -2048.0, A.mult)
+        ts(v("KD", 1, 32, 2), v("JR", 0, 256, 16), float(W), A.add)
+        ts(v("KD", 33, 64, 2), v("JR", 0, 16), 0.0, A.mult, v("RF"), A.add)
 
     def consts_b():
-        ts(v("B2"), v("JR", 0, 144), v("G15"), A.is_equal, v("WC", 7, 8), A.mult)
-        ts(v("WS"), v("JR", 0, 144), v("G15"), A.is_equal, v("WC", 2, 3), A.mult)
-        ts(v("GZ"), v("JG2"), v("GF"), A.is_equal, 64.0, A.mult)
-        ts(v("G2Z"), v("JG2"), v("GF"), A.is_equal, v("WC", 8, 9), A.mult)
-        ts(v("P1"), v("JR", 0, 128), -112.0, A.add, v("TG"), A.is_equal)
-        cp(v("RR", 0, 6), v("EXI"))
-        ts(v("DA"), v("DA"), v("RF"), A.add)
-
-    def consts_c():
-        fill(v("CC2"), float(C2))
-        mul(v("BOB"), v("BO"), BIG)
-        mul(v("IDB"), v("ID"), BIG)
-        mul(v("W2B"), v("BO"), v("WC", 3, 4))
-
-    def consts_d():
-        fill(v("NEG1"), -1.0)
-        fill(v("ZC", 0, 512, 2), Z0 - 2 * C2)
-        fill(v("ZC", 1, 512, 2), Z1 - 2 * C2)
+        mul(v("NID"), v("ID"), -8192.0)
         for k, c in enumerate((-64.0, 80.0, 64.0, -176.0)):
             mul(v("IZ", 128 * k, 128 * k + 128), v("ID"), c)
 
+    def consts_c():
+        ts(v("B2"), v("JR", 0, 144), v("G15"), A.is_equal, v("WC", 7, 8), A.mult)
+        ts(v("PM"), v("JR", 0, 128), v("PMC"), A.is_equal)
+        ts(v("GZ"), v("JG2"), v("GF"), A.is_equal, 64.0, A.mult)
+        ts(v("G2Z"), v("JG2"), v("GF"), A.is_equal, v("WC", 8, 9), A.mult)
+        cp(v("RR", 0, 6), v("EXI"))
+
+    def consts_d():
+        ts(v("TC5"), v("TC"), 0.5, A.add)
+        cp(v("DIAG", 16, 32), v("DIAG", 0, 16))
+        ts(v("TRI2", 0, 32), v("JR", 0, 32), v("TC", 0, 1), A.is_gt)
+        ts(v("TRI2", 32, 64), v("JR", 0, 32), v("TC", 1, 2), A.is_gt)
+        ts(v("P1"), v("JR", 0, 128), -112.0, A.add, v("TG"), A.is_equal)
+        ts(v("IDU"), v("IDF"), v("RF"), A.add, float(TW - 1), A.min)
+
     def consts_e():
-        for w, z in enumerate((Z0, Z1)):
-            fill(v("ZI", w, 256, 2, p=(0, 96)), z)
-            fill(v("ZI", w, 256, 2, p=(96, 128)), z - 1024)
+        ts(v("BS"), v("JR", 0, 144), v("G15"), A.is_equal, 2048.0, A.mult)
+        ts(v("WS"), v("JR", 0, 144), v("G15"), A.is_equal, v("WC", 2, 3), A.mult)
+        ts(v("WL"), v("JR", 0, 2), v("PMC"), A.add, v("PMC"), A.add)
+        ts(v("DA"), v("DA"), v("RF"), A.add)
+
+    def consts_f():
         mul(v("NGZ"), v("GZ"), -1.0)
-        fill(v("NBD"), 0.0)
-        fill(v("FL"), 1.0)
+        for w, z in enumerate((Z0, Z1)):
+            fill(v("ZI", w, 256, 2, p=(96, 128)), z - 1024)
         mul(v("P2", 16, 128), v("P1", 0, 112), 1.0)
         mul(v("P2", 0, 16), v("P1", 112, 128), 1.0)
 
     def init_table():
         for b in range(3):
-            lo, hi = 480 * b, 480 * b + 480
-            mm([(v("PS%d" % b, 0, 480), v("ID"), v("XB", lo, hi)), (v("PS%d" % b, 0, 480), v("NID"), v("ZB", lo, hi))])
+            o, code = v("PS%d" % b, 0, 480), v("CODE", 480 * b, 480 * b + 480)
+            mm([(o, v("ID"), code), (o, v("L2"), code)], False, True, False)
+        for b in range(3):
+            mm([(v("PS%d" % b, 0, 480), v("B60"), v("XB", 480 * b, 480 * b + 480))], False, False, True)
         for b in range(3):
             lo, hi = 480 * b, 480 * b + 480
-            tt(v("TT", lo, hi), v("PS%d" % b, 0, 480), v("CODE", lo, hi), A.max)
-        cp(v("TT", V, W), v("CODE", V, W))
+            tt(v("TT", lo, hi), v("PS%d" % b, 0, 480), v("XB", lo, hi), A.min)
 
     TTw, FFw, FCw = v("TT"), v("FF"), v("FC")
 
@@ -349,7 +349,14 @@ def rank_program(g, core, T, topo):
         mm(head + [(v("PS7", 16 * i, 16 * i + 16), v("OH", 2048 * t + 128 * i, 2048 * t + 128 * i + 128),
                     v("WW", 256 * t + 16 * i, 256 * t + 16 * i + 16)) for t in tiles for i in range(16)], True, start, stop)
 
-    OWN, IMP, PI, PU = (0, 1), (2,), (0, 96), (96, 128)
+    def floats(k):
+        lo, hi = ((0, 32), (32, 64), (64, 124))[k]
+        act(v("CF", 16 * lo, 16 * hi), ind(v("CC"), v("IDU", lo, hi)))
+
+    def row_sums(b):
+        mul(v("YC", 512 * b, 512 * b + 512), v("PS%d" % (5 + b)), 1.0)
+
+    OWN, IMP = (0, 1), (2,)
     for s in range(S):
         last = s == S - 1
         CN = "CC" if s == 0 else "CF"
@@ -361,26 +368,27 @@ def rank_program(g, core, T, topo):
             tt(v("NK2"), v("AW"), v("KC2"), A.mult)
         tt(v("PRE"), v("NK"), v("NK2"), A.subtract)
         ts(v("POSU"), v("PRE"), v("PS4", 32, 33), A.add, float(G), A.add)
+        ts(v("REM2"), v("PRE"), v("PS4", 32, 33), A.add, 256.0 - G, A.is_lt)
         if s == 0:
             consts_a()
             ts(v("GP", 0, 16 * SA), ind(v("GV"), v("KCU", 0, SA)), -DX * KX, A.mult, 0.5 + (SENT - MID) * DX * KX, A.add)
             act(v("GP", 16 * SA, G), ind(v("GV"), v("KCU", SA, 48)), AF.Identity, (SENT - MID) * DX, -DX)
-            consts_b()
-        ts(v("REM2"), v("PRE"), v("PS4", 32, 33), A.add, 256.0 - G, A.is_lt)
+            cp(v("TT", V, W), v("CODE", V, W))
         cp(ind(v("GA"), v("POSU", 0, SA)), v("GP", 0, 16 * SA))
         act(ind(v("GB"), v("POSU", SA, 48)), v("GP", 16 * SA, G), AF.Sigmoid)
         if s == 0:
             init_table()
-            consts_c()
+            consts_b()
         else:
-            ts(v("RR", 0, 6 + 2 * s), v("PS3", 64, 70 + 2 * s), float(-K0), A.add)
-            act(v("RT", 0, 32 * s), ind(TTw, v("RR", 6, 6 + 2 * s)))
+            cp(ind(TTw, v("AL", 0, 2 * s)), v("RT", 0, 32 * s))
             act(v("NBD", 0, 96), v("TT", V, W), AF.Relu, 1.0, 1.0)
+        if s == 1:
+            cp(ind(v("CF", 0, TW), v("UW", 0, 2)), v("MG"))
+        if last:
+            row_sums(2)
         parts = ((0, NA // 16), (NA // 16, NL // 16), (NL // 16, 256))
         for lo, hi in parts:
             tt(v("GC", lo, hi), v("GA", lo, hi), v("GB", lo, hi), A.max)
-        if s > 0:
-            cp(ind(TTw, v("AL", 0, 2 * s)), v("RT", 0, 32 * s))
         for lo, hi in parts:
             ts(v("OFF", lo, hi), v("GC", lo, hi), UNY, A.mult, UNC, A.add)
         mm(wrap(v("PS4", 0, 16), "B15", "GC", 0, 256))
@@ -412,6 +420,10 @@ def rank_program(g, core, T, topo):
                 ts(v("DO", 1, 32, 2), v("PS4", 0, 16), UNY, A.mult, UNC, A.add)
             if k == 3:
                 tt(v("REM"), v("REM2"), v("AW"), A.is_ge)
+                if s == 0:
+                    consts_c()
+                if last:
+                    cp(ind(XW, v("AL", 0, 8)), v("NEG1", 0, 128))
                 largest(0)
             scan(v("MX", lo, hi), v("MASK", 0, hi - lo), v("GG", lo, hi), A.min, A.max)
         sums(0)
@@ -427,15 +439,19 @@ def rank_program(g, core, T, topo):
         own = [(t, v("CW", 128 * t, 128 * t + 128)) for t in OWN]
         imp = [(2, v("CI"))]
         if last:
-            cp(ind(XW, v("AL", 0, 8)), v("NEG1", 0, 128))
+            cp(ind(v("YC"), v("UW", 0, 2)), v("YM", 0, 32))
+        if s == 0:
+            consts_d()
+            dma(v("FC", 0, W), v("CODE"), after=v("CC"))
+            dma(v("FC", W, TW), v("CODE", 0, TW - W))
         ts(v("RC"), v("RL"), 15.0, A.min, -15.0, A.add)
         tt(v("EQ"), v("PS1", 0, 256), v("ZS", 0, 256), A.is_equal)
         scan(v("LS"), v("DO"), v("PS3", 0, 32), A.max, A.min)
         mm([(v("PS2", 0, 256), v("ID"), v("AD")), (v("PS2", 0, 256), v("IDB"), v("EQ"))], False, False, True)
         turn(own)
-        if s == 0:
-            consts_d()
         mul(v("OS", 0, 256), v("PS1", 0, 256), 1.0)
+        if s == 0:
+            consts_e()
         cp(v("LB"), v("LS", 1, 32, 2))
         act(v("WA"), v("PS2", 0, 256), AF.Sigmoid, 5000.0, -1.0)
         cp(ind(XW, v("LB")), v("MX", 14, 4096, 16))
@@ -448,12 +464,16 @@ def rank_program(g, core, T, topo):
         if last:
             dma(T.yx[:, 0:V], v("YX", 0, V))
         send(s)
+        if s == 0:
+            iota(v("FF"), [[1, TW]])
+            iota(v("YX", W, TW), [[0, TW - W]], 0)
+            keep(v("BOF"), v("BO"), [[0, 128]], A.is_equal, 0, 0)
         for k in range(2):
             act(v("LE", 256 * k, 256 * k + 256), v("PX"), AF.Sign, v("TC5", k, k + 1), -1.0, v("KA", k, k + 1))
         mm(z_split("PS6", OWN), True, False, True)
         mm([(v("PS0", 0, 256), v("WN"), v("GG", 15, 4096, 16)), (v("PS0", 0, 256), v("IDB"), v("WA")), (v("PS0", 0, 256), v("IDB"), v("NEG1"))])
         if s == 0:
-            consts_e()
+            consts_f()
         powers("PS6", OWN)
         onehot(OWN, 0, 6)
         ts(v("KU"), v("KA"), 0.5, A.mult, 128.0, A.add)
@@ -471,12 +491,17 @@ def rank_program(g, core, T, topo):
         ts(v("UL"), v("US", 15, 32, 16), float(-K0), A.add)
         ts(v("FI"), v("US", 15, 32, 16), float(16 - K0 - V), A.add, 111.0, A.min)
         for k in range(2):
-            ts(v("ET", 32 * k, 32 * k + 32), v("UT", 32 * k, 32 * k + 32), v("US", 15 + 16 * k, 16 + 16 * k), A.is_equal)
-        tt(CL, ind(CCw, v("UL")), CO, A.min)
+            ts(v("ET", 32 * k, 32 * k + 32), v("UT", 32 * k, 32 * k + 32), v("US", 15 + 16 * k, 16 + 16 * k), A.is_equal, -1.0, A.add)
+        onehot(OWN, 10, 11)
+        tt(v("CL"), ind(CCw, v("UL")), CO, A.min)
+        tt(v("EM"), v("ET", 0, 32), v("ET", 32, 64), A.max)
         act(v("UR"), ind(TTw, v("UL")))
-        onehot(OWN, 10, 16)
-        mm([(v("PS2", 0, 256, p=PU), v("ET", 32 * k, 32 * k + 32), v("NGZ")) for k in range(2)] +
-           [(v("PS2", 0, 256), v("NBD"), v("NGZ"))] + z_split("PS2", IMP), True, False, False)
+        if s == 0:
+            floats(0)
+        onehot(OWN, 11, 13)
+        tt(CL, v("CL"), v("EM"), A.max)
+        onehot(OWN, 13, 16)
+        mm(z_split("PS2", IMP) + [(v("PS2", 0, 256), v("NBD"), v("NGZ"))], True, False, False)
         arrival(s)
         c = 96 * s
         land = [(v("PS1", 32 * d, 32 * d + 32), v(("P1", "P2", "ID")[d]), v("LD", c + 32 * d, c + 32 * d + 32)) for d in range(3)]
@@ -484,16 +509,15 @@ def rank_program(g, core, T, topo):
         words(OWN, True, False)
         act(v("FL", 16, 112), v("PS1", 0, 96), AF.Relu, 1.0, -1.0)
         onehot(IMP, 0, NI)
+        tt(v("CT"), ind(XW, v("UL")), CL, A.max)
         cp(v("FL", 112, 144), ind(v("FL", 0, 112), v("FI")))
         onehot(IMP, NI, 16)
         mm([(v("PS2", 0, 256), v("FL", 16, 144), v("NGZ"))], True, False, True)
         powers("PS2", IMP)
-        tt(v("CT"), ind(XW, v("UL")), CL, A.max)
         tt(v("UD", 32, 64), ind(v("OS"), v("KU")), v("DIAG"), A.mult)
-        mm([(v("PS3", 32, 34), v("ID"), v("KP"))] + wrap(v("PS3", 32, 34), "BS", "ET", 0, 32), False, True, False)
+        mm([(v("PS3", 32, 34), v("ID"), v("KP"))] + wrap(v("PS3", 32, 34), "BS", "CT", 0, 32))
         words(IMP, False, True)
         mul(v("WO"), v("PS7", 0, 256), 2.0 ** LOW)
-        mm(wrap(v("PS3", 32, 34), "BS", "ET", 32, 64) + wrap(v("PS3", 32, 34), "BS", "CT", 0, 32), False, False, True)
         for k in range(2):
             ts(v("EE", 256 * k, 256 * k + 256), v("PS0", 0, 256), v("US", 15 + 16 * k, 16 + 16 * k), A.is_equal, 2048.0, A.mult)
         scan(v("US", 32, 64), v("M01", 0, 32), v("UD", 32, 64), A.mult, A.add)
@@ -507,53 +531,74 @@ def rank_program(g, core, T, topo):
             scan(v("ES", 256 * k, 256 * k + 256), v("ONES"), v("EE", 256 * k, 256 * k + 256), A.mult, A.max)
         ts(v("UOC"), v("US", 15, 64, 16), float(K0 + W), A.min, float(-K0), A.add)
         tt(v("MG"), ind(CCw, v("UL")), CO, A.max)
-        cp(v("D2"), ind(v("WO"), v("WL")))
-        for k in range(6):
-            ts(v("D3", 32 * k, 32 * k + 32), v("D2"), k, A.logical_shift_right, 0o01010101, A.bitwise_and)
         tt(v("X1"), v("PS3", 32, 34), v("ES", 255, 512, 256), A.max)
-        scan(v("D5"), v("M01"), v("D3"), A.mult, A.add)
+        late = s - (S - 2)
+        if late >= 0:
+            mm([(v("PS0", 256, 288), v("BOF"), v("MG"))])
+        if late == 0:
+            mm([(v("PS5"), v("BOF"), v("CF", 0, 512))])
+            ts(v("YX", 0, 512), v("TT", 0, 512), -1.0, A.max)
 
         def pick(name, base, src):
             for k in range(2):
                 ts(v(name, base + k, base + k + 1), v("X1", k, k + 1), v("DA", 2 * s + k, 2 * s + k + 1), A.min,
                    v("UOC", src + k, src + k + 1), A.max)
-        if not last:
-            tt(v("TT", V, W), v("PS1", 128, 224), v("CODE", V, W), A.max)
         pick("AL", 2 * s, 2)
         pick("RR", 6 + 2 * s, 2)
-        for f in range(4):
-            ts(v("D7", 12 * f, 12 * f + 12), v("D5", 15, 192, 16), 63 << (6 * f), A.bitwise_and)
+        if late == 0:
+            ts(v("YX", 512, 1024), v("TT", 512, 1024), -1.0, A.max)
         cp(ind(FCw, v("AL", 2 * s, 2 * s + 2)), v("UR"))
         nr = 8 + 2 * s
         r0 = 6 if last else 0
         act(v("RG", 16 * r0, 16 * nr), ind(FCw, v("RR", r0, nr)))
+        if late >= 0:
+            mul(v("YM", 32 * late, 32 * late + 32), v("PS0", 256, 288), 1.0)
+        if s == 0:
+            floats(1)
+        cp(v("D2"), ind(v("WO"), v("WL")))
+        if not last:
+            tt(v("TT", V, W), v("PS1", 128, 224), v("CODE", V, W), A.max)
+        UW = v("UW", 2 * last, 2 * last + 2)
+        if last:
+            mm([(v("PS4", 0, 160), v("WN"), v("RG", 96, 256))])
+            mul(v("RO"), v("PS4", 0, 160), 1.0, float(-K0))
+        else:
+            mm(wrap(v("PS3", 64, 64 + nr), "WS", "RG", 0, 16 * nr))
+        if late == 0:
+            mm([(v("PS6"), v("BOF"), v("CF", 512, 1024))])
+        for k in range(6):
+            ts(v("D3", 32 * k, 32 * k + 32), v("D2"), k, A.logical_shift_right, 0o01010101, A.bitwise_and)
+        pick("UW", UW[2], 0)
+        scan(v("D5"), v("M01"), v("D3"), A.mult, A.add)
+        if last:
+            cp(ind(v("YC"), UW), v("YM", 32, 64))
+            dma(T.yc[:], v("YC", 0, W, p=(0, 128, 16)), "a")
+        else:
+            ts(v("RR", 0, nr), v("PS3", 64, 64 + nr), float(-K0), A.add)
+            act(v("RT", 0, 32 * s + 32), ind(TTw, v("RR", 6, nr)))
+        if late == 0:
+            row_sums(0)
+            row_sums(1)
+        if s == 0:
+            floats(2)
+        for f in range(4):
+            ts(v("D7", 12 * f, 12 * f + 12), v("D5", 15, 192, 16), 63 << (6 * f), A.bitwise_and)
+        if late == 0:
+            ts(v("YX", 1024, W), v("TT", 1024, W), -1.0, A.max)
         for w in range(2):
             tt(v("AWF" if last else "AW", 24 * w, 24 * w + 24), v("D7", w, 48, 2), v("REM", 24 * w, 24 * w + 24), A.is_ge)
-        pick("UW", 0, 0)
-        if not last:
+        if last:
+            dma(T.yw[:], v("AWF"))
+            cp(ind(FFw, v("AL")), v("RO"))
+            dma(T.yf[:], v("FF", 0, W, p=(0, 128, 16)))
+        else:
             scan(v("NK"), v("ONES", 0, 48), v("AW"), A.add, A.add)
             mm([(v("PS4", 32, 33), v("TRI"), v("NK", 47, 48))])
             tt(v("NK2"), v("AW"), v("KC2"), A.mult)
-        cp(ind(CCw, v("UW")), v("MG"))
-        if not last:
-            mm(wrap(v("PS3", 64, 64 + nr), "WS", "RG", 0, 16 * nr))
-            if s == 0:
-                ts(v("IDU"), v("IDF"), v("RF"), A.add, float(TW - 1), A.min)
-                act(v("CF"), ind(CCw, v("IDU")))
-            if s == S - 2:
-                act(v("YR"), TTw, AF.Relu, 1.0, 1.0)
-                mul(v("YX"), v("YR"), 1.0, -1.0)
-        else:
-            dma(T.yw[:], v("AWF"))
-            mm([(v("PS4", 0, 160), v("WN"), v("RG", 96, 256))])
-            for b in range(3):
-                mm([(v("PS%d" % b, p=(0, 8)), v("B8"), v("CF", 512 * b, 512 * b + 512))])
-            mul(v("RO"), v("PS4", 0, 160), 1.0, float(-K0))
-            cp(ind(FFw, v("AL")), v("RO"))
-            dma(T.yf[:], v("FF", 0, W, p=(0, 128, 16)))
-            for b in range(3):
-                mul(v("YC", 512 * b, 512 * b + 512, p=(0, 8)), v("PS%d" % b, p=(0, 8)), 1.0)
-            dma(T.yc[:], v("YC", p=(0, 8)), "a")
+            if s > 0:
+                cp(ind(v("CF", 0, TW), UW), v("MG"))
+        if late == 0:
+            mm([(v("PS7"), v("BOF"), v("CF", 1024, 1536))])
 
     Q = {"v": g.vector, "a": g.scalar, "p": g.tensor, "g": g, "s": g.sync}
     SEM = {"v": "sv", "a": "sa", "p": "sp", "g": "sg"}

import math
from concourse.bass import DstId, RemoteDMATransfer
from concourse.mybir import AluOpType as A, ActivationFunctionType as AF

S, V, W, G = 5, 1440, 1536, 768
TW = 1968
SENT = 1952
C2 = 480
K0 = 257 + 256 * C2
BIG = float(2 ** 20)
MID, DX = 1184.5, 2.0 ** -14
KX = 0.25 - (768 * DX) ** 2 / 64
UNY, UNC = -1.0 / (DX * KX), SENT - MID + 0.25 + 0.5 / (DX * KX)
OA, OW, LOW = 136, 170, 40
Z0, Z1 = 88.0, 176.0 * OA - 64.0 * OW
LN2 = math.log(2.0)
SA = 22
NA, NC, NV = 1024, 1024, 1280
NL = NA + NC + NV
NM, NI = 1536, 12

f32, bf, i32, u16 = "float32", "bfloat16", "int32", "uint16"
BUF = {
    "TT": (TW, bf), "CC": (TW, i32), "CF": (1984, f32), "FF": (TW, f32), "FC": (TW, bf), "GA": (2304, f32), "GB": (2304, f32), "GC": (256, f32),
    "XB": (V, bf), "ZB": (V, bf), "CODE": (W, bf), "CC2": (256, bf), "C15": (256, bf), "HB": (6, f32), "IDF": (124, f32), "IDU": (124, u16),
    "GV": (G, i32), "GP": (G, f32), "AWI": (48, i32), "EXI": (6, i32), "FILL": (256, f32),
    "AW": (48, bf), "AWF": (48, f32), "NK": (48, bf), "PRE": (48, f32), "NK2": (48, f32), "POSU": (48, u16),
    "REM": (48, f32), "REM2": (48, f32), "KC2": (48, f32), "KCU": (48, u16), "ONES": (256, bf), "ZO": (256, bf),
    "OFF": (256, u16), "GG": (4096, bf), "MX": (4096, bf), "MASK": (NM, bf), "M01": (192, f32), "DIAG": (32, f32),
    "RL": (256, bf), "RC": (256, bf), "ZS": (272, f32), "OS": (272, f32), "AD": (256, bf), "EQ": (256, bf),
    "LO": (16, u16), "DO": (32, f32), "LS": (32, f32), "LB": (16, u16), "KD": (64, bf),
    "CW": (272, f32), "AA": (384, bf), "WB": (384, bf), "WW": (768, bf), "OH": (6144, bf), "WO": (256, f32), "WL": (2, u16),
    "WA": (256, bf), "PX": (256, bf), "LE": (512, bf), "KA": (2, f32), "KU": (2, u16), "TC": (2, f32), "TC5": (2, f32),
    "UD": (64, f32), "US": (64, f32), "UL": (2, u16), "FI": (2, u16), "UOC": (4, f32), "UR": (32, bf), "UT": (64, f32), "TRI2": (64, f32),
    "MG": (32, f32), "CL": (32, bf), "EM": (32, bf), "CT": (32, bf), "ET": (64, bf), "EE": (512, bf), "ES": (512, bf),
    "X1": (2, f32), "DA": (10, f32), "UW": (4, u16), "AL": (10, u16), "RR": (16, u16),
    "RG": (256, bf), "RO": (160, f32), "RT": (160, bf), "NEG1": (256, bf),
    "SB": (96 * S, bf), "LD": (96 * S, bf), "NBD": (128, bf), "CI": (128, f32), "FL": (144, bf),
    "D2": (32, i32), "D3": (192, i32), "D5": (192, i32), "D7": (48, i32), "ZC": (512, bf), "ZI": (256, bf),
    "PC": (1, i32), "GCI": (1, i32), "RCI": (1, i32), "PF": (1, f32), "GF": (1, f32), "RF": (1, f32), "R48": (1, f32), "WC": (10, f32),
    "TG": (1, f32), "G15": (1, f32), "PMC": (1, f32), "JR": (256, bf), "JG": (128, bf), "JG2": (256, bf), "B8": (8, f32),
    "ID": (128, bf), "NID": (128, bf), "BO": (128, bf), "TRI": (128, bf), "WZ": (128, bf), "WN": (128, bf), "BOB": (128, bf),
    "W2B": (128, bf), "IDB": (128, bf), "P1": (128, bf), "P2": (128, bf),
    "PM": (128, f32), "IZ": (128 * 4, bf), "GZ": (256, bf), "NGZ": (256, bf), "G2Z": (256, bf),
    "BS": (144, bf), "BN": (144, bf), "B2": (144, bf), "B15": (144, f32), "WS": (144, bf), "KP": (2, bf),
    "YC": (TW, f32), "YM": (64, f32), "YX": (TW, bf), "BOF": (128, f32), "B60": (128, bf), "L2": (128, bf),
}
SCRATCH, PLACE, _fill = {}, {}, {}
for _k, (_n, _d) in BUF.items():
    if _n > 64 or _k in ("AWI", "EXI", "AWF"):
        SCRATCH[_k] = ("sbuf", [128, _n], _d)
        PLACE[_k] = (_k, 0)
    else:
        PLACE[_k] = ("pool_" + _d, _fill.get(_d, 0))
        _fill[_d] = _fill.get(_d, 0) + (_n + 15) // 16 * 16
for _d, _n in _fill.items():
    SCRATCH["pool_" + _d] = ("sbuf", [128, _n], _d)
for _b in range(8):
    SCRATCH["PS%d" % _b] = ("psum", [128, 512], f32)
NDMA = 36
SEMAPHORES = ["sv", "sa", "sp", "sg", "sent"] + ["arr%d" % s for s in range(S)] + ["d%d" % k for k in range(NDMA)]


def send_masks(src, peers, topo):
    near = [p for p in peers if p in topo.cores_of(src)]
    far = [p for p in peers if p not in near]
    out, used = {}, []
    for grp in (far, near):
        for k, p in enumerate(grp):
            free = [e for e in topo.engines(src, p) if e not in used]
            n = max(1, len(free) // (len(grp) - k))
            while n & (n - 1):
                n -= 1
            out[p] = free[:n]
            used += free[:n]
    return out


def rank_program(g, core, T, topo):
    rank = T.rank_of(core)
    if rank is None:
        return
    N = len(T.cores)
    ops = []

    def v(name, lo=0, hi=None, step=1, p=None):
        n = 512 if name.startswith("PS") else BUF[name][0]
        return ("v", name, lo, n if hi is None else hi, step, p)

    def ind(win, off):
        return ("i", win, off)

    def ap(x):
        if not isinstance(x, tuple):
            return x
        if x[0] == "i":
            return ap(x[1]).indirect(ap(x[2]))
        _, name, lo, hi, step, p = x
        ps = slice(None) if p is None else slice(*p)
        name, base = PLACE.get(name, (name, 0))
        lo, hi = lo + base, hi + base
        return T[name][ps, lo:hi:step] if step != 1 else T[name][ps, lo:hi]

    def spans(xs):
        return [(x[1], x[2], x[3], x[4]) for x in xs if isinstance(x, tuple) and x[0] == "v"]

    def op(q, fn, outs, ins, kind="c"):
        rd, wr = [], []
        for x in outs:
            if isinstance(x, tuple) and x[0] == "i":
                wr += spans([x[1]])
                rd += spans([x[2]])
            else:
                wr += spans([x])
        for x in ins:
            rd += spans([x[1], x[2]]) if isinstance(x, tuple) and x[0] == "i" else spans([x])
        ops.append((q, fn, rd, wr, kind))

    def cp(o, i):
        op("v", lambda: g.vector.tensor_copy(ap(o), ap(i)), [o], [i])

    def tt(o, a, b, f):
        op("v", lambda: g.vector.tensor_tensor(ap(o), ap(a), ap(b), f), [o], [a, b])

    def ts(o, a, s1, f1, s2=None, f2=None):
        if f2 is None:
            op("v", lambda: g.vector.tensor_scalar(ap(o), ap(a), ap(s1), None, f1), [o], [a, s1])
        else:
            op("v", lambda: g.vector.tensor_scalar(ap(o), ap(a), ap(s1), ap(s2), f1, f2), [o], [a, s1, s2])

    def scan(o, d0, d1, f0, f1, init=0.0):
        op("v", lambda: g.vector.tensor_tensor_scan(ap(o), ap(d0), ap(d1), init, f0, f1), [o], [d0, d1])

    def mset(o, c):
        op("v", lambda: g.vector.memset(ap(o), c), [o], [])

    def act(o, i, f=AF.Identity, bias=0.0, scale=1.0, acc=None):
        if o[0] == "i":
            op("a", lambda: g.scalar.activation(ap(o), ap(i), f), [o], [i])
        elif acc is not None:
            op("a", lambda: g.scalar.activation(ap(o), ap(i), f, bias=ap(bias), scale=ap(scale), accum_out=ap(acc)), [o, acc], [i, bias, scale])
        else:
            op("a", lambda: g.scalar.activation(ap(o), ap(i), f, bias=ap(bias), scale=ap(scale)), [o], [i, bias, scale])

    def mul(o, i, scale, bias=0.0):
        act(o, i, AF.Identity, bias, scale)

    def fill(o, c):
        act(o, v("ZO", 0, len(range(o[2], o[3], o[4])), p=o[5]), AF.Identity, c, 0.0)

    def mm(items, whole=False, start=True, stop=True):
        def fn():
            last = None
            for k, (o, l, r) in enumerate(items):
                first = start and (k == 0 if whole else all(o != z[0] for z in items[:k]))
                final = stop and (k == len(items) - 1 if whole else all(o != z[0] for z in items[k + 1:]))
                last = g.tensor.matmul(ap(o), ap(l), ap(r), first, final)
            return last
        op("p", fn, [x[0] for x in items], [y for x in items for y in x[1:]])

    def iota(o, pat, base=0, cm=0):
        if BUF[o[1]][1] == i32:
            op("g", lambda: g.iota(ap(o), pat, base, cm), [o], [])
        else:
            op("g", lambda: g.iota(ap(o), pat, base, cm, allow_small_or_imprecise_dtypes=True), [o], [])

    def keep(o, i, pat, f, base, cm):
        op("g", lambda: g.affine_select(ap(o), ap(i), pat, f, 0.0, base, cm), [o], [i])

    def dma(o, i, q="s", after=None):
        e = g.sync if q == "s" else g.scalar
        op(q, lambda: e.dma_start(ap(o), ap(i)), [o], [i, after], "d")

    def wrap(o, mat, src, lo, hi, step=1):
        return [(o, v(mat, 15 - r, 143 - r), v(src, lo + step * r, hi, 16 * step)) for r in range(16)]

    peers = [T.cores[rank ^ d] for d in range(1, N)]
    masks = send_masks(core, peers, topo)
    arrive = sum(len(send_masks(p, [T.cores[T.rank_of(p) ^ d] for d in range(1, N)], topo)[core]) for p in peers)
    leave = sum(len(m) for m in masks.values())

    def send(s):
        def fn():
            tr = []
            for d in range(N - 1, 0, -1):
                p = peers[d - 1]
                rid, pid = topo.addr(p, core)
                c = 96 * s + 32 * (d - 1)
                tr.append(RemoteDMATransfer(dst_ids=[DstId(rid=rid, pnc=pid)], dma_engine_mask=sum(1 << e for e in masks[p]),
                                            remote_sem=T.sem["arr%d" % s], src=T.SB[:, c:c + 32], dst=T.LD[:, c:c + 32]))
            g.remote_dma_fused(tr, local_sem=T.sem.sent)
        op("g", fn, [], [v("SB", 96 * s, 96 * s + 96)], "r")

    def arrival(s):
        op("p", lambda: g.tensor.wait_ge(T.sem["arr%d" % s], arrive), [], [], "w")

    dma(v("AWI"), T.aw[:], "a")
    dma(v("GV"), T.gv[:])
    dma(v("XB"), T.x0[:])
    dma(v("EXI"), T.ex[:], "a")
    dma(v("CC", 0, W), T.co[:], after=v("XB"))
    iota(v("PC"), [[1, 1]], 0, 1)
    iota(v("JR"), [[1, 256]])
    iota(v("JG"), [[1, 8], [0, 16]])
    mset(v("ZO"), 0.0)
    act(v("ONES"), v("ZO"), AF.Sigmoid, 40.0, 0.0)
    mset(v("GA", 0, 256), 0.5 - MID * DX * KX)
    mset(v("TT", W, TW), 0.0)
    ts(v("RCI"), v("PC"), 15, A.bitwise_and)
    ts(v("GCI"), v("PC"), 4, A.arith_shift_right)
    cp(v("PF"), v("PC"))
    mset(v("GB", 0, 256), 0.5 - MID * DX * KX)
    cp(v("RF"), v("RCI"))
    cp(v("GF"), v("GCI"))
    mset(v("DO", 0, 32, 2), 1e29)
    mset(v("KD", 0, 32, 2), C2 * 2.0 ** 24)
    mset(v("KD", 32, 64, 2), 240 * 2048.0)
    ts(v("DIAG", 0, 16), v("JR", 0, 16), v("RF"), A.is_equal)
    ts(v("R48"), v("RF"), 48.0, A.mult)
    ts(v("ID"), v("JR", 0, 128), v("PF"), A.is_equal)
    ts(v("G15"), v("GF"), 16.0, A.mult, 15.0, A.add)
    ts(v("BO"), v("JG"), v("GF"), A.is_equal)
    keep(v("TRI"), v("BO"), [[1, 128]], A.is_gt, 0, -1)
    ts(v("WC", 5, 6), v("DIAG", 2, 3), 1.0 - C2, A.mult, -1.0, A.add)
    ts(v("WC", 6, 7), v("DIAG", 1, 2), -1.0, A.mult)
    ts(v("WC", 4, 5), v("DIAG", 0, 1), -1.0, A.mult)
    ts(v("WC", 8, 9), v("DIAG", 2, 3), -2.0, A.mult)
    ts(v("KCU"), v("JR", 0, 48), v("R48"), A.add)
    ts(v("KC2"), v("JR", 0, 48), v("R48"), A.add, float(G + 2), A.add)
    ts(v("HB"), v("JR", 0, 6), v("WC", 6, 7), A.mult, v("WC", 5, 6), A.add)
    ts(v("B60"), v("BO"), C2 / 8.0, A.mult)
    ts(v("L2"), v("BO"), v("WC", 8, 9), A.mult)
    cp(v("AW"), v("AWI"))
    for h in range(6):
        ts(v("CODE", 256 * h, 256 * h + 256), v("JR"), v("WC", 4, 5), A.mult, v("HB", h, h + 1), A.add)
    iota(v("MASK", 0, 384), [[0, 24], [16, 16]])
    for q in range(1, 4):
        dma(v("MASK", 384 * q, 384 * q + 384), v("MASK", 0, 384))
    fill(v("FILL"), 0.5 - MID * DX * KX)
    fill(v("KP"), 32768.0)
    fill(v("ZS", 256, 272), float(K0 + SENT))
    fill(v("OS", 256, 272), float(K0 + SENT))
    fill(v("CW", 256, 272), -1.0)
    mul(v("WC", 0, 1), v("DIAG", 1, 2), 256.0, v("DIAG", 0, 1))
    mul(v("WC", 3, 4), v("DIAG", 2, 3), BIG)
    mul(v("WC", 7, 8), v("DIAG", 2, 3), 2.0 ** 24)
    mul(v("IDB"), v("ID"), BIG)
    mul(v("WC", 1, 2), v("DIAG", 2, 3), 256.0, v("WC", 0, 1))
    mul(v("BOB"), v("BO"), BIG)
    mul(v("WC", 2, 3), v("WC", 1, 2), -1.0)
    mul(v("WZ"), v("BO"), v("WC", 1, 2))
    mul(v("W2B"), v("BO"), v("WC", 3, 4))
    mul(v("WN"), v("BO"), v("WC", 2, 3))
    iota(v("JG2"), [[0, 16], [1, 8], [0, 2]])
    iota(v("C15"), [[0, 256]], 15)
    iota(v("CC", W, TW), [[0, TW - W]], -1)
    iota(v("CC2"), [[0, 256]], C2)
    iota(v("ZC"), [[0, 256], [int(Z1 - Z0), 2]], int(Z0 - 2 * C2))
    iota(v("NEG1"), [[0, 256]], -1)
    keep(v("M01"), v("ONES", 0, 192), [[0, 12], [1, 16]], A.is_gt, 0, 0)
    iota(v("ZI"), [[0, 128], [int(Z1 - Z0), 2]], int(Z0))
    iota(v("NBD"), [[0, 128]], 0)
    iota(v("FL"), [[0, 144]], 1)
    iota(v("DA"), [[16, 10]], W + 256, 0)
    iota(v("IDF"), [[16, 124]])

    def consts_a():
        ts(v("B15"), v("JR", 0, 144), v("G15"), A.is_equal, v("DIAG", 15, 16), A.mult)
        ts(v("TC"), v("JR", 0, 32, 16), v("RF"), A.add)
        ts(v("PMC"), v("RF"), 8.0, A.mult, v("GF"), A.add)
        ts(v("TG"), v("RF"), 2.0, A.mult, v("PF"), A.subtract)
        ts(v("BN"), v("JR", 0, 144), v("G15"), A.is_equal, -2048.0, A.mult)
        ts(v("KD", 1, 32, 2), v("JR", 0, 256, 16), float(W), A.add)
        ts(v("KD", 33, 64, 2), v("JR", 0, 16), 0.0, A.mult, v("RF"), A.add)

    def consts_b():
        mul(v("NID"), v("ID"), -8192.0)
        for k, c in enumerate((-64.0, 80.0, 64.0, -176.0)):
            mul(v("IZ", 128 * k, 128 * k + 128), v("ID"), c)

    def consts_c():
        ts(v("B2"), v("JR", 0, 144), v("G15"), A.is_equal, v("WC", 7, 8), A.mult)
        ts(v("PM"), v("JR", 0, 128), v("PMC"), A.is_equal)
        ts(v("GZ"), v("JG2"), v("GF"), A.is_equal, 64.0, A.mult)
        ts(v("G2Z"), v("JG2"), v("GF"), A.is_equal, v("WC", 8, 9), A.mult)
        cp(v("RR", 0, 6), v("EXI"))

    def consts_d():
        ts(v("TC5"), v("TC"), 0.5, A.add)
        cp(v("DIAG", 16, 32), v("DIAG", 0, 16))
        ts(v("TRI2", 0, 32), v("JR", 0, 32), v("TC", 0, 1), A.is_gt)
        ts(v("TRI2", 32, 64), v("JR", 0, 32), v("TC", 1, 2), A.is_gt)
        ts(v("P1"), v("JR", 0, 128), -112.0, A.add, v("TG"), A.is_equal)
        ts(v("IDU"), v("IDF"), v("RF"), A.add, float(TW - 1), A.min)

    def consts_e():
        ts(v("BS"), v("JR", 0, 144), v("G15"), A.is_equal, 2048.0, A.mult)
        ts(v("WS"), v("JR", 0, 144), v("G15"), A.is_equal, v("WC", 2, 3), A.mult)
        ts(v("WL"), v("JR", 0, 2), v("PMC"), A.add, v("PMC"), A.add)
        ts(v("DA"), v("DA"), v("RF"), A.add)

    def consts_f():
        mul(v("NGZ"), v("GZ"), -1.0)
        for w, z in enumerate((Z0, Z1)):
            fill(v("ZI", w, 256, 2, p=(96, 128)), z - 1024)
        mul(v("P2", 16, 128), v("P1", 0, 112), 1.0)
        mul(v("P2", 0, 16), v("P1", 112, 128), 1.0)

    def init_table():
        for b in range(3):
            o, code = v("PS%d" % b, 0, 480), v("CODE", 480 * b, 480 * b + 480)
            mm([(o, v("ID"), code), (o, v("L2"), code)], False, True, False)
        for b in range(3):
            mm([(v("PS%d" % b, 0, 480), v("B60"), v("XB", 480 * b, 480 * b + 480))], False, False, True)
        for b in range(3):
            lo, hi = 480 * b, 480 * b + 480
            tt(v("TT", lo, hi), v("PS%d" % b, 0, 480), v("XB", lo, hi), A.min)

    TTw, FFw, FCw = v("TT"), v("FF"), v("FC")

    def turn(src):
        mm([(v("PS5", 128 * t, 128 * t + 128), x, v("PM")) for t, x in src])

    def split(tiles):
        lo, hi = 128 * tiles[0], 128 * tiles[-1] + 128
        mul(v("AA", lo, hi), v("PS5", lo, hi), 1.0 / 48, OA - 23.5 / 48)
        mul(v("WB", lo, hi), v("PS5", lo, hi), 1.0 / 24, OW - 11.5 / 24)

    def z_open(bank, const, src):
        t0 = src[0][0]
        return [(v(bank, 0, const[3]), v("ID"), const)] + \
               [(v(bank, 256 * (t - t0) + w, 256 * (t - t0) + 256, 2), x, v("PM")) for w in range(2) for t, x in src]

    def z_split(bank, tiles):
        lo, hi = 128 * tiles[0], 128 * tiles[-1] + 128
        return [(v(bank, w, 2 * (hi - lo), 2), v("IZ", 256 * w + 128 * k, 256 * w + 128 * k + 128), v(("WB", "AA")[k], lo, hi))
                for w in range(2) for k in range(2)]

    def powers(bank, tiles):
        act(v("WW", 256 * tiles[0], 256 * tiles[-1] + 256), v(bank, 0, 256 * len(tiles)), AF.Sigmoid, -LN2 * (LOW + Z0), LN2)

    def onehot(tiles, lo, hi):
        for a in range(lo, hi):
            ts(v("OH", 2048 * tiles[0] + a, 2048 * tiles[-1] + 2048, 16), v("AA", 128 * tiles[0], 128 * tiles[-1] + 128),
               float(OA + a), A.is_equal)

    def words(tiles, start, stop):
        head = [(v("PS7", 0, 256), v("ID"), v("ZO"))] if start else []
        mm(head + [(v("PS7", 16 * i, 16 * i + 16), v("OH", 2048 * t + 128 * i, 2048 * t + 128 * i + 128),
                    v("WW", 256 * t + 16 * i, 256 * t + 16 * i + 16)) for t in tiles for i in range(16)], True, start, stop)

    def floats(k):
        lo, hi = ((0, 32), (32, 64), (64, 124))[k]
        act(v("CF", 16 * lo, 16 * hi), ind(v("CC"), v("IDU", lo, hi)))

    def row_sums(b):
        mul(v("YC", 512 * b, 512 * b + 512), v("PS%d" % (5 + b)), 1.0)

    OWN, IMP = (0, 1), (2,)
    for s in range(S):
        last = s == S - 1
        CN = "CC" if s == 0 else "CF"
        CCw = v(CN, 0, TW)
        XW = v("YX") if last else TTw
        if s == 0:
            scan(v("NK"), v("ONES", 0, 48), v("AW"), A.add, A.add)
            mm([(v("PS4", 32, 33), v("TRI"), v("NK", 47, 48))])
            tt(v("NK2"), v("AW"), v("KC2"), A.mult)
        tt(v("PRE"), v("NK"), v("NK2"), A.subtract)
        ts(v("POSU"), v("PRE"), v("PS4", 32, 33), A.add, float(G), A.add)
        ts(v("REM2"), v("PRE"), v("PS4", 32, 33), A.add, 256.0 - G, A.is_lt)
        if s == 0:
            consts_a()
            ts(v("GP", 0, 16 * SA), ind(v("GV"), v("KCU", 0, SA)), -DX * KX, A.mult, 0.5 + (SENT - MID) * DX * KX, A.add)
            act(v("GP", 16 * SA, G), ind(v("GV"), v("KCU", SA, 48)), AF.Identity, (SENT - MID) * DX, -DX)
            cp(v("TT", V, W), v("CODE", V, W))
        cp(ind(v("GA"), v("POSU", 0, SA)), v("GP", 0, 16 * SA))
        act(ind(v("GB"), v("POSU", SA, 48)), v("GP", 16 * SA, G), AF.Sigmoid)
        if s == 0:
            init_table()
            consts_b()
        else:
            cp(ind(TTw, v("AL", 0, 2 * s)), v("RT", 0, 32 * s))
            act(v("NBD", 0, 96), v("TT", V, W), AF.Relu, 1.0, 1.0)
        if s == 1:
            cp(ind(v("CF", 0, TW), v("UW", 0, 2)), v("MG"))
        if last:
            row_sums(2)
        parts = ((0, NA // 16), (NA // 16, NL // 16), (NL // 16, 256))
        for lo, hi in parts:
            tt(v("GC", lo, hi), v("GA", lo, hi), v("GB", lo, hi), A.max)
        for lo, hi in parts:
            ts(v("OFF", lo, hi), v("GC", lo, hi), UNY, A.mult, UNC, A.add)
        mm(wrap(v("PS4", 0, 16), "B15", "GC", 0, 256))
        if not last:
            dma(v("GA", 0, 256), v("FILL"))
            dma(v("GB", 0, 256), v("FILL"))
        act(v("GG", 0, NA), ind(TTw, v("OFF", 0, NA // 16)))
        cp(v("GG", NA + NC, NL), ind(TTw, v("OFF", (NA + NC) // 16, NL // 16)))
        act(v("GG", NA, NA + NC), ind(TTw, v("OFF", NA // 16, (NA + NC) // 16)))
        act(v("GG", NL, 4096), ind(TTw, v("OFF", NL // 16, 256)))
        chunks = ((0, NA, "PS0"), (NA + NC, NA + NC + NV, "PS0"), (NA, NA + NC, "PS0"), (NL, 4096, "PS5"))
        for lo, hi, bank in chunks:
            o = v(bank, lo // 16, hi // 16)
            mm([(o, v("ID"), v("C15", lo // 16, hi // 16))] + [(o, v("WZ"), v("GG", lo + i, hi, 16)) for i in range(15)])
        halves = ((0, NL // 16, "PS0"), (NL // 16, 256, "PS5"))

        def largest(k):
            lo, hi, bank = halves[k]
            tt(v("RL", lo, hi), v(bank, lo, hi), v("MX", 16 * lo + 14, 16 * hi, 16), A.max)

        def sums(k):
            lo, hi, bank = halves[k]
            mul(v("ZS", lo, hi), v(bank, lo, hi), -1.0, 15.0)
            act(v("AD", lo, hi), v(bank, lo, hi), AF.Abs, float(K0 + W // 2 - 15), 1.0)

        for k, (lo, hi, bank) in enumerate(chunks):
            if k == 1:
                ts(v("LO"), v("PS4", 0, 16), UNY, A.mult, UNC, A.add)
                ts(v("DO", 1, 32, 2), v("PS4", 0, 16), UNY, A.mult, UNC, A.add)
            if k == 3:
                tt(v("REM"), v("REM2"), v("AW"), A.is_ge)
                if s == 0:
                    consts_c()
                if last:
                    cp(ind(XW, v("AL", 0, 8)), v("NEG1", 0, 128))
                largest(0)
            scan(v("MX", lo, hi), v("MASK", 0, hi - lo), v("GG", lo, hi), A.min, A.max)
        sums(0)
        act(v("CW", 0, 256), ind(CCw, v("LO")))
        mm([(v("PS1", 0, 256), v("WN"), v("GG", 15, 4096, 16))])
        mm([(v("PS3", 0, 32), v("ID"), v("KD", 0, 32))] + wrap(v("PS3", 0, 32, 2), "B2", "GG", 15, 4096, 16), True, True, False)
        cp(v("CI", 0, 96), v(CN, V, W))
        largest(1)
        mm([(v("PS3", 0, 32), v("ID"), v("KD", 32, 64))] + wrap(v("PS3", 0, 32, 2), "BN", "RL", 0, 256), True, False, True)
        sums(1)
        mm([(v("PS2", 0, 256), v("IDB"), v("CC2")), (v("PS2", 0, 256), v("W2B"), v("GG", 15, 4096, 16)),
            (v("PS2", 0, 256), v("BOB"), v("MX", 14, 4096, 16))], False, True, False)
        own = [(t, v("CW", 128 * t, 128 * t + 128)) for t in OWN]
        imp = [(2, v("CI"))]
        if last:
            cp(ind(v("YC"), v("UW", 0, 2)), v("YM", 0, 32))
        if s == 0:
            consts_d()
            dma(v("FC", 0, W), v("CODE"), after=v("CC"))
            dma(v("FC", W, TW), v("CODE", 0, TW - W))
        ts(v("RC"), v("RL"), 15.0, A.min, -15.0, A.add)
        tt(v("EQ"), v("PS1", 0, 256), v("ZS", 0, 256), A.is_equal)
        scan(v("LS"), v("DO"), v("PS3", 0, 32), A.max, A.min)
        mm([(v("PS2", 0, 256), v("ID"), v("AD")), (v("PS2", 0, 256), v("IDB"), v("EQ"))], False, False, True)
        turn(own)
        mul(v("OS", 0, 256), v("PS1", 0, 256), 1.0)
        if s == 0:
            consts_e()
        cp(v("LB"), v("LS", 1, 32, 2))
        act(v("WA"), v("PS2", 0, 256), AF.Sigmoid, 5000.0, -1.0)
        cp(ind(XW, v("LB")), v("MX", 14, 4096, 16))
        split(OWN)
        mm(z_open("PS6", v("ZC"), own) +
           [(v("PS6", 256 * t, 256 * t + 256), v("GG", 2048 * t + 15, 2048 * t + 2048, 16), v("G2Z")) for t in OWN] +
           [(v("PS6", 256 * t, 256 * t + 256), v("RC", 128 * t, 128 * t + 128), v("GZ")) for t in OWN], True, True, False)
        scan(v("PX"), v("ONES"), v("WA"), A.mult, A.add)
        ts(v("SB", 96 * s, 96 * s + 96), ind(XW, v("RR", 0, 6)), -1.0, A.max, 1.0, A.add)
        if last:
            dma(T.yx[:, 0:V], v("YX", 0, V))
        send(s)
        if s == 0:
            iota(v("FF"), [[1, TW]])
            iota(v("YX", W, TW), [[0, TW - W]], 0)
            keep(v("BOF"), v("BO"), [[0, 128]], A.is_equal, 0, 0)
        for k in range(2):
            act(v("LE", 256 * k, 256 * k + 256), v("PX"), AF.Sign, v("TC5", k, k + 1), -1.0, v("KA", k, k + 1))
        mm(z_split("PS6", OWN), True, False, True)
        mm([(v("PS0", 0, 256), v("WN"), v("GG", 15, 4096, 16)), (v("PS0", 0, 256), v("IDB"), v("WA")), (v("PS0", 0, 256), v("IDB"), v("NEG1"))])
        if s == 0:
            consts_f()
        powers("PS6", OWN)
        onehot(OWN, 0, 6)
        ts(v("KU"), v("KA"), 0.5, A.mult, 128.0, A.add)
        onehot(OWN, 6, 8)
        CO, CL = v("CI", 96, 128), v("NBD", 96, 128)
        cp(CO, ind(v("CW"), v("KU")))
        tt(v("UD", 0, 32), ind(v("ZS"), v("KU")), v("DIAG"), A.mult)
        turn(imp)
        split(IMP)
        mm(z_open("PS2", v("ZI"), imp), True, True, False)
        tt(v("UT", 0, 32), ind(v("ZS"), v("KU")), v("TRI2", 0, 32), A.mult)
        tt(v("UT", 32, 64), ind(v("ZS"), v("KU")), v("TRI2", 32, 64), A.mult)
        scan(v("US", 0, 32), v("M01", 0, 32), v("UD", 0, 32), A.mult, A.add)
        onehot(OWN, 8, 10)
        ts(v("UL"), v("US", 15, 32, 16), float(-K0), A.add)
        ts(v("FI"), v("US", 15, 32, 16), float(16 - K0 - V), A.add, 111.0, A.min)
        for k in range(2):
            ts(v("ET", 32 * k, 32 * k + 32), v("UT", 32 * k, 32 * k + 32), v("US", 15 + 16 * k, 16 + 16 * k), A.is_equal, -1.0, A.add)
        onehot(OWN, 10, 11)
        tt(v("CL"), ind(CCw, v("UL")), CO, A.min)
        tt(v("EM"), v("ET", 0, 32), v("ET", 32, 64), A.max)
        act(v("UR"), ind(TTw, v("UL")))
        if s == 0:
            floats(0)
        onehot(OWN, 11, 13)
        tt(CL, v("CL"), v("EM"), A.max)
        onehot(OWN, 13, 16)
        mm(z_split("PS2", IMP) + [(v("PS2", 0, 256), v("NBD"), v("NGZ"))], True, False, False)
        arrival(s)
        c = 96 * s
        land = [(v("PS1", 32 * d, 32 * d + 32), v(("P1", "P2", "ID")[d]), v("LD", c + 32 * d, c + 32 * d + 32)) for d in range(3)]
        mm(land)
        words(OWN, True, False)
        act(v("FL", 16, 112), v("PS1", 0, 96), AF.Relu, 1.0, -1.0)
        onehot(IMP, 0, NI)
        tt(v("CT"), ind(XW, v("UL")), CL, A.max)
        cp(v("FL", 112, 144), ind(v("FL", 0, 112), v("FI")))
        onehot(IMP, NI, 16)
        mm([(v("PS2", 0, 256), v("FL", 16, 144), v("NGZ"))], True, False, True)
        powers("PS2", IMP)
        tt(v("UD", 32, 64), ind(v("OS"), v("KU")), v("DIAG"), A.mult)
        mm([(v("PS3", 32, 34), v("ID"), v("KP"))] + wrap(v("PS3", 32, 34), "BS", "CT", 0, 32))
        words(IMP, False, True)
        mul(v("WO"), v("PS7", 0, 256), 2.0 ** LOW)
        for k in range(2):
            ts(v("EE", 256 * k, 256 * k + 256), v("PS0", 0, 256), v("US", 15 + 16 * k, 16 + 16 * k), A.is_equal, 2048.0, A.mult)
        scan(v("US", 32, 64), v("M01", 0, 32), v("UD", 32, 64), A.mult, A.add)
        if last:
            mul(v("YX", V, W), v("PS1", 0, 96), 1.0, -1.0)
            dma(T.yx[:, V:W], v("YX", V, W))
        else:
            mm([(v("PS1", 128, 224), v("ID"), v("NEG1", 0, 96)), (v("PS1", 128, 224), v("NID"), v("FL", 16, 112))] +
               [(v("PS1", 128 + o[2], 128 + o[3]), l, r) for o, l, r in land], True)
        for k in range(2):
            scan(v("ES", 256 * k, 256 * k + 256), v("ONES"), v("EE", 256 * k, 256 * k + 256), A.mult, A.max)
        ts(v("UOC"), v("US", 15, 64, 16), float(K0 + W), A.min, float(-K0), A.add)
        tt(v("MG"), ind(CCw, v("UL")), CO, A.max)
        tt(v("X1"), v("PS3", 32, 34), v("ES", 255, 512, 256), A.max)
        late = s - (S - 2)
        if late >= 0:
            mm([(v("PS0", 256, 288), v("BOF"), v("MG"))])
        if late == 0:
            mm([(v("PS5"), v("BOF"), v("CF", 0, 512))])
            ts(v("YX", 0, 512), v("TT", 0, 512), -1.0, A.max)

        def pick(name, base, src):
            for k in range(2):
                ts(v(name, base + k, base + k + 1), v("X1", k, k + 1), v("DA", 2 * s + k, 2 * s + k + 1), A.min,
                   v("UOC", src + k, src + k + 1), A.max)
        pick("AL", 2 * s, 2)
        pick("RR", 6 + 2 * s, 2)
        if late == 0:
            ts(v("YX", 512, 1024), v("TT", 512, 1024), -1.0, A.max)
        cp(ind(FCw, v("AL", 2 * s, 2 * s + 2)), v("UR"))
        nr = 8 + 2 * s
        r0 = 6 if last else 0
        act(v("RG", 16 * r0, 16 * nr), ind(FCw, v("RR", r0, nr)))
        if late >= 0:
            mul(v("YM", 32 * late, 32 * late + 32), v("PS0", 256, 288), 1.0)
        if s == 0:
            floats(1)
        cp(v("D2"), ind(v("WO"), v("WL")))
        if not last:
            tt(v("TT", V, W), v("PS1", 128, 224), v("CODE", V, W), A.max)
        UW = v("UW", 2 * last, 2 * last + 2)
        if last:
            mm([(v("PS4", 0, 160), v("WN"), v("RG", 96, 256))])
            mul(v("RO"), v("PS4", 0, 160), 1.0, float(-K0))
        else:
            mm(wrap(v("PS3", 64, 64 + nr), "WS", "RG", 0, 16 * nr))
        if late == 0:
            mm([(v("PS6"), v("BOF"), v("CF", 512, 1024))])
        for k in range(6):
            ts(v("D3", 32 * k, 32 * k + 32), v("D2"), k, A.logical_shift_right, 0o01010101, A.bitwise_and)
        pick("UW", UW[2], 0)
        scan(v("D5"), v("M01"), v("D3"), A.mult, A.add)
        if last:
            cp(ind(v("YC"), UW), v("YM", 32, 64))
            dma(T.yc[:], v("YC", 0, W, p=(0, 128, 16)), "a")
        else:
            ts(v("RR", 0, nr), v("PS3", 64, 64 + nr), float(-K0), A.add)
            act(v("RT", 0, 32 * s + 32), ind(TTw, v("RR", 6, nr)))
        if late == 0:
            row_sums(0)
            row_sums(1)
        if s == 0:
            floats(2)
        for f in range(4):
            ts(v("D7", 12 * f, 12 * f + 12), v("D5", 15, 192, 16), 63 << (6 * f), A.bitwise_and)
        if late == 0:
            ts(v("YX", 1024, W), v("TT", 1024, W), -1.0, A.max)
        for w in range(2):
            tt(v("AWF" if last else "AW", 24 * w, 24 * w + 24), v("D7", w, 48, 2), v("REM", 24 * w, 24 * w + 24), A.is_ge)
        if last:
            dma(T.yw[:], v("AWF"))
            cp(ind(FFw, v("AL")), v("RO"))
            dma(T.yf[:], v("FF", 0, W, p=(0, 128, 16)))
        else:
            scan(v("NK"), v("ONES", 0, 48), v("AW"), A.add, A.add)
            mm([(v("PS4", 32, 33), v("TRI"), v("NK", 47, 48))])
            tt(v("NK2"), v("AW"), v("KC2"), A.mult)
            if s > 0:
                cp(ind(v("CF", 0, TW), UW), v("MG"))
        if late == 0:
            mm([(v("PS7"), v("BOF"), v("CF", 1024, 1536))])

    Q = {"v": g.vector, "a": g.scalar, "p": g.tensor, "g": g, "s": g.sync}
    SEM = {"v": "sv", "a": "sa", "p": "sp", "g": "sg"}
    count = {k: 0 for k in SEMAPHORES}
    known = {q: {} for q in Q}
    hist = {}
    nd = 0
    waited = {}
    for q, fn, rd, wr, kind in ops:
        need = {}
        for spn, isw in [(x, False) for x in rd] + [(x, True) for x in wr]:
            name, lo, hi, st = spn
            ps = name.startswith("PS")
            for (l2, h2, w2, q2, sem, val, kn, s2) in hist.get(name, []):
                if ps and q2 != q:
                    hit = True
                else:
                    hit = l2 < hi and lo < h2 and (isw or w2) and not (q == "p" and q2 == "p")
                    hit = hit and not (st == s2 > 1 and (lo - l2) % st)
                if hit and known[q].get(sem, 0) < val and need.get(sem, (0,))[0] < val:
                    need[sem] = (val, kn)
        for sem, (val, kn) in sorted(need.items(), key=lambda z: -len(z[1][1])):
            if known[q].get(sem, 0) >= val:
                continue
            Q[q].wait_ge(T.sem[sem], val)
            known[q][sem] = val
            waited[sem] = max(waited.get(sem, 0), val)
            for k2, v2 in kn.items():
                if known[q].get(k2, 0) < v2:
                    known[q][k2] = v2
        ins = fn()
        if kind in "rw":
            continue
        if kind == "d":
            sem = "d%d" % nd
            nd += 1
            count[sem] += 16
            ins.then_inc(T.sem[sem], 16)
        else:
            sem = SEM[q]
            count[sem] += 1
            ins.then_inc(T.sem[sem], 1)
        kn = dict(known[q])
        for spn, isw in [(x, False) for x in rd] + [(x, True) for x in wr]:
            h = hist.setdefault(spn[0], [])
            if isw:
                h[:] = [e for e in h if not (spn[3] == 1 and spn[1] <= e[0] and e[1] <= spn[2] and known[q].get(e[4], 0) >= e[5])]
            h.append((spn[1], spn[2], isw, q, sem, count[sem], kn, spn[3]))
    g.wait_ge(T.sem.sent, leave * S)
    for k, n in count.items():
        if n > waited.get(k, 0):
            g.wait_ge(T.sem[k], n)
